import numpy as np, ml_dtypes
CORES = [36,164,52,180,100,228,116,244]
N = 8
import mx_ref
BF = ml_dtypes.bfloat16
def cut(t, i, w=512):
    return t[:, w * i:w * i + w]
def tile(rs):
    return np.stack(rs, axis=2).reshape(128, -1).astype(BF)
def pick(q, e):
    c = np.concatenate([q[0].reshape(128, -1, 4), np.zeros((128, 1, 4), np.uint8)], axis=1); s = np.concatenate([q[1], np.ones((16, 1), np.uint8)], axis=1)
    return (np.ascontiguousarray(c[:, e].reshape(128, -1)), np.ascontiguousarray(s[:, e]))
def join(*qs):
    return (np.concatenate([q[0] for q in qs], axis=1), np.concatenate([q[1] for q in qs], axis=1))
def put(q, e, v):
    c, s = q[0].reshape(128, -1, 4).copy(), q[1].copy(); c[:, e] = v[0].reshape(128, -1, 4); s[:, e] = v[1]
    return (c.reshape(128, -1), s)
def pk(c, s):
    return (np.ascontiguousarray(c), mx_ref.live(s))
def emit(q):
    return q[0], q[1]
def f(rng, *shape):
    return mx_ref.flush((rng.standard_normal(shape, dtype=np.float32) * np.exp2(rng.integers(-2, 3, shape[:-1] + (1,)))).astype(BF))
def wide(rng, *shape, cols=0):
    v = rng.standard_normal(shape, dtype=np.float32) * np.exp2(rng.integers(-12, 13, shape)).astype(np.float32)
    if cols: v *= np.repeat(np.exp2(rng.integers(-cols, cols + 1, shape[:-2] + (1, shape[-1] // 4))) * (rng.random(shape[:-2] + (1, shape[-1] // 4)) > 0.0625), 4, axis=-1).astype(np.float32)
    return mx_ref.flush(v.astype(BF))
P, S, R = 256, 24, 3
E = P + 2 * S * R
def randoms(rng):
    s = np.where(rng.random((N, P)) < rng.random((N, 1)), -1, 1)
    x = np.abs(f(rng, N, 128, 4 * P).astype(np.float32)) * np.repeat(s, 4, axis=1)[:, None, :].astype(np.float32)
    a = f(rng, N, 128, 512).astype(np.float32) + np.float32(0.05) * rng.standard_normal((N, 1, 1)).astype(np.float32)
    return {"x": mx_ref.flush(x.astype(BF)), "a": mx_ref.flush(a.astype(BF)), "w": f(rng, N, 128, 2048)}
def planted(rng, n, sign):
    up = np.stack([rng.permutation(128) < n[r] for r in range(N)])
    a = (1 + rng.random((N, 128, 512))) * np.exp2(rng.integers(-2, 3, (N, 128, 1))) * np.repeat(np.where(up, 1.0, -1.0), 4, axis=1)[:, None, :]
    x = np.abs(f(rng, N, 128, 4 * P).astype(np.float32)) * np.float32(sign)
    return {"x": x.astype(BF), "a": a.astype(np.float32).astype(BF), "w": f(rng, N, 128, 2048)}
def setup_inputs(rng):
    return randoms(rng)
def setup_inputs_shrink(rng):
    k = N // 2 - int(rng.integers(0, 2))
    n = rng.integers(0, 2, N)
    n[k] = rng.integers(112, 128)
    d = planted(rng, n, 1)
    d["x"][k, :, :4 * S * R] = 0
    d["x"][k, :, 4 * (P - S * R):] = 0
    return d
def setup_inputs_grow(rng):
    k, big = N // 2 - int(rng.integers(0, 2)), int(rng.integers(113, 129))
    less = big if N > 4 else 3 * big // 4
    n = np.full(N, less - 1)
    if k < N // 2: n[:k] = big - 1
    else: n[k + 1:] = big - 1
    n[k] = rng.integers(0, 4)
    return planted(rng, n, 1)
def setup_inputs_spread(rng):
    return {**randoms(rng), "x": wide(rng, N, 128, 4 * P, cols=6)}
def setup_inputs_part(rng):
    k, m = (N - 1) * int(rng.integers(0, 2)), 4 * int(rng.integers(0, 4)) + 2
    d = planted(rng, np.where(np.arange(N) == k, 1, 0), 1)
    on = np.zeros(P, bool)
    on[16 + rng.permutation(P - 32)[:m]] = True
    d["x"][k][:, np.repeat(~on, 4)] = 0
    return d
def setup_inputs_turn(rng):
    k = N // 2 - int(rng.integers(0, 2))
    n = np.full(N, int(rng.integers(112, 128)))
    n[k] = rng.integers(0, 4)
    return planted(rng, n, -1)
def check_inputs(d):
    b = []
    for k in ("x", "a", "w"):
        v = np.abs(d[k].astype(np.float32))
        if not (np.isfinite(v).all() and ((v == 0) | (v >= 2.0 ** -30) & (v <= 2.0 ** 30)).all()): b.append("a value of " + k)
    return b
def held(row, bo, r, m=4):
    e = np.arange(bo[r], bo[r + 1])
    return pick(row, np.concatenate([e, np.full(-e.size % m, -1)]))
def moved(bo, cost):
    before, new = np.concatenate([[0], np.cumsum(cost)]), bo.copy()
    for b in range(1, N):
        g = int(np.argmax(N * before >= b * before[-1]))
        new[b] = bo[b] + min(S, max(-S, g - int(bo[b])))
    return new
def reference(x, a, w):
    qa = [mx_ref.quantize(np.ascontiguousarray(a[r])) for r in range(N)]
    qw = [[mx_ref.quantize(np.ascontiguousarray(cut(w[r], b))) for b in range(4)] for r in range(N)]
    bo, out = P * np.arange(N + 1), []
    row = join(*[mx_ref.quantize(np.ascontiguousarray(x[r])) for r in range(N)])
    for t in range(R):
        cost = []
        for r in range(N):
            z = mx_ref.matmul(qa[r], held(row, bo, r))[:, :bo[r + 1] - bo[r]]
            cost.append(1 + np.sum(z > 0, axis=0).astype(np.int64))
        bo = moved(bo, np.concatenate(cost))
        new = []
        for r in range(N):
            h = held(row, bo, r)
            v = tile([np.maximum(mx_ref.matmul(qw[r][b], h), np.float32(0)) * np.float32(0.0625) for b in range(4)])
            new.append(pick(mx_ref.quantize(np.ascontiguousarray(v)), np.arange(bo[r + 1] - bo[r])))
        row = join(*new)
        out.append(bo)
    y, oc, osc = np.zeros((N, 128, E), np.float32), np.zeros((N, 128, 4 * E), np.uint8), np.zeros((N, 16, E), np.uint8)
    for r in range(N):
        n = int(bo[r + 1] - bo[r])
        y[r, :, :n] = mx_ref.matmul(qa[r], held(row, bo, r))[:, :n]
        oc[r], osc[r] = emit(held(row, bo, r, E))
    return {"y": y, "oc": oc, "osc": osc, "bd": np.stack([np.stack(out).astype(np.float32) for r in range(N)])}

@@ -1,0 +1,444 @@
+from concourse.bass import DstId, RemoteDMATransfer
+from concourse.mybir import dt, AluOpType, AxisListType, ActivationFunctionType
+
+N, P, S, R = 8, 256, 24, 3
+E = P + 2 * S * R
+W = 3 * S
+I0 = 80
+MR, ML, MA = I0 + P, I0 + P + W, I0 + P + 2 * W
+FR, FL, FZ = P, P + W, P + 2 * W
+X4 = "float8_e4m3fn_x4"
+
+SCRATCH = {
+    "xe": ("sbuf", [128, 512], "bfloat16"),
+    "xt": ("sbuf", [128, 4 * P], "bfloat16"),
+    "at": ("sbuf", [128, 512], "bfloat16"),
+    "wt": ("sbuf", [128, 2048], "bfloat16"),
+    "junk": ("sbuf", [128, 512], "bfloat16"),
+    "ys": ("sbuf", [128, FZ + 2], "float32"),
+    "yo": ("sbuf", [128, E], "float32"),
+    "pint": ("sbuf", [128, 2], "int32"),
+    "off1": ("sbuf", [128, 10], "uint16"),
+    "off2": ("sbuf", [128, 10], "uint16"),
+    "off3": ("sbuf", [128, 26], "uint16"),
+}
+for _n, _c in (("qxe", 128), ("qa", 128), ("qw", 512), ("e0", 128 + 2 * S + P), ("e1", 160), ("e2", 160),
+               ("m0", MA + W), ("m1", MA + W), ("m2", FZ + 2), ("fin", E)):
+    SCRATCH[_n] = ("sbuf", [128, _c], X4)
+    SCRATCH[_n + "s"] = ("sbuf", [128, _c], "uint8")
+for _t in range(R):
+    SCRATCH["hi%d" % _t] = ("sbuf", [128, 4 * P], "bfloat16")
+    SCRATCH["he%d" % _t] = ("sbuf", [128, 4 * (2 * W + 2)], "bfloat16")
+    SCRATCH["ct%d" % _t] = ("sbuf", [128, 128], "float32")
+    SCRATCH["yt%d" % _t] = ("sbuf", [128, 128], "float32")
+    SCRATCH["cd%d" % _t] = ("dram", [N, 128, 4], "float32")
+for _n, _c in (("tiny", 1), ("cadd", 128), ("pref", 132), ("dm0", 96), ("dm1", 96), ("ar", 32), ("amat", 32), ("bcol", 1),
+               ("xl", 32), ("xlt", 32), ("sg", 32), ("pp", 32), ("ppt", 128), ("val", 128), ("cap", 128), ("zz", 128),
+               ("cown", 96), ("mx", 32), ("mt", 32),
+               ("th", 1), ("ind", 128), ("cnt", 1), ("cl", 32), ("wtm", 32), ("i1", 36), ("i2", 32), ("wa", 32), ("wb", 32),
+               ("pcol", 1), ("p16", 1), ("j0", 25), ("jj", 25), ("b256", 9), ("base", 10), ("bu", 10), ("bv", 10),
+               ("lt", 10), ("lu", 10), ("lw", 10), ("ss", 9), ("dd0", 9), ("dd1", 9), ("dev1", 9), ("kk", 9), ("kd", 9),
+               ("kb", 9), ("bdr", 27), ("dl", 2), ("fc", 8), ("jk", 25), ("ft", 25), ("fe", 1), ("fu1", 25), ("fu2", 25),
+               ("fv", 25), ("fw1", 25), ("fw2", 25), ("fw", 25)):
+    SCRATCH[_n] = ("sbuf", [128, _c], "float32")
+for _b in range(8):
+    SCRATCH["ps%d" % _b] = ("psum", [128, 512], "float32")
+
+SEMAPHORES = ["sV", "sS", "sT", "sG", "loc", "out", "h0", "h1", "h2", "a0", "a1", "a2"] + ["d%d" % _i for _i in range(14)]
+
+A = AluOpType
+F = ActivationFunctionType
+
+
+def _bits(engs):
+    m = 0
+    for e in engs:
+        m |= 1 << e
+    return m
+
+
+def _halo_engines(T, topo, q, side):
+    engs = topo.engines(T.cores[q], T.cores[q + side])
+    if 0 < q < N - 1:
+        h = len(engs) // 2
+        return engs[:h] if side < 0 else engs[h:]
+    return engs
+
+
+def _all_mask(T, topo, q):
+    m = -1
+    for o in range(N):
+        if o != q:
+            m &= topo.mask(T.cores[q], T.cores[o])
+    return m
+
+
+def rank_program(g, core, T, topo):
+    r = T.rank_of(core)
+    if r is None:
+        return
+    V = g.vector
+    queue = {"V": g.vector, "S": g.scalar, "T": g.tensor, "G": g, "Y": g.sync}
+    known = {k: {} for k in queue}
+    total, waited, wr, rd = {}, {}, {}, {}
+    nd = [0]
+
+    def need(q, reads, writes):
+        evs = {}
+        cand = [wr[k] for k in reads if k in wr] + [wr[k] for k in writes if k in wr]
+        for k in writes:
+            cand += rd.get(k, [])
+        for ev in cand:
+            if ev[0] not in evs or evs[ev[0]][1] < ev[1]:
+                evs[ev[0]] = ev
+        for s, ev in evs.items():
+            if any(o[2].get(s, 0) >= ev[1] for s2, o in evs.items() if s2 != s):
+                continue
+            if known[q].get(s, 0) < ev[1]:
+                queue[q].wait_ge(T.sem[s], ev[1])
+                waited[s] = max(waited.get(s, 0), ev[1])
+        for s, ev in evs.items():
+            known[q][s] = max(known[q].get(s, 0), ev[1])
+            for s2, v in ev[2].items():
+                known[q][s2] = max(known[q].get(s2, 0), v)
+
+    def done(q, s, n, reads, writes):
+        total[s] = total.get(s, 0) + n
+        ev = (s, total[s], dict(known[q]))
+        for k in reads:
+            rd.setdefault(k, []).append(ev)
+        for k in writes:
+            wr[k] = ev
+            rd[k] = []
+
+    def op(q, fn, reads, writes):
+        need(q, reads, writes)
+        fn().then_inc(T.sem["s" + q], 1)
+        done(q, "s" + q, 1, reads, writes)
+
+    def load(q, out, in_, key, reads=()):
+        s = "d%d" % nd[0]
+        nd[0] += 1
+        need(q, list(reads), [])
+        queue[q].dma_start(out, in_).then_inc(T.sem[s], 16)
+        done(q, s, 16, [], [key])
+
+    def store(q, out, in_, reads):
+        need(q, reads, [])
+        queue[q].dma_start(out, in_).then_inc(T.sem.out, 16)
+        total["out"] = total.get("out", 0) + 16
+
+    def arrives(key, s, n):
+        total[s] = n
+        wr[key] = (s, n, {})
+
+    def ts(out, in0, s1, s2, o0, o1, reads, writes):
+        if s2 is None:
+            op("V", lambda: V.tensor_scalar(out, in0, s1, None, o0), reads, writes)
+        else:
+            op("V", lambda: V.tensor_scalar(out, in0, s1, s2, o0, o1), reads, writes)
+
+    def tt(out, in0, in1, o, reads, writes):
+        op("V", lambda: V.tensor_tensor(out, in0, in1, o), reads, writes)
+
+    def turn(out, in_, reads, key):
+        op("V", lambda: V.transpose(out, in_), reads, [key])
+
+    def fill(ap, c, *keys):
+        op("V", lambda: V.memset(ap, c), [], list(keys))
+
+    def lin(out, in_, scale, bias, reads, writes):
+        op("S", lambda: g.scalar.activation(out, in_, F.Identity, bias=float(bias), scale=float(scale)), reads, writes)
+
+    def iota(out, pat, base, cm, key, flt=True):
+        if flt:
+            op("G", lambda: g.iota(out, pat, base, cm, allow_small_or_imprecise_dtypes=True), [], [key])
+        else:
+            op("G", lambda: g.iota(out, pat, base, cm), [], [key])
+
+    def quant(name, a, n, src, reads, key):
+        op("V", lambda: V.quantize_mx(T[name][:, a:a + n], T[name + "s"][:, a:a + n], src), reads, [key])
+
+    def mm(bank, ln, la, rn, ra, n, reads):
+        op("T", lambda: g.tensor.matmul_mx(T["ps%d" % bank][:, 0:n], T[ln][:, la:la + 128], T[ln + "s"][:, la:la + 128],
+                                           T[rn][:, ra:ra + n], T[rn + "s"][:, ra:ra + n], True, True),
+           reads, ["ps%d" % bank])
+
+    def dst(o):
+        rid, pid = topo.addr(T.cores[o], core)
+        return DstId(rid=rid, pnc=pid)
+
+    sides = [s for s in (-1, 1) if 0 <= r + s < N]
+
+    def halo(t, src, dname, n, from_to, reads):
+        need("G", reads, [])
+        for codes in (True, False):
+            trs = []
+            for s in sides:
+                a, b = from_to[s]
+                if codes:
+                    i, o = T[src][:, a:a + n].bitcast(dt.uint8), T[dname][:, b:b + n].bitcast(dt.uint8)
+                else:
+                    i, o = T[src + "s"][:, a:a + n], T[dname + "s"][:, b:b + n]
+                engs = _halo_engines(T, topo, r, s)
+                trs.append(RemoteDMATransfer(dst_ids=[dst(r + s)], dma_engine_mask=_bits(engs),
+                                             remote_sem=T.sem["h%d" % t], src=i, dst=o))
+                total["loc"] = total.get("loc", 0) + len(engs)
+            g.remote_dma_fused(trs, local_sem=T.sem.loc)
+        arrives("arr%d" % t, "h%d" % t, sum(2 * len(_halo_engines(T, topo, r + s, -s)) for s in sides))
+
+    def share(t):
+        ct, cd = T["ct%d" % t], T["cd%d" % t]
+        for a in range(4):
+            turn(ct[0:32, 32 * a:32 * a + 32], T.cown[32 * a:32 * a + 32, 32 * t:32 * t + 32],
+                 ["c%d_%d" % (t, j) for j in range(4)], "ct%d_%d" % (t, a))
+        load("S", cd[r], ct[0:4, 0:128], "cd%d" % t, ["ct%d_%d" % (t, a) for a in range(4)])
+        need("G", ["cd%d" % t], [])
+        others = [(r + k) % N for k in range(1, N)]
+        m = _all_mask(T, topo, r)
+        g.remote_dma_fused([RemoteDMATransfer(dst_ids=[dst(o) for o in others], dma_engine_mask=m,
+                                              remote_sem=T.sem["a%d" % t], srcs=[cd[r]], dsts=[cd[r] for o in others])],
+                           local_sem=T.sem.loc)
+        total["loc"] = total.get("loc", 0) + bin(m).count("1")
+        arrives("ag%d" % t, "a%d" % t, sum(bin(_all_mask(T, topo, o)).count("1") for o in others))
+        load("Y", T["yt%d" % t][0:32, 0:128], cd[:], "yt%d" % t, ["cd%d" % t, "ag%d" % t])
+
+    def cost(t, j, name, a, reads):
+        mm(4 + j, name, a, "qa", 0, 128, reads + ["qa"])
+        op("S", lambda: g.scalar.activation(T.junk[:, 128 * j:128 * j + 128], T["ps%d" % (4 + j)][:, 0:128], F.Sign,
+                                            bias=T.tiny[:, 0:1], accum_out=T.cown[:, 32 * t + j:32 * t + j + 1]),
+           ["tiny"], ["ps%d" % (4 + j), "junk%d" % j, "c%d_%d" % (t, j)])
+
+    def make(h, src, a, n, reads):
+        for b in range(4):
+            mm(b, "qw", 128 * b, src, a, n, reads + ["qw%d" % (b // 2)])
+        for b in range(4):
+            o, i = T[h][:, b:4 * n:4], T["ps%d" % b][:, 0:n]
+            if b % 2 == 0:
+                ts(o, i, 0.0, 0.0625, A.max, A.mult, [], ["ps%d" % b, h + "_%d" % b])
+            else:
+                op("S", lambda: g.scalar.activation(o, i, F.Relu, scale=0.0625), [], ["ps%d" % b, h + "_%d" % b])
+        return [h + "_%d" % b for b in range(4)]
+
+    def interior(t):
+        h = "hi%d" % t
+        if t == 0:
+            keys = make(h, "e0", 128 + 2 * S, P, ["e0b"])
+        else:
+            keys = make(h, "m%d" % (t - 1), I0, P, ["mi%d" % (t - 1)])
+        if t < R - 1:
+            n = 4 * S * (t + 1)
+            ts(T[h][:, 0:n], T[h][:, 0:n], 2.0 ** 31, None, A.min, None, keys, [h + "l"])
+            ts(T[h][:, 4 * P - n:4 * P], T[h][:, 4 * P - n:4 * P], 2.0 ** 31, None, A.min, None, keys, [h + "r"])
+            keys = keys + [h + "l", h + "r"]
+        quant("m%d" % t, I0 if t < R - 1 else 0, P, T[h][:, 0:4 * P], keys, "mi%d" % t)
+        if t < R - 1:
+            cost(t + 1, 1, "m%d" % t, I0, ["mi%d" % t])
+            cost(t + 1, 2, "m%d" % t, I0 + 128, ["mi%d" % t])
+
+    def edge(t):
+        h = "he%d" % t
+        if t == 0:
+            keys = make(h, "e0", 128 - 2 * S, 2 * W, ["e0a", "e0b", "arr0", "e0z", "e0zs"])
+        else:
+            keys = make(h, "e%d" % t, 8, 2 * W, ["ec%d" % t, "es%d" % t])
+        if t < R - 1:
+            quant("m%d" % t, MR, 2 * W, T[h][:, 0:8 * W], keys, "me%d" % t)
+            halo(t + 1, "m%d" % t, "m%d" % t, W, {-1: (ML, MA), 1: (MR, 0)}, ["me%d" % t])
+            cost(t + 1, 0, "m%d" % t, MA - 128, ["me%d" % t])
+            cost(t + 1, 3, "m%d" % t, ML - 128, ["me%d" % t, "mi%d" % t])
+            share(t + 1)
+        else:
+            quant("m%d" % t, FR, 2 * W + 2, T[h][:, 0:8 * W + 8], keys + ["hez"], "me%d" % t)
+
+    def pick(t):
+        m, e, off = "m%d" % (t - 1), "e%d" % t, T["off%d" % t][:, 0:10]
+        reads = ["mi%d" % (t - 1), "me%d" % (t - 1), "arr%d" % t, "off%d" % t]
+        op("V", lambda: V.tensor_copy(T[e][:, 0:160].bitcast(dt.uint32), T[m][:, 0:MA + W].bitcast(dt.uint32).indirect(off)),
+           reads, ["ec%d" % t])
+        op("S", lambda: g.scalar.activation(T[e + "s"][:, 0:160], T[m + "s"][:, 0:MA + W].indirect(off), F.Copy),
+           reads, ["es%d" % t])
+
+    def borders(t):
+        cg, dm, key = T["yt%d" % t], ("dm0" if t == 0 else "dm1"), "yt%d" % t
+        if t > 0:
+            tt(T.zz[0:32, :], cg[0:32, :], T.cap[0:32, :], A.min, [key, "cap"], ["zz"])
+            cg, key = T.zz, "zz"
+        op("V", lambda: V.tensor_tensor_scan(T.pref[0:32, 1:129], cg[0:32, 0:128], T.cadd[0:32, 0:128], 0.0, A.add, A.add),
+           [key, "cadd"], ["pref"])
+        ts(T.mx[0:32, :], T.wtm[0:32, :], T.pref[0:32, 128:129], None, A.mult, None, ["wtm", "pref"], ["mx"])
+        turn(T.mt[0:32, :], T.mx[0:32, :], ["mx"], "mt")
+        op("V", lambda: V.tensor_reduce(T.th[0:32, :], T.mt[0:32, :], AxisListType.X, A.add), ["mt"], ["th"])
+        w0 = 0 if t == 0 else 128 - W
+        ts(T.ind[0:32, w0:128], T.pref[0:32, w0:128], T.th[0:32, 0:1], None, A.is_lt, None, ["pref", "pref0", "th"], ["ind"])
+        op("V", lambda: V.tensor_reduce(T.cnt[0:32, :], T.ind[0:32, w0:128], AxisListType.X, A.add), ["ind"], ["cnt"])
+        ts(T.cl[0:32, :], T.amat[0:32, :], T.cnt[0:32, 0:1], T.bcol[0:32, 0:1], A.max, A.min, ["amat", "bcol", "cnt"], ["cl"])
+        for a in range(4):
+            turn(T[dm][32 * a:32 * a + 32, 32:64], T.cl[0:32, :], ["cl"], dm + "_%d" % a)
+        return T[dm], [dm + "_%d" % a for a in range(4)] + [dm + "a", dm + "b"]
+
+    def bounds():
+        turn(T.amat[0:32, :], T.ar[0:32, :], ["ar0", "ar3", "ar"], "amat")
+        ts(T.bcol[0:32, :], T.amat[0:32, 0:1], float(S), None, A.add, None, ["amat"], ["bcol"])
+
+    def after(t):
+        dm, keys = borders(t)
+        d, dk = T["dd%d" % t], "dd%d" % t
+        tt(T.ss[:], dm[:, 31:64:4], dm[:, 32:65:4], A.add, keys, ["ss"])
+        if t == 0:
+            ts(d[:], T.ss[:], -128.0, None, A.add, None, ["ss"], [dk])
+            dr, dlf = -2.0 * S, float(I0 - S - ML)
+        else:
+            tt(d[:], T.ss[:], T.kk[:], A.subtract, ["ss", "kk"], [dk])
+            dr, dlf = T.dl[:, 0:1], T.dl[:, 1:2]
+        ts(T.lt[:, 0:5], T.base[:, 0:5], d[:, r + 1:r + 2], None, A.add, None, ["base", dk], ["ltr"])
+        ts(T.lt[:, 5:10], T.base[:, 5:10], d[:, r:r + 1], None, A.add, None, ["base", dk], ["ltl"])
+        ts(T.lu[:, 0:5], T.lt[:, 0:5], float(MR), dr, A.is_lt, A.mult, ["ltr", "dl0"], ["lur"])
+        ts(T.lu[:, 5:10], T.lt[:, 5:10], float(MA), dlf, A.is_ge, A.mult, ["ltl", "dl1"], ["lul"])
+        tt(T.lw[:], T.lt[:], T.lu[:], A.add, ["ltr", "ltl", "lur", "lul"], ["lw"])
+        op("V", lambda: V.tensor_copy(T["off%d" % (t + 1)][:], T.lw[:]), ["lw"], ["off%d" % (t + 1)])
+
+    def prepare(t):
+        d, dk = T["dd%d" % t], "dd%d" % t
+        w0 = 128 - W
+        lin(T.xl[0:32, 0:32:4], d[0:32, 0:8], 1, w0 + S, [dk], ["xl0"])
+        lin(T.xl[0:32, 3:32:4], d[0:32, 1:9], -1, 1 - w0 - 2 * S, [dk], ["xl3"])
+        lin(T.ar[0:32, 0:32:4], d[0:32, 0:8], 1, S, [dk], ["ar0"])
+        lin(T.ar[0:32, 3:32:4], d[0:32, 1:9], 1, S, [dk], ["ar3"])
+        lin(T.kk[:], d[:], 2, W, [dk], ["kk"])
+        if t == 0:
+            lin(T.dl[:, 0:1], d[:, r + 1:r + 2], 1, -2 * S, [dk], ["dl0"])
+            lin(T.dl[:, 1:2], d[:, r:r + 1], 1, I0 - S - ML, [dk], ["dl1"])
+            tt(T.bdr[:, 0:9], d[:], T.b256[:], A.add, [dk, "b256"], ["bd0"])
+        else:
+            tt(T.dev1[:], d[:], T.dd0[:], A.add, [dk, "dd0"], ["dev1"])
+            tt(T.bdr[:, 9:18], T.dev1[:], T.b256[:], A.add, ["dev1", "b256"], ["bd1"])
+        turn(T.xlt[0:32, :], T.xl[0:32, :], ["xl0", "xl1", "xl2", "xl3"], "xlt")
+        bounds()
+        ts(T.val[0:32, :], T.ppt[0:32, :], T.xlt[0:32, 0:1], 400.0, A.is_ge, A.mult,
+           ["xlt"] + ["ppt%d" % a for a in range(4)], ["val"])
+        ts(T.cap[0:32, :], T.val[0:32, :], -130.0, None, A.add, None, ["val"], ["cap"])
+        if t == 0:
+            lin(T.xl[0:32, 1:32:4], T.dd0[0:32, 0:8], 1, 2 * S, ["dd0"], ["xl1"])
+            lin(T.xl[0:32, 2:32:4], T.dd0[0:32, 1:9], -1, 1 - 128 + 2 * S, ["dd0"], ["xl2"])
+
+    load("Y", T.xe[:, 0:4 * S], T.x[:, 4 * (P - S):4 * P], "xer")
+    load("S", T.xe[:, 4 * S:8 * S], T.x[:, 0:4 * S], "xel")
+    load("Y", T.xt[:], T.x[:, :], "xt")
+    load("S", T.at[:], T.a[:, :], "at")
+    load("Y", T.wt[:, 0:1024], T.w[:, 0:1024], "wt0")
+    load("S", T.wt[:, 1024:2048], T.w[:, 1024:2048], "wt1")
+
+    iota(T.pint[:, 0:1], [[1, 1]], 0, 1, "pint0", False)
+    iota(T.j0[:], [[16, 25]], 0, 0, "j0")
+    iota(T.pcol[:], [[1, 1]], 0, 1, "pcol")
+    iota(T.i1[0:32, :], [[1, 9], [0, 4]], 0, 0, "i1")
+    iota(T.i2[0:32, :], [[1, 32]], 0, -1, "i2")
+    iota(T.b256[:], [[P, 9]], 0, 0, "b256")
+    fill(T.xe[:, 8 * S:512], 0.0, "xez")
+    fill(T.tiny[:], -2.0 ** -120, "tiny")
+    fill(T.cown[:], -130.0, *["c%d_%d" % (t, j) for t in range(R) for j in range(4)])
+    fill(T.he2[:, 8 * W:8 * W + 8], 0.0, "hez")
+    fill(T.cadd[0:32, :], 130.0, "cadd")
+    fill(T.pref[0:32, 0:1], 0.0, "pref0")
+    fill(T.dm0[:, 31:32], 128.0, "dm0a")
+    fill(T.dm0[:, 64:65], 0.0, "dm0b")
+    fill(T.dm1[:, 31:32], 2.0 * S, "dm1a")
+    fill(T.dm1[:, 64:65], 1.0 * S, "dm1b")
+    fill(T.ar[0:32, :], 0.0, "ar")
+    fill(T.sg[:], 1.0, "sg")
+    fill(T.xl[0:32, 1:32:4], 2.0 * S, "xl1")
+    fill(T.xl[0:32, 2:32:4], 1.0 - 128 + 2 * S, "xl2")
+    op("V", lambda: V.memset(T.ar[0:32, 3:32:4], 128.0 - S), ["ar"], ["ar3"])
+    op("V", lambda: V.memset(T.sg[:, 2:32:4], -1.0), ["sg"], ["sg2"])
+    op("V", lambda: V.memset(T.sg[:, 3:32:4], -1.0), ["sg"], ["sg3"])
+
+    quant("qxe", 0, 128, T.xe[:], ["xer", "xel", "xez"], "qxe")
+    halo(0, "qxe", "e0", S, {-1: (S, 128), 1: (0, 128 + S)}, ["qxe"])
+    if len(sides) == 1:
+        z = 128 + S if r == 0 else 128
+        load("Y", T.e0[:, z:z + S].bitcast(dt.uint8), T.qxe[:, 2 * S:3 * S].bitcast(dt.uint8), "e0z", ["qxe"])
+        load("Y", T.e0s[:, z:z + S], T.qxes[:, 2 * S:3 * S], "e0zs", ["qxe"])
+
+    ts(T.pint[:, 1:2], T.pint[:, 0:1], 15, None, A.bitwise_and, None, ["pint0"], ["pint1"])
+    ts(T.pp[:], T.sg[:], T.pcol[:, 0:1], None, A.mult, None, ["sg", "sg2", "sg3", "pcol"], ["pp"])
+    ts(T.wa[0:32, :], T.i2[0:32, :], 0.0, None, A.is_gt, None, ["i2"], ["wa"])
+    ts(T.wb[0:32, :], T.i1[0:32, 1:33], 1.0 / N, None, A.mult, None, ["i1"], ["wb"])
+    op("V", lambda: V.tensor_copy(T.p16[:], T.pint[:, 1:2]), ["pint1"], ["p16"])
+    quant("e0", 128 + 2 * S, P, T.xt[:], ["xt"], "e0b")
+    quant("qa", 0, 128, T.at[:], ["at"], "qa")
+    cost(0, 0, "e0", 128 + 2 * S, ["e0b"])
+    cost(0, 3, "e0", 256 + 2 * S, ["e0b"])
+    quant("e0", 0, 128, T.xt[:, 512:1024], ["xt"], "e0a")
+    op("V", lambda: V.memset(T.pp[0:32, 3:32:4], -1000.0), ["pp"], ["ppa"])
+    op("V", lambda: V.memset(T.pp[32:128 - W, 3:32:4], -1000.0), ["pp"], ["ppb"])
+    tt(T.wtm[0:32, :], T.wb[0:32, :], T.wa[0:32, :], A.subtract, ["wa", "wb"], ["wtm"])
+    ts(T.jj[:], T.j0[:], T.p16[:, 0:1], None, A.add, None, ["j0", "p16"], ["jj"])
+    share(0)
+    quant("qw", 0, 256, T.wt[:, 0:1024], ["wt0"], "qw0")
+    quant("qw", 256, 256, T.wt[:, 1024:2048], ["wt1"], "qw1")
+    interior(0)
+    edge(0)
+    bounds()
+    ts(T.bu[:, 0:5], T.jj[:, 0:5], 8.0 + 2 * S, 0.0 if r == N - 1 else float(MA - S - MR), A.is_ge, A.mult, ["jj"], ["bur"])
+    ts(T.bu[:, 5:10], T.jj[:, 0:5], float(S), 0.0 if r == 0 else float(S - ML), A.is_lt, A.mult, ["jj"], ["bul"])
+    ts(T.bv[:, 0:5], T.jj[:, 0:5], float(MR - 8), None, A.add, None, ["jj"], ["bvr"])
+    ts(T.bv[:, 5:10], T.jj[:, 0:5], float(ML), None, A.add, None, ["jj"], ["bvl"])
+    tt(T.base[:], T.bu[:], T.bv[:], A.add, ["bur", "bul", "bvr", "bvl"], ["base"])
+    interior(1)
+    after(0)
+    pick(1)
+    edge(1)
+    for a in range(4):
+        turn(T.ppt[0:32, 32 * a:32 * a + 32], T.pp[32 * a:32 * a + 32, :], ["pp", "ppa", "ppb"], "ppt%d" % a)
+    prepare(0)
+    after(1)
+    interior(2)
+    mm(5, "qa", 0, "m2", 0, P, ["qa", "mi2"])
+    op("S", lambda: g.scalar.activation(T.ys[:, 0:P], T.ps5[:, 0:P], F.Copy), [], ["ps5", "ysi"])
+    pick(2)
+    edge(2)
+    mm(6, "qa", 0, "m2", FR, 2 * W + 2, ["qa", "me2"])
+    prepare(1)
+    op("S", lambda: g.scalar.activation(T.ys[:, FR:FZ + 2], T.ps6[:, 0:2 * W + 2], F.Copy), [], ["ps6", "yse"])
+    tt(T.kd[:], T.dev1[:], T.kk[:], A.subtract, ["dev1", "kk"], ["kd"])
+    tt(T.kb[:], T.bdr[:, 9:18], T.kk[:], A.subtract, ["bd1", "kk"], ["kb"])
+    lin(T.fc[:, 0:1], T.dev1[:, r:r + 1], 1, 2 * S, ["dev1"], ["fc0"])
+    lin(T.fc[:, 1:2], T.dev1[:, r:r + 1], -1, FL + S, ["dev1"], ["fc1"])
+    lin(T.fc[:, 2:3], T.dev1[:, r + 1:r + 2], 1, P - 2 * S, ["dev1"], ["fc2"])
+    lin(T.fc[:, 3:4], T.dev1[:, r + 1:r + 2], -1, FR - P + 2 * S, ["dev1"], ["fc3"])
+    lin(T.fc[:, 4:5], T.kd[:, r + 1:r + 2], 1, P, ["kd"], ["fc4"])
+    op("S", lambda: g.scalar.activation(T.jk[:], T.jj[:], F.Identity, bias=T.kd[:, r:r + 1]), ["jj", "kd"], ["jk"])
+    dm, keys = borders(2)
+    ca, cb = 31 + 4 * r, 32 + 4 * r
+    ts(T.ft[:], T.jk[:], dm[:, ca:ca + 1], dm[:, cb:cb + 1], A.add, A.add, keys + ["jk"], ["ft"])
+    ts(T.fe[:], T.fc[:, 4:5], dm[:, ca + 4:ca + 5], dm[:, cb + 4:cb + 5], A.add, A.add, keys + ["fc4"], ["fe"])
+    ts(T.fu1[:], T.ft[:], T.fc[:, 0:1], T.fc[:, 1:2], A.is_lt, A.mult, ["ft", "fc0", "fc1"], ["fu1"])
+    ts(T.fu2[:], T.ft[:], T.fc[:, 2:3], T.fc[:, 3:4], A.is_ge, A.mult, ["ft", "fc2", "fc3"], ["fu2"])
+    ts(T.fv[:], T.ft[:], T.fe[:, 0:1], 1000.0, A.is_ge, A.mult, ["ft", "fe"], ["fv"])
+    tt(T.fw1[:], T.ft[:], T.fu1[:], A.add, ["ft", "fu1"], ["fw1"])
+    tt(T.fw2[:], T.fu2[:], T.fv[:], A.add, ["fu2", "fv"], ["fw2"])
+    tt(T.fw[:], T.fw1[:], T.fw2[:], A.add, ["fw1", "fw2"], ["fw"])
+    ts(T.off3[:, 0:25], T.fw[:], float(FZ), None, A.min, None, ["fw"], ["off3"])
+
+    reads = ["mi2", "me2", "off3"]
+    off = T.off3[:, 0:25]
+    op("V", lambda: V.tensor_copy(T.fin[:, 0:E].bitcast(dt.uint32), T.m2[:, 0:FZ + 2].bitcast(dt.uint32).indirect(off)),
+       reads, ["fin"])
+    op("S", lambda: g.scalar.activation(T.yo[:, 0:E], T.ys[:, 0:FZ + 2].indirect(off), F.Copy), ["ysi", "yse", "off3"], ["yo"])
+    hs = 192
+    op("V", lambda: V.tensor_copy(T.fins[:, 0:hs], T.m2s[:, 0:FZ + 2].indirect(T.off3[:, 0:12])), reads, ["fina"])
+    op("S", lambda: g.scalar.activation(T.fins[:, hs:E], T.m2s[:, 0:FZ + 2].indirect(T.off3[:, 12:25]), F.Copy),
+       reads, ["finb"])
+    tt(T.ss[:], dm[:, 31:64:4], dm[:, 32:65:4], A.add, keys, ["ss"])
+    tt(T.bdr[:, 18:27], T.ss[:], T.kb[:], A.add, ["ss", "kb"], ["bd2"])
+    store("Y", T.oc[:, :], T.fin[:, 0:E].bitcast(dt.uint8), ["fin"])
+    store("Y", T.y[:, :], T.yo[:, 0:E], ["yo"])
+    for k in range(4):
+        store("Y" if k < 2 else "S", T.osc[4 * k:4 * k + 4, :], T.fins[32 * k:32 * k + 4, 0:E], ["fina", "finb"])
+    store("S", T.bd[:, :], T.bdr[0:1, 0:27], ["bd0", "bd1", "bd2"])
+
+    for s in SEMAPHORES:
+        if s != "out" and total.get(s, 0) > waited.get(s, 0):
+            g.wait_ge(T.sem[s], total[s])
+    g.wait_ge(T.sem.out, total["out"])

@@ -29,12 +29,9 @@ for _n, _c in (("qxe", 128), ("qa", 128), ("qw", 512), ("e0", 128 + 2 * S + P), 
 for _t in range(R):
     SCRATCH["hi%d" % _t] = ("sbuf", [128, 4 * P], "bfloat16")
     SCRATCH["he%d" % _t] = ("sbuf", [128, 4 * (2 * W + 2)], "bfloat16")
-    SCRATCH["ct%d" % _t] = ("sbuf", [128, 128], "float32")
-    SCRATCH["yt%d" % _t] = ("sbuf", [128, 128], "float32")
-    SCRATCH["cd%d" % _t] = ("dram", [N, 128, 4], "float32")
+    SCRATCH["cg%d" % _t] = ("sbuf", [128, 32], "float32")
 for _n, _c in (("tiny", 1), ("cadd", 128), ("pref", 132), ("dm0", 96), ("dm1", 96), ("ar", 32), ("amat", 32), ("bcol", 1),
-               ("xl", 32), ("xlt", 32), ("sg", 32), ("pp", 32), ("ppt", 128), ("val", 128), ("cap", 128), ("zz", 128),
-               ("cown", 96), ("mx", 32), ("mt", 32),
+               ("xl", 32), ("sg", 32), ("pp", 32), ("val", 32), ("cap", 32), ("zz", 32), ("yt", 128), ("mx", 32), ("mt", 32),
                ("th", 1), ("ind", 128), ("cnt", 1), ("cl", 32), ("wtm", 32), ("i1", 36), ("i2", 32), ("wa", 32), ("wb", 32),
                ("pcol", 1), ("p16", 1), ("j0", 25), ("jj", 25), ("b256", 9), ("base", 10), ("bu", 10), ("bv", 10),
                ("lt", 10), ("lu", 10), ("lw", 10), ("ss", 9), ("dd0", 9), ("dd1", 9), ("dev1", 9), ("kk", 9), ("kd", 9),
@@ -44,7 +41,7 @@ for _n, _c in (("tiny", 1), ("cadd", 128), ("pref", 132), ("dm0", 96), ("dm1", 9
 for _b in range(8):
     SCRATCH["ps%d" % _b] = ("psum", [128, 512], "float32")
 
-SEMAPHORES = ["sV", "sS", "sT", "sG", "loc", "out", "h0", "h1", "h2", "a0", "a1", "a2"] + ["d%d" % _i for _i in range(14)]
+SEMAPHORES = ["sV", "sS", "sT", "sG", "loc", "out", "h0", "h1", "h2", "a0", "a1", "a2"] + ["d%d" % _i for _i in range(8)]
 
 A = AluOpType
 F = ActivationFunctionType
@@ -144,8 +141,8 @@ def rank_program(g, core, T, topo):
     def turn(out, in_, reads, key):
         op("V", lambda: V.transpose(out, in_), reads, [key])
 
-    def fill(ap, c, *keys):
-        op("V", lambda: V.memset(ap, c), [], list(keys))
+    def fill(ap, c, key):
+        op("V", lambda: V.memset(ap, c), [], [key])
 
     def lin(out, in_, scale, bias, reads, writes):
         op("S", lambda: g.scalar.activation(out, in_, F.Identity, bias=float(bias), scale=float(scale)), reads, writes)
@@ -188,25 +185,20 @@ def rank_program(g, core, T, topo):
         arrives("arr%d" % t, "h%d" % t, sum(2 * len(_halo_engines(T, topo, r + s, -s)) for s in sides))
 
     def share(t):
-        ct, cd = T["ct%d" % t], T["cd%d" % t]
-        for a in range(4):
-            turn(ct[0:32, 32 * a:32 * a + 32], T.cown[32 * a:32 * a + 32, 32 * t:32 * t + 32],
-                 ["c%d_%d" % (t, j) for j in range(4)], "ct%d_%d" % (t, a))
-        load("S", cd[r], ct[0:4, 0:128], "cd%d" % t, ["ct%d_%d" % (t, a) for a in range(4)])
-        need("G", ["cd%d" % t], [])
+        need("G", ["c%d_%d" % (t, j) for j in range(4)], [])
+        slot = T["cg%d" % t][:, 4 * r:4 * r + 4]
         others = [(r + k) % N for k in range(1, N)]
         m = _all_mask(T, topo, r)
         g.remote_dma_fused([RemoteDMATransfer(dst_ids=[dst(o) for o in others], dma_engine_mask=m,
-                                              remote_sem=T.sem["a%d" % t], srcs=[cd[r]], dsts=[cd[r] for o in others])],
+                                              remote_sem=T.sem["a%d" % t], srcs=[slot], dsts=[slot for o in others])],
                            local_sem=T.sem.loc)
         total["loc"] = total.get("loc", 0) + bin(m).count("1")
         arrives("ag%d" % t, "a%d" % t, sum(bin(_all_mask(T, topo, o)).count("1") for o in others))
-        load("Y", T["yt%d" % t][0:32, 0:128], cd[:], "yt%d" % t, ["cd%d" % t, "ag%d" % t])
 
     def cost(t, j, name, a, reads):
         mm(4 + j, name, a, "qa", 0, 128, reads + ["qa"])
         op("S", lambda: g.scalar.activation(T.junk[:, 128 * j:128 * j + 128], T["ps%d" % (4 + j)][:, 0:128], F.Sign,
-                                            bias=T.tiny[:, 0:1], accum_out=T.cown[:, 32 * t + j:32 * t + j + 1]),
+                                            bias=T.tiny[:, 0:1], accum_out=T["cg%d" % t][:, 4 * r + j:4 * r + j + 1]),
            ["tiny"], ["ps%d" % (4 + j), "junk%d" % j, "c%d_%d" % (t, j)])
 
     def make(h, src, a, n, reads):
@@ -244,10 +236,14 @@ def rank_program(g, core, T, topo):
             keys = make(h, "e%d" % t, 8, 2 * W, ["ec%d" % t, "es%d" % t])
         if t < R - 1:
             quant("m%d" % t, MR, 2 * W, T[h][:, 0:8 * W], keys, "me%d" % t)
-            halo(t + 1, "m%d" % t, "m%d" % t, W, {-1: (ML, MA), 1: (MR, 0)}, ["me%d" % t])
+            ends = {-1: (ML, MA), 1: (MR, 0)}
+            if t == 0:
+                halo(t + 1, "m%d" % t, "m%d" % t, W, ends, ["me%d" % t])
             cost(t + 1, 0, "m%d" % t, MA - 128, ["me%d" % t])
             cost(t + 1, 3, "m%d" % t, ML - 128, ["me%d" % t, "mi%d" % t])
             share(t + 1)
+            if t > 0:
+                halo(t + 1, "m%d" % t, "m%d" % t, W, ends, ["me%d" % t])
         else:
             quant("m%d" % t, FR, 2 * W + 2, T[h][:, 0:8 * W + 8], keys + ["hez"], "me%d" % t)
 
@@ -260,12 +256,15 @@ def rank_program(g, core, T, topo):
            reads, ["es%d" % t])
 
     def borders(t):
-        cg, dm, key = T["yt%d" % t], ("dm0" if t == 0 else "dm1"), "yt%d" % t
+        cg, dm = T["cg%d" % t], ("dm0" if t == 0 else "dm1")
+        reads = ["ag%d" % t] + ["c%d_%d" % (t, j) for j in range(4)]
         if t > 0:
-            tt(T.zz[0:32, :], cg[0:32, :], T.cap[0:32, :], A.min, [key, "cap"], ["zz"])
-            cg, key = T.zz, "zz"
-        op("V", lambda: V.tensor_tensor_scan(T.pref[0:32, 1:129], cg[0:32, 0:128], T.cadd[0:32, 0:128], 0.0, A.add, A.add),
-           [key, "cadd"], ["pref"])
+            tt(T.zz[:], cg[:], T.cap[:], A.min, reads + ["cap"], ["zz"])
+            cg, reads = T.zz, ["zz"]
+        for a in range(4):
+            turn(T.yt[0:32, 32 * a:32 * a + 32], cg[32 * a:32 * a + 32, 0:32], reads, "yt%d" % a)
+        op("V", lambda: V.tensor_tensor_scan(T.pref[0:32, 1:129], T.yt[0:32, 0:128], T.cadd[0:32, 0:128], 0.0, A.add, A.add),
+           ["yt%d" % a for a in range(4)] + ["cadd"], ["pref"])
         ts(T.mx[0:32, :], T.wtm[0:32, :], T.pref[0:32, 128:129], None, A.mult, None, ["wtm", "pref"], ["mx"])
         turn(T.mt[0:32, :], T.mx[0:32, :], ["mx"], "mt")
         op("V", lambda: V.tensor_reduce(T.th[0:32, :], T.mt[0:32, :], AxisListType.X, A.add), ["mt"], ["th"])
@@ -281,16 +280,18 @@ def rank_program(g, core, T, topo):
         turn(T.amat[0:32, :], T.ar[0:32, :], ["ar0", "ar3", "ar"], "amat")
         ts(T.bcol[0:32, :], T.amat[0:32, 0:1], float(S), None, A.add, None, ["amat"], ["bcol"])
 
-    def after(t):
+    def moves(t):
         dm, keys = borders(t)
         d, dk = T["dd%d" % t], "dd%d" % t
         tt(T.ss[:], dm[:, 31:64:4], dm[:, 32:65:4], A.add, keys, ["ss"])
         if t == 0:
             ts(d[:], T.ss[:], -128.0, None, A.add, None, ["ss"], [dk])
-            dr, dlf = -2.0 * S, float(I0 - S - ML)
         else:
             tt(d[:], T.ss[:], T.kk[:], A.subtract, ["ss", "kk"], [dk])
-            dr, dlf = T.dl[:, 0:1], T.dl[:, 1:2]
+
+    def picklist(t):
+        d, dk = T["dd%d" % t], "dd%d" % t
+        dr, dlf = (-2.0 * S, float(I0 - S - ML)) if t == 0 else (T.dl[:, 0:1], T.dl[:, 1:2])
         ts(T.lt[:, 0:5], T.base[:, 0:5], d[:, r + 1:r + 2], None, A.add, None, ["base", dk], ["ltr"])
         ts(T.lt[:, 5:10], T.base[:, 5:10], d[:, r:r + 1], None, A.add, None, ["base", dk], ["ltl"])
         ts(T.lu[:, 0:5], T.lt[:, 0:5], float(MR), dr, A.is_lt, A.mult, ["ltr", "dl0"], ["lur"])
@@ -301,26 +302,27 @@ def rank_program(g, core, T, topo):
     def prepare(t):
         d, dk = T["dd%d" % t], "dd%d" % t
         w0 = 128 - W
-        lin(T.xl[0:32, 0:32:4], d[0:32, 0:8], 1, w0 + S, [dk], ["xl0"])
-        lin(T.xl[0:32, 3:32:4], d[0:32, 1:9], -1, 1 - w0 - 2 * S, [dk], ["xl3"])
+        lin(T.xl[:, 0:32:4], d[:, 0:8], 1, w0 + S, [dk], ["xl0"])
+        lin(T.xl[:, 3:32:4], d[:, 1:9], -1, 1 - w0 - 2 * S, [dk], ["xl3"])
         lin(T.ar[0:32, 0:32:4], d[0:32, 0:8], 1, S, [dk], ["ar0"])
         lin(T.ar[0:32, 3:32:4], d[0:32, 1:9], 1, S, [dk], ["ar3"])
         lin(T.kk[:], d[:], 2, W, [dk], ["kk"])
         if t == 0:
             lin(T.dl[:, 0:1], d[:, r + 1:r + 2], 1, -2 * S, [dk], ["dl0"])
             lin(T.dl[:, 1:2], d[:, r:r + 1], 1, I0 - S - ML, [dk], ["dl1"])
+
+    def prepare2(t):
+        d, dk = T["dd%d" % t], "dd%d" % t
+        tt(T.val[:], T.pp[:], T.xl[:], A.is_ge, ["pp", "ppa", "ppb", "xl0", "xl1", "xl2", "xl3"], ["val"])
+        if t == 0:
             tt(T.bdr[:, 0:9], d[:], T.b256[:], A.add, [dk, "b256"], ["bd0"])
         else:
-            tt(T.dev1[:], d[:], T.dd0[:], A.add, [dk, "dd0"], ["dev1"])
             tt(T.bdr[:, 9:18], T.dev1[:], T.b256[:], A.add, ["dev1", "b256"], ["bd1"])
-        turn(T.xlt[0:32, :], T.xl[0:32, :], ["xl0", "xl1", "xl2", "xl3"], "xlt")
+        ts(T.cap[:], T.val[:], 400.0, -130.0, A.mult, A.add, ["val"], ["cap"])
         bounds()
-        ts(T.val[0:32, :], T.ppt[0:32, :], T.xlt[0:32, 0:1], 400.0, A.is_ge, A.mult,
-           ["xlt"] + ["ppt%d" % a for a in range(4)], ["val"])
-        ts(T.cap[0:32, :], T.val[0:32, :], -130.0, None, A.add, None, ["val"], ["cap"])
         if t == 0:
-            lin(T.xl[0:32, 1:32:4], T.dd0[0:32, 0:8], 1, 2 * S, ["dd0"], ["xl1"])
-            lin(T.xl[0:32, 2:32:4], T.dd0[0:32, 1:9], -1, 1 - 128 + 2 * S, ["dd0"], ["xl2"])
+            lin(T.xl[:, 1:32:4], T.dd0[:, 0:8], 1, 2 * S, ["dd0"], ["xl1"])
+            lin(T.xl[:, 2:32:4], T.dd0[:, 1:9], -1, 1 - 128 + 2 * S, ["dd0"], ["xl2"])
 
     load("Y", T.xe[:, 0:4 * S], T.x[:, 4 * (P - S):4 * P], "xer")
     load("S", T.xe[:, 4 * S:8 * S], T.x[:, 0:4 * S], "xel")
@@ -337,7 +339,8 @@ def rank_program(g, core, T, topo):
     iota(T.b256[:], [[P, 9]], 0, 0, "b256")
     fill(T.xe[:, 8 * S:512], 0.0, "xez")
     fill(T.tiny[:], -2.0 ** -120, "tiny")
-    fill(T.cown[:], -130.0, *["c%d_%d" % (t, j) for t in range(R) for j in range(4)])
+    fill(T.cg0[:, 4 * r + 1:4 * r + 2], -130.0, "c0_1")
+    fill(T.cg0[:, 4 * r + 2:4 * r + 3], -130.0, "c0_2")
     fill(T.he2[:, 8 * W:8 * W + 8], 0.0, "hez")
     fill(T.cadd[0:32, :], 130.0, "cadd")
     fill(T.pref[0:32, 0:1], 0.0, "pref0")
@@ -347,8 +350,8 @@ def rank_program(g, core, T, topo):
     fill(T.dm1[:, 64:65], 1.0 * S, "dm1b")
     fill(T.ar[0:32, :], 0.0, "ar")
     fill(T.sg[:], 1.0, "sg")
-    fill(T.xl[0:32, 1:32:4], 2.0 * S, "xl1")
-    fill(T.xl[0:32, 2:32:4], 1.0 - 128 + 2 * S, "xl2")
+    fill(T.xl[:, 1:32:4], 2.0 * S, "xl1")
+    fill(T.xl[:, 2:32:4], 1.0 - 128 + 2 * S, "xl2")
     op("V", lambda: V.memset(T.ar[0:32, 3:32:4], 128.0 - S), ["ar"], ["ar3"])
     op("V", lambda: V.memset(T.sg[:, 2:32:4], -1.0), ["sg"], ["sg2"])
     op("V", lambda: V.memset(T.sg[:, 3:32:4], -1.0), ["sg"], ["sg3"])
@@ -369,74 +372,86 @@ def rank_program(g, core, T, topo):
     quant("qa", 0, 128, T.at[:], ["at"], "qa")
     cost(0, 0, "e0", 128 + 2 * S, ["e0b"])
     cost(0, 3, "e0", 256 + 2 * S, ["e0b"])
+    share(0)
     quant("e0", 0, 128, T.xt[:, 512:1024], ["xt"], "e0a")
     op("V", lambda: V.memset(T.pp[0:32, 3:32:4], -1000.0), ["pp"], ["ppa"])
     op("V", lambda: V.memset(T.pp[32:128 - W, 3:32:4], -1000.0), ["pp"], ["ppb"])
     tt(T.wtm[0:32, :], T.wb[0:32, :], T.wa[0:32, :], A.subtract, ["wa", "wb"], ["wtm"])
     ts(T.jj[:], T.j0[:], T.p16[:, 0:1], None, A.add, None, ["j0", "p16"], ["jj"])
-    share(0)
+    bounds()
     quant("qw", 0, 256, T.wt[:, 0:1024], ["wt0"], "qw0")
     quant("qw", 256, 256, T.wt[:, 1024:2048], ["wt1"], "qw1")
     interior(0)
     edge(0)
-    bounds()
     ts(T.bu[:, 0:5], T.jj[:, 0:5], 8.0 + 2 * S, 0.0 if r == N - 1 else float(MA - S - MR), A.is_ge, A.mult, ["jj"], ["bur"])
     ts(T.bu[:, 5:10], T.jj[:, 0:5], float(S), 0.0 if r == 0 else float(S - ML), A.is_lt, A.mult, ["jj"], ["bul"])
     ts(T.bv[:, 0:5], T.jj[:, 0:5], float(MR - 8), None, A.add, None, ["jj"], ["bvr"])
     ts(T.bv[:, 5:10], T.jj[:, 0:5], float(ML), None, A.add, None, ["jj"], ["bvl"])
     tt(T.base[:], T.bu[:], T.bv[:], A.add, ["bur", "bul", "bvr", "bvl"], ["base"])
     interior(1)
-    after(0)
+    moves(0)
+    prepare(0)
+    picklist(0)
+    prepare2(0)
     pick(1)
     edge(1)
-    for a in range(4):
-        turn(T.ppt[0:32, 32 * a:32 * a + 32], T.pp[32 * a:32 * a + 32, :], ["pp", "ppa", "ppb"], "ppt%d" % a)
-    prepare(0)
-    after(1)
-    interior(2)
-    mm(5, "qa", 0, "m2", 0, P, ["qa", "mi2"])
-    op("S", lambda: g.scalar.activation(T.ys[:, 0:P], T.ps5[:, 0:P], F.Copy), [], ["ps5", "ysi"])
-    pick(2)
-    edge(2)
-    mm(6, "qa", 0, "m2", FR, 2 * W + 2, ["qa", "me2"])
+    moves(1)
     prepare(1)
-    op("S", lambda: g.scalar.activation(T.ys[:, FR:FZ + 2], T.ps6[:, 0:2 * W + 2], F.Copy), [], ["ps6", "yse"])
+    tt(T.dev1[:], T.dd1[:], T.dd0[:], A.add, ["dd1", "dd0"], ["dev1"])
+    picklist(1)
+    prepare2(1)
     tt(T.kd[:], T.dev1[:], T.kk[:], A.subtract, ["dev1", "kk"], ["kd"])
-    tt(T.kb[:], T.bdr[:, 9:18], T.kk[:], A.subtract, ["bd1", "kk"], ["kb"])
     lin(T.fc[:, 0:1], T.dev1[:, r:r + 1], 1, 2 * S, ["dev1"], ["fc0"])
     lin(T.fc[:, 1:2], T.dev1[:, r:r + 1], -1, FL + S, ["dev1"], ["fc1"])
     lin(T.fc[:, 2:3], T.dev1[:, r + 1:r + 2], 1, P - 2 * S, ["dev1"], ["fc2"])
     lin(T.fc[:, 3:4], T.dev1[:, r + 1:r + 2], -1, FR - P + 2 * S, ["dev1"], ["fc3"])
     lin(T.fc[:, 4:5], T.kd[:, r + 1:r + 2], 1, P, ["kd"], ["fc4"])
     op("S", lambda: g.scalar.activation(T.jk[:], T.jj[:], F.Identity, bias=T.kd[:, r:r + 1]), ["jj", "kd"], ["jk"])
+    for b in range(4):
+        mm(b, "qw", 128 * b, "m1", I0, P, ["mi1"])
+        op("S", lambda: g.scalar.activation(T.hi2[:, b:4 * P:4], T["ps%d" % b][:, 0:P], F.Relu, scale=0.0625),
+           [], ["ps%d" % b, "hi2_%d" % b])
     dm, keys = borders(2)
+    quant("m2", 0, P, T.hi2[:, 0:4 * P], ["hi2_%d" % b for b in range(4)], "mi2")
+    mm(5, "qa", 0, "m2", 0, P, ["qa", "mi2"])
+    op("S", lambda: g.scalar.activation(T.ys[:, 0:P], T.ps5[:, 0:P], F.Copy), [], ["ps5", "ysi"])
     ca, cb = 31 + 4 * r, 32 + 4 * r
     ts(T.ft[:], T.jk[:], dm[:, ca:ca + 1], dm[:, cb:cb + 1], A.add, A.add, keys + ["jk"], ["ft"])
     ts(T.fe[:], T.fc[:, 4:5], dm[:, ca + 4:ca + 5], dm[:, cb + 4:cb + 5], A.add, A.add, keys + ["fc4"], ["fe"])
+    tt(T.ss[:], dm[:, 31:64:4], dm[:, 32:65:4], A.add, keys, ["ss"])
+    tt(T.kb[:], T.bdr[:, 9:18], T.kk[:], A.subtract, ["bd1", "kk"], ["kb"])
     ts(T.fu1[:], T.ft[:], T.fc[:, 0:1], T.fc[:, 1:2], A.is_lt, A.mult, ["ft", "fc0", "fc1"], ["fu1"])
     ts(T.fu2[:], T.ft[:], T.fc[:, 2:3], T.fc[:, 3:4], A.is_ge, A.mult, ["ft", "fc2", "fc3"], ["fu2"])
     ts(T.fv[:], T.ft[:], T.fe[:, 0:1], 1000.0, A.is_ge, A.mult, ["ft", "fe"], ["fv"])
+    tt(T.bdr[:, 18:27], T.ss[:], T.kb[:], A.add, ["ss", "kb"], ["bd2"])
+    store("Y", T.bd[:, :], T.bdr[0:1, 0:27], ["bd0", "bd1", "bd2"])
+    pick(2)
     tt(T.fw1[:], T.ft[:], T.fu1[:], A.add, ["ft", "fu1"], ["fw1"])
     tt(T.fw2[:], T.fu2[:], T.fv[:], A.add, ["fu2", "fv"], ["fw2"])
+    for b in range(4):
+        mm(b, "qw", 128 * b, "e2", 8, 2 * W, ["ec2", "es2"])
     tt(T.fw[:], T.fw1[:], T.fw2[:], A.add, ["fw1", "fw2"], ["fw"])
+    for b in range(4):
+        o, i = T.he2[:, b:8 * W:4], T["ps%d" % b][:, 0:2 * W]
+        if b % 2 == 0:
+            ts(o, i, 0.0, 0.0625, A.max, A.mult, [], ["ps%d" % b, "he2_%d" % b])
+        else:
+            op("S", lambda: g.scalar.activation(o, i, F.Relu, scale=0.0625), [], ["ps%d" % b, "he2_%d" % b])
     ts(T.off3[:, 0:25], T.fw[:], float(FZ), None, A.min, None, ["fw"], ["off3"])
+    quant("m2", FR, 2 * W + 2, T.he2[:, 0:8 * W + 8], ["he2_%d" % b for b in range(4)] + ["hez"], "me2")
+    mm(6, "qa", 0, "m2", FR, 2 * W + 2, ["qa", "me2"])
 
     reads = ["mi2", "me2", "off3"]
     off = T.off3[:, 0:25]
     op("V", lambda: V.tensor_copy(T.fin[:, 0:E].bitcast(dt.uint32), T.m2[:, 0:FZ + 2].bitcast(dt.uint32).indirect(off)),
        reads, ["fin"])
+    op("S", lambda: g.scalar.activation(T.ys[:, FR:FZ + 2], T.ps6[:, 0:2 * W + 2], F.Copy), [], ["ps6", "yse"])
     op("S", lambda: g.scalar.activation(T.yo[:, 0:E], T.ys[:, 0:FZ + 2].indirect(off), F.Copy), ["ysi", "yse", "off3"], ["yo"])
-    hs = 192
-    op("V", lambda: V.tensor_copy(T.fins[:, 0:hs], T.m2s[:, 0:FZ + 2].indirect(T.off3[:, 0:12])), reads, ["fina"])
-    op("S", lambda: g.scalar.activation(T.fins[:, hs:E], T.m2s[:, 0:FZ + 2].indirect(T.off3[:, 12:25]), F.Copy),
-       reads, ["finb"])
-    tt(T.ss[:], dm[:, 31:64:4], dm[:, 32:65:4], A.add, keys, ["ss"])
-    tt(T.bdr[:, 18:27], T.ss[:], T.kb[:], A.add, ["ss", "kb"], ["bd2"])
+    op("V", lambda: V.tensor_copy(T.fins[:, 0:E], T.m2s[:, 0:FZ + 2].indirect(off)), reads, ["fins"])
     store("Y", T.oc[:, :], T.fin[:, 0:E].bitcast(dt.uint8), ["fin"])
-    store("Y", T.y[:, :], T.yo[:, 0:E], ["yo"])
+    store("S", T.y[:, :], T.yo[:, 0:E], ["yo"])
     for k in range(4):
-        store("Y" if k < 2 else "S", T.osc[4 * k:4 * k + 4, :], T.fins[32 * k:32 * k + 4, 0:E], ["fina", "finb"])
-    store("S", T.bd[:, :], T.bdr[0:1, 0:27], ["bd0", "bd1", "bd2"])
+        store("Y" if k < 2 else "S", T.osc[4 * k:4 * k + 4, :], T.fins[32 * k:32 * k + 4, 0:E], ["fins"])
 
     for s in SEMAPHORES:
         if s != "out" and total.get(s, 0) > waited.get(s, 0):

@@ -7,6 +7,7 @@ W = 3 * S
 I0 = 80
 MR, ML, MA = I0 + P, I0 + P + W, I0 + P + 2 * W
 FR, FL, FZ = P, P + W, P + 2 * W
+W0 = 128 - W
 X4 = "float8_e4m3fn_x4"
 
 SCRATCH = {
@@ -35,7 +36,8 @@ for _n, _c in (("tiny", 1), ("cadd", 128), ("pref", 132), ("dm0", 96), ("dm1", 9
                ("th", 1), ("ind", 128), ("cnt", 1), ("cl", 32), ("wtm", 32), ("i1", 36), ("i2", 32), ("wa", 32), ("wb", 32),
                ("pcol", 1), ("p16", 1), ("j0", 25), ("jj", 25), ("b256", 9), ("base", 10), ("bu", 10), ("bv", 10),
                ("lt", 10), ("lu", 10), ("lw", 10), ("ss", 9), ("dd0", 9), ("dd1", 9), ("dev1", 9), ("kk", 9), ("kd", 9),
-               ("kb", 9), ("bdr", 27), ("dl", 2), ("fc", 8), ("jk", 25), ("ft", 25), ("fe", 1), ("fu1", 25), ("fu2", 25),
+               ("kb", 9), ("kx0", 9), ("kx3", 9), ("k2", 9), ("s2", 9),
+               ("bdr", 27), ("dl", 2), ("fc", 8), ("jk", 25), ("ft", 25), ("fe", 1), ("fu1", 25), ("fu2", 25),
                ("fv", 25), ("fw1", 25), ("fw2", 25), ("fw", 25)):
     SCRATCH[_n] = ("sbuf", [128, _c], "float32")
 for _b in range(8):
@@ -201,51 +203,44 @@ def rank_program(g, core, T, topo):
                                             bias=T.tiny[:, 0:1], accum_out=T["cg%d" % t][:, 4 * r + j:4 * r + j + 1]),
            ["tiny"], ["ps%d" % (4 + j), "junk%d" % j, "c%d_%d" % (t, j)])
 
-    def make(h, src, a, n, reads):
+    def products(src, a, n, reads):
         for b in range(4):
             mm(b, "qw", 128 * b, src, a, n, reads + ["qw%d" % (b // 2)])
+
+    def totile(h, n, on_vector):
         for b in range(4):
             o, i = T[h][:, b:4 * n:4], T["ps%d" % b][:, 0:n]
-            if b % 2 == 0:
+            if b in on_vector:
                 ts(o, i, 0.0, 0.0625, A.max, A.mult, [], ["ps%d" % b, h + "_%d" % b])
             else:
                 op("S", lambda: g.scalar.activation(o, i, F.Relu, scale=0.0625), [], ["ps%d" % b, h + "_%d" % b])
         return [h + "_%d" % b for b in range(4)]
 
-    def interior(t):
+    def bound(t, side):
+        h, n = "hi%d" % t, 4 * S * (t + 1)
+        v = T[h][:, 0:n] if side == "l" else T[h][:, 4 * P - n:4 * P]
+        ts(v, v, 2.0 ** 31, None, A.min, None, [h + "_%d" % b for b in range(4)], [h + side])
+
+    def interior_codes(t):
         h = "hi%d" % t
-        if t == 0:
-            keys = make(h, "e0", 128 + 2 * S, P, ["e0b"])
-        else:
-            keys = make(h, "m%d" % (t - 1), I0, P, ["mi%d" % (t - 1)])
-        if t < R - 1:
-            n = 4 * S * (t + 1)
-            ts(T[h][:, 0:n], T[h][:, 0:n], 2.0 ** 31, None, A.min, None, keys, [h + "l"])
-            ts(T[h][:, 4 * P - n:4 * P], T[h][:, 4 * P - n:4 * P], 2.0 ** 31, None, A.min, None, keys, [h + "r"])
-            keys = keys + [h + "l", h + "r"]
-        quant("m%d" % t, I0 if t < R - 1 else 0, P, T[h][:, 0:4 * P], keys, "mi%d" % t)
+        quant("m%d" % t, I0 if t < R - 1 else 0, P, T[h][:, 0:4 * P], [h + "_%d" % b for b in range(4)] + [h + "l", h + "r"],
+              "mi%d" % t)
         if t < R - 1:
             cost(t + 1, 1, "m%d" % t, I0, ["mi%d" % t])
             cost(t + 1, 2, "m%d" % t, I0 + 128, ["mi%d" % t])
 
-    def edge(t):
+    def edge_out(t):
         h = "he%d" % t
+        keys = totile(h, 2 * W, (0, 2))
+        quant("m%d" % t, MR, 2 * W, T[h][:, 0:8 * W], keys, "me%d" % t)
+        ends = {-1: (ML, MA), 1: (MR, 0)}
         if t == 0:
-            keys = make(h, "e0", 128 - 2 * S, 2 * W, ["e0a", "e0b", "arr0", "e0z", "e0zs"])
-        else:
-            keys = make(h, "e%d" % t, 8, 2 * W, ["ec%d" % t, "es%d" % t])
-        if t < R - 1:
-            quant("m%d" % t, MR, 2 * W, T[h][:, 0:8 * W], keys, "me%d" % t)
-            ends = {-1: (ML, MA), 1: (MR, 0)}
-            if t == 0:
-                halo(t + 1, "m%d" % t, "m%d" % t, W, ends, ["me%d" % t])
-            cost(t + 1, 0, "m%d" % t, MA - 128, ["me%d" % t])
-            cost(t + 1, 3, "m%d" % t, ML - 128, ["me%d" % t, "mi%d" % t])
-            share(t + 1)
-            if t > 0:
-                halo(t + 1, "m%d" % t, "m%d" % t, W, ends, ["me%d" % t])
-        else:
-            quant("m%d" % t, FR, 2 * W + 2, T[h][:, 0:8 * W + 8], keys + ["hez"], "me%d" % t)
+            halo(t + 1, "m%d" % t, "m%d" % t, W, ends, ["me%d" % t])
+        cost(t + 1, 0, "m%d" % t, MA - 128, ["me%d" % t])
+        cost(t + 1, 3, "m%d" % t, ML - 128, ["me%d" % t, "mi%d" % t])
+        share(t + 1)
+        if t > 0:
+            halo(t + 1, "m%d" % t, "m%d" % t, W, ends, ["me%d" % t])
 
     def pick(t):
         m, e, off = "m%d" % (t - 1), "e%d" % t, T["off%d" % t][:, 0:10]
@@ -254,75 +249,64 @@ def rank_program(g, core, T, topo):
            reads, ["ec%d" % t])
         op("S", lambda: g.scalar.activation(T[e + "s"][:, 0:160], T[m + "s"][:, 0:MA + W].indirect(off), F.Copy),
            reads, ["es%d" % t])
+        products(e, 8, 2 * W, ["ec%d" % t, "es%d" % t])
 
-    def borders(t):
+    def borders(t, between):
+        def gap(k):
+            for fn in between.get(k, ()):
+                fn()
         cg, dm = T["cg%d" % t], ("dm0" if t == 0 else "dm1")
         reads = ["ag%d" % t] + ["c%d_%d" % (t, j) for j in range(4)]
         if t > 0:
             tt(T.zz[:], cg[:], T.cap[:], A.min, reads + ["cap"], ["zz"])
             cg, reads = T.zz, ["zz"]
+        gap(0)
         for a in range(4):
             turn(T.yt[0:32, 32 * a:32 * a + 32], cg[32 * a:32 * a + 32, 0:32], reads, "yt%d" % a)
+        gap(1)
         op("V", lambda: V.tensor_tensor_scan(T.pref[0:32, 1:129], T.yt[0:32, 0:128], T.cadd[0:32, 0:128], 0.0, A.add, A.add),
            ["yt%d" % a for a in range(4)] + ["cadd"], ["pref"])
+        gap(2)
         ts(T.mx[0:32, :], T.wtm[0:32, :], T.pref[0:32, 128:129], None, A.mult, None, ["wtm", "pref"], ["mx"])
+        gap(3)
         turn(T.mt[0:32, :], T.mx[0:32, :], ["mx"], "mt")
+        gap(4)
         op("V", lambda: V.tensor_reduce(T.th[0:32, :], T.mt[0:32, :], AxisListType.X, A.add), ["mt"], ["th"])
-        w0 = 0 if t == 0 else 128 - W
+        gap(5)
+        w0 = 0 if t == 0 else W0
         ts(T.ind[0:32, w0:128], T.pref[0:32, w0:128], T.th[0:32, 0:1], None, A.is_lt, None, ["pref", "pref0", "th"], ["ind"])
+        gap(6)
         op("V", lambda: V.tensor_reduce(T.cnt[0:32, :], T.ind[0:32, w0:128], AxisListType.X, A.add), ["ind"], ["cnt"])
+        gap(7)
         ts(T.cl[0:32, :], T.amat[0:32, :], T.cnt[0:32, 0:1], T.bcol[0:32, 0:1], A.max, A.min, ["amat", "bcol", "cnt"], ["cl"])
+        gap(8)
         for a in range(4):
             turn(T[dm][32 * a:32 * a + 32, 32:64], T.cl[0:32, :], ["cl"], dm + "_%d" % a)
+        gap(9)
         return T[dm], [dm + "_%d" % a for a in range(4)] + [dm + "a", dm + "b"]
 
-    def bounds():
+    def clamp_lo():
         turn(T.amat[0:32, :], T.ar[0:32, :], ["ar0", "ar3", "ar"], "amat")
-        ts(T.bcol[0:32, :], T.amat[0:32, 0:1], float(S), None, A.add, None, ["amat"], ["bcol"])
 
-    def moves(t):
-        dm, keys = borders(t)
-        d, dk = T["dd%d" % t], "dd%d" % t
-        tt(T.ss[:], dm[:, 31:64:4], dm[:, 32:65:4], A.add, keys, ["ss"])
-        if t == 0:
-            ts(d[:], T.ss[:], -128.0, None, A.add, None, ["ss"], [dk])
-        else:
-            tt(d[:], T.ss[:], T.kk[:], A.subtract, ["ss", "kk"], [dk])
+    def clamp_hi():
+        ts(T.bcol[0:32, :], T.amat[0:32, 0:1], float(S), None, A.add, None, ["amat"], ["bcol"])
 
     def picklist(t):
         d, dk = T["dd%d" % t], "dd%d" % t
         dr, dlf = (-2.0 * S, float(I0 - S - ML)) if t == 0 else (T.dl[:, 0:1], T.dl[:, 1:2])
-        ts(T.lt[:, 0:5], T.base[:, 0:5], d[:, r + 1:r + 2], None, A.add, None, ["base", dk], ["ltr"])
-        ts(T.lt[:, 5:10], T.base[:, 5:10], d[:, r:r + 1], None, A.add, None, ["base", dk], ["ltl"])
-        ts(T.lu[:, 0:5], T.lt[:, 0:5], float(MR), dr, A.is_lt, A.mult, ["ltr", "dl0"], ["lur"])
-        ts(T.lu[:, 5:10], T.lt[:, 5:10], float(MA), dlf, A.is_ge, A.mult, ["ltl", "dl1"], ["lul"])
-        tt(T.lw[:], T.lt[:], T.lu[:], A.add, ["ltr", "ltl", "lur", "lul"], ["lw"])
-        op("V", lambda: V.tensor_copy(T["off%d" % (t + 1)][:], T.lw[:]), ["lw"], ["off%d" % (t + 1)])
+        return [
+            lambda: ts(T.lt[:, 0:5], T.base[:, 0:5], d[:, r + 1:r + 2], None, A.add, None, ["base", dk], ["ltr"]),
+            lambda: ts(T.lt[:, 5:10], T.base[:, 5:10], d[:, r:r + 1], None, A.add, None, ["base", dk], ["ltl"]),
+            lambda: ts(T.lu[:, 0:5], T.lt[:, 0:5], float(MR), dr, A.is_lt, A.mult, ["ltr", "dl0"], ["lur"]),
+            lambda: ts(T.lu[:, 5:10], T.lt[:, 5:10], float(MA), dlf, A.is_ge, A.mult, ["ltl", "dl1"], ["lul"]),
+            lambda: tt(T.lw[:], T.lt[:], T.lu[:], A.add, ["ltr", "ltl", "lur", "lul"], ["lw"]),
+            lambda: op("V", lambda: V.tensor_copy(T["off%d" % (t + 1)][:], T.lw[:]), ["lw"], ["off%d" % (t + 1)])]
 
-    def prepare(t):
-        d, dk = T["dd%d" % t], "dd%d" % t
-        w0 = 128 - W
-        lin(T.xl[:, 0:32:4], d[:, 0:8], 1, w0 + S, [dk], ["xl0"])
-        lin(T.xl[:, 3:32:4], d[:, 1:9], -1, 1 - w0 - 2 * S, [dk], ["xl3"])
-        lin(T.ar[0:32, 0:32:4], d[0:32, 0:8], 1, S, [dk], ["ar0"])
-        lin(T.ar[0:32, 3:32:4], d[0:32, 1:9], 1, S, [dk], ["ar3"])
-        lin(T.kk[:], d[:], 2, W, [dk], ["kk"])
-        if t == 0:
-            lin(T.dl[:, 0:1], d[:, r + 1:r + 2], 1, -2 * S, [dk], ["dl0"])
-            lin(T.dl[:, 1:2], d[:, r:r + 1], 1, I0 - S - ML, [dk], ["dl1"])
-
-    def prepare2(t):
-        d, dk = T["dd%d" % t], "dd%d" % t
+    def valid():
         tt(T.val[:], T.pp[:], T.xl[:], A.is_ge, ["pp", "ppa", "ppb", "xl0", "xl1", "xl2", "xl3"], ["val"])
-        if t == 0:
-            tt(T.bdr[:, 0:9], d[:], T.b256[:], A.add, [dk, "b256"], ["bd0"])
-        else:
-            tt(T.bdr[:, 9:18], T.dev1[:], T.b256[:], A.add, ["dev1", "b256"], ["bd1"])
+
+    def mask():
         ts(T.cap[:], T.val[:], 400.0, -130.0, A.mult, A.add, ["val"], ["cap"])
-        bounds()
-        if t == 0:
-            lin(T.xl[:, 1:32:4], T.dd0[:, 0:8], 1, 2 * S, ["dd0"], ["xl1"])
-            lin(T.xl[:, 2:32:4], T.dd0[:, 1:9], -1, 1 - 128 + 2 * S, ["dd0"], ["xl2"])
 
     load("Y", T.xe[:, 0:4 * S], T.x[:, 4 * (P - S):4 * P], "xer")
     load("S", T.xe[:, 4 * S:8 * S], T.x[:, 0:4 * S], "xel")
@@ -374,84 +358,119 @@ def rank_program(g, core, T, topo):
     cost(0, 3, "e0", 256 + 2 * S, ["e0b"])
     share(0)
     quant("e0", 0, 128, T.xt[:, 512:1024], ["xt"], "e0a")
-    op("V", lambda: V.memset(T.pp[0:32, 3:32:4], -1000.0), ["pp"], ["ppa"])
-    op("V", lambda: V.memset(T.pp[32:128 - W, 3:32:4], -1000.0), ["pp"], ["ppb"])
-    tt(T.wtm[0:32, :], T.wb[0:32, :], T.wa[0:32, :], A.subtract, ["wa", "wb"], ["wtm"])
     ts(T.jj[:], T.j0[:], T.p16[:, 0:1], None, A.add, None, ["j0", "p16"], ["jj"])
-    bounds()
-    quant("qw", 0, 256, T.wt[:, 0:1024], ["wt0"], "qw0")
-    quant("qw", 256, 256, T.wt[:, 1024:2048], ["wt1"], "qw1")
-    interior(0)
-    edge(0)
+    op("V", lambda: V.memset(T.pp[0:32, 3:32:4], -1000.0), ["pp"], ["ppa"])
+    op("V", lambda: V.memset(T.pp[32:W0, 3:32:4], -1000.0), ["pp"], ["ppb"])
+    tt(T.wtm[0:32, :], T.wb[0:32, :], T.wa[0:32, :], A.subtract, ["wa", "wb"], ["wtm"])
+    clamp_lo()
     ts(T.bu[:, 0:5], T.jj[:, 0:5], 8.0 + 2 * S, 0.0 if r == N - 1 else float(MA - S - MR), A.is_ge, A.mult, ["jj"], ["bur"])
     ts(T.bu[:, 5:10], T.jj[:, 0:5], float(S), 0.0 if r == 0 else float(S - ML), A.is_lt, A.mult, ["jj"], ["bul"])
-    ts(T.bv[:, 0:5], T.jj[:, 0:5], float(MR - 8), None, A.add, None, ["jj"], ["bvr"])
-    ts(T.bv[:, 5:10], T.jj[:, 0:5], float(ML), None, A.add, None, ["jj"], ["bvl"])
+    lin(T.bv[:, 0:5], T.jj[:, 0:5], 1, MR - 8, ["jj"], ["bvr"])
+    lin(T.bv[:, 5:10], T.jj[:, 0:5], 1, ML, ["jj"], ["bvl"])
+    clamp_hi()
+    quant("qw", 0, 256, T.wt[:, 0:1024], ["wt0"], "qw0")
+    quant("qw", 256, 256, T.wt[:, 1024:2048], ["wt1"], "qw1")
+    products("e0", 128 + 2 * S, P, ["e0b"])
     tt(T.base[:], T.bu[:], T.bv[:], A.add, ["bur", "bul", "bvr", "bvl"], ["base"])
-    interior(1)
-    moves(0)
-    prepare(0)
-    picklist(0)
-    prepare2(0)
+    totile("hi0", P, (0, 2))
+    bound(0, "l")
+    bound(0, "r")
+    interior_codes(0)
+    products("e0", 128 - 2 * S, 2 * W, ["e0a", "e0b", "arr0", "e0z", "e0zs"])
+    edge_out(0)
+    products("m0", I0, P, ["mi0"])
+    totile("hi1", P, ())
+    dm, keys = borders(0, {})
+    tt(T.ss[:], dm[:, 31:64:4], dm[:, 32:65:4], A.add, keys, ["ss"])
+    bound(1, "l")
+    ts(T.dd0[:], T.ss[:], -128.0, None, A.add, None, ["ss"], ["dd0"])
+    bound(1, "r")
+    pl = picklist(0)
+    pl[0](), pl[1](), pl[2](), pl[3]()
+    interior_codes(1)
+    pl[4](), pl[5]()
+    d = T.dd0
+    lin(T.xl[:, 0:32:4], d[:, 0:8], 1, W0 + S, ["dd0"], ["xl0"])
+    lin(T.xl[:, 3:32:4], d[:, 1:9], -1, 1 - W0 - 2 * S, ["dd0"], ["xl3"])
+    lin(T.ar[0:32, 0:32:4], d[0:32, 0:8], 1, S, ["dd0"], ["ar0"])
+    lin(T.ar[0:32, 3:32:4], d[0:32, 1:9], 1, S, ["dd0"], ["ar3"])
     pick(1)
-    edge(1)
-    moves(1)
-    prepare(1)
+    valid()
+    clamp_lo()
+    edge_out(1)
+    mask()
+    clamp_hi()
+    lin(T.kk[:], d[:], 2, W, ["dd0"], ["kk"])
+    lin(T.kx0[:], d[:], -2, W0 + S - W, ["dd0"], ["kx0"])
+    lin(T.kx3[:], d[:], 2, W + 1 - W0 - 2 * S, ["dd0"], ["kx3"])
+    lin(T.xl[:, 1:32:4], d[:, 0:8], 1, 2 * S, ["dd0"], ["xl1"])
+    lin(T.xl[:, 2:32:4], d[:, 1:9], -1, 1 - 128 + 2 * S, ["dd0"], ["xl2"])
+    lin(T.dl[:, 0:1], d[:, r + 1:r + 2], 1, -2 * S, ["dd0"], ["dl0"])
+    lin(T.dl[:, 1:2], d[:, r:r + 1], 1, I0 - S - ML, ["dd0"], ["dl1"])
+    products("m1", I0, P, ["mi1"])
+    totile("hi2", P, ())
+    dm, keys = borders(1, {2: [lambda: tt(T.bdr[:, 0:9], T.dd0[:], T.b256[:], A.add, ["dd0", "b256"], ["bd0"])]})
+    tt(T.ss[:], dm[:, 31:64:4], dm[:, 32:65:4], A.add, keys, ["ss"])
+    interior_codes(2)
+    mm(5, "qa", 0, "m2", 0, P, ["qa", "mi2"])
+    tt(T.xl[:, 0:32:4], T.ss[:, 0:8], T.kx0[:, 0:8], A.add, ["ss", "kx0"], ["xl0"])
+    tt(T.xl[:, 3:32:4], T.kx3[:, 1:9], T.ss[:, 1:9], A.subtract, ["ss", "kx3"], ["xl3"])
+    tt(T.dd1[:], T.ss[:], T.kk[:], A.subtract, ["ss", "kk"], ["dd1"])
+    valid()
     tt(T.dev1[:], T.dd1[:], T.dd0[:], A.add, ["dd1", "dd0"], ["dev1"])
-    picklist(1)
-    prepare2(1)
-    tt(T.kd[:], T.dev1[:], T.kk[:], A.subtract, ["dev1", "kk"], ["kd"])
+    mask()
+    d = T.dd1
+    lin(T.ar[0:32, 0:32:4], d[0:32, 0:8], 1, S, ["dd1"], ["ar0"])
+    lin(T.ar[0:32, 3:32:4], d[0:32, 1:9], 1, S, ["dd1"], ["ar3"])
+    lin(T.k2[:], d[:], 2, W, ["dd1"], ["k2"])
     lin(T.fc[:, 0:1], T.dev1[:, r:r + 1], 1, 2 * S, ["dev1"], ["fc0"])
     lin(T.fc[:, 1:2], T.dev1[:, r:r + 1], -1, FL + S, ["dev1"], ["fc1"])
     lin(T.fc[:, 2:3], T.dev1[:, r + 1:r + 2], 1, P - 2 * S, ["dev1"], ["fc2"])
     lin(T.fc[:, 3:4], T.dev1[:, r + 1:r + 2], -1, FR - P + 2 * S, ["dev1"], ["fc3"])
-    lin(T.fc[:, 4:5], T.kd[:, r + 1:r + 2], 1, P, ["kd"], ["fc4"])
-    op("S", lambda: g.scalar.activation(T.jk[:], T.jj[:], F.Identity, bias=T.kd[:, r:r + 1]), ["jj", "kd"], ["jk"])
-    for b in range(4):
-        mm(b, "qw", 128 * b, "m1", I0, P, ["mi1"])
-        op("S", lambda: g.scalar.activation(T.hi2[:, b:4 * P:4], T["ps%d" % b][:, 0:P], F.Relu, scale=0.0625),
-           [], ["ps%d" % b, "hi2_%d" % b])
-    dm, keys = borders(2)
-    quant("m2", 0, P, T.hi2[:, 0:4 * P], ["hi2_%d" % b for b in range(4)], "mi2")
-    mm(5, "qa", 0, "m2", 0, P, ["qa", "mi2"])
     op("S", lambda: g.scalar.activation(T.ys[:, 0:P], T.ps5[:, 0:P], F.Copy), [], ["ps5", "ysi"])
+
+    def consts():
+        tt(T.kd[:], T.dev1[:], T.k2[:], A.subtract, ["dev1", "k2"], ["kd"])
+        lin(T.fc[:, 4:5], T.kd[:, r + 1:r + 2], 1, P, ["kd"], ["fc4"])
+        op("S", lambda: g.scalar.activation(T.jk[:], T.jj[:], F.Identity, bias=T.kd[:, r:r + 1]), ["jj", "kd"], ["jk"])
+
+    pl = picklist(1)
+    pl[0](), pl[1]()
+    dm, keys = borders(2, {
+        0: [pl[2]], 1: [pl[3]], 2: [clamp_lo], 3: [pl[4]], 4: [clamp_hi], 5: [consts], 6: [pl[5]],
+        7: [lambda: tt(T.bdr[:, 9:18], T.dev1[:], T.b256[:], A.add, ["dev1", "b256"], ["bd1"])],
+        8: [lambda: tt(T.kb[:], T.kd[:], T.b256[:], A.add, ["kd", "b256"], ["kb"])]})
     ca, cb = 31 + 4 * r, 32 + 4 * r
     ts(T.ft[:], T.jk[:], dm[:, ca:ca + 1], dm[:, cb:cb + 1], A.add, A.add, keys + ["jk"], ["ft"])
     ts(T.fe[:], T.fc[:, 4:5], dm[:, ca + 4:ca + 5], dm[:, cb + 4:cb + 5], A.add, A.add, keys + ["fc4"], ["fe"])
-    tt(T.ss[:], dm[:, 31:64:4], dm[:, 32:65:4], A.add, keys, ["ss"])
-    tt(T.kb[:], T.bdr[:, 9:18], T.kk[:], A.subtract, ["bd1", "kk"], ["kb"])
+    pick(2)
     ts(T.fu1[:], T.ft[:], T.fc[:, 0:1], T.fc[:, 1:2], A.is_lt, A.mult, ["ft", "fc0", "fc1"], ["fu1"])
     ts(T.fu2[:], T.ft[:], T.fc[:, 2:3], T.fc[:, 3:4], A.is_ge, A.mult, ["ft", "fc2", "fc3"], ["fu2"])
     ts(T.fv[:], T.ft[:], T.fe[:, 0:1], 1000.0, A.is_ge, A.mult, ["ft", "fe"], ["fv"])
-    tt(T.bdr[:, 18:27], T.ss[:], T.kb[:], A.add, ["ss", "kb"], ["bd2"])
-    store("Y", T.bd[:, :], T.bdr[0:1, 0:27], ["bd0", "bd1", "bd2"])
-    pick(2)
     tt(T.fw1[:], T.ft[:], T.fu1[:], A.add, ["ft", "fu1"], ["fw1"])
     tt(T.fw2[:], T.fu2[:], T.fv[:], A.add, ["fu2", "fv"], ["fw2"])
-    for b in range(4):
-        mm(b, "qw", 128 * b, "e2", 8, 2 * W, ["ec2", "es2"])
+    keys2 = totile("he2", 2 * W, (0, 2))
     tt(T.fw[:], T.fw1[:], T.fw2[:], A.add, ["fw1", "fw2"], ["fw"])
-    for b in range(4):
-        o, i = T.he2[:, b:8 * W:4], T["ps%d" % b][:, 0:2 * W]
-        if b % 2 == 0:
-            ts(o, i, 0.0, 0.0625, A.max, A.mult, [], ["ps%d" % b, "he2_%d" % b])
-        else:
-            op("S", lambda: g.scalar.activation(o, i, F.Relu, scale=0.0625), [], ["ps%d" % b, "he2_%d" % b])
-    ts(T.off3[:, 0:25], T.fw[:], float(FZ), None, A.min, None, ["fw"], ["off3"])
-    quant("m2", FR, 2 * W + 2, T.he2[:, 0:8 * W + 8], ["he2_%d" % b for b in range(4)] + ["hez"], "me2")
+    quant("m2", FR, 2 * W + 2, T.he2[:, 0:8 * W + 8], keys2 + ["hez"], "me2")
     mm(6, "qa", 0, "m2", FR, 2 * W + 2, ["qa", "me2"])
+    ts(T.off3[:, 0:25], T.fw[:], float(FZ), None, A.min, None, ["fw"], ["off3"])
+    tt(T.s2[:], dm[:, 31:64:4], dm[:, 32:65:4], A.add, keys, ["s2"])
 
     reads = ["mi2", "me2", "off3"]
-    off = T.off3[:, 0:25]
-    op("V", lambda: V.tensor_copy(T.fin[:, 0:E].bitcast(dt.uint32), T.m2[:, 0:FZ + 2].bitcast(dt.uint32).indirect(off)),
-       reads, ["fin"])
+    lo, hi, hs = T.off3[:, 0:12], T.off3[:, 12:25], 192
+    op("V", lambda: V.tensor_copy(T.fin[:, 0:E].bitcast(dt.uint32),
+                                  T.m2[:, 0:FZ + 2].bitcast(dt.uint32).indirect(T.off3[:, 0:25])), reads, ["fin"])
     op("S", lambda: g.scalar.activation(T.ys[:, FR:FZ + 2], T.ps6[:, 0:2 * W + 2], F.Copy), [], ["ps6", "yse"])
-    op("S", lambda: g.scalar.activation(T.yo[:, 0:E], T.ys[:, 0:FZ + 2].indirect(off), F.Copy), ["ysi", "yse", "off3"], ["yo"])
-    op("V", lambda: V.tensor_copy(T.fins[:, 0:E], T.m2s[:, 0:FZ + 2].indirect(off)), reads, ["fins"])
+    op("S", lambda: g.scalar.activation(T.yo[:, hs:E], T.ys[:, 0:FZ + 2].indirect(hi), F.Copy), ["ysi", "yse", "off3"], ["yob"])
+    op("V", lambda: V.tensor_copy(T.yo[:, 0:hs], T.ys[:, 0:FZ + 2].indirect(lo)), ["ysi", "yse", "off3"], ["yoa"])
+    op("S", lambda: g.scalar.activation(T.fins[:, hs:E], T.m2s[:, 0:FZ + 2].indirect(hi), F.Copy), reads, ["finb"])
+    op("V", lambda: V.tensor_copy(T.fins[:, 0:hs], T.m2s[:, 0:FZ + 2].indirect(lo)), reads, ["fina"])
+    tt(T.bdr[:, 18:27], T.s2[:], T.kb[:], A.add, ["s2", "kb"], ["bd2"])
     store("Y", T.oc[:, :], T.fin[:, 0:E].bitcast(dt.uint8), ["fin"])
-    store("S", T.y[:, :], T.yo[:, 0:E], ["yo"])
+    store("Y", T.y[:, :], T.yo[:, 0:E], ["yoa", "yob"])
     for k in range(4):
-        store("Y" if k < 2 else "S", T.osc[4 * k:4 * k + 4, :], T.fins[32 * k:32 * k + 4, 0:E], ["fins"])
+        store("Y" if k < 2 else "S", T.osc[4 * k:4 * k + 4, :], T.fins[32 * k:32 * k + 4, 0:E], ["fina", "finb"])
+    store("S", T.bd[:, :], T.bdr[0:1, 0:27], ["bd0", "bd1", "bd2"])
 
     for s in SEMAPHORES:
         if s != "out" and total.get(s, 0) > waited.get(s, 0):

@@ -169,9 +169,9 @@ def rank_program(g, core, T, topo):
 
     sides = [s for s in (-1, 1) if 0 <= r + s < N]
 
-    def halo(t, src, dname, n, from_to, reads):
+    def halo(t, src, dname, n, from_to, reads, calls=(True, False)):
         need("G", reads, [])
-        for codes in (True, False):
+        for codes in calls:
             trs = []
             for s in sides:
                 a, b = from_to[s]
@@ -207,8 +207,8 @@ def rank_program(g, core, T, topo):
         for b in range(4):
             mm(b, "qw", 128 * b, src, a, n, reads + ["qw%d" % (b // 2)])
 
-    def totile(h, n, on_vector):
-        for b in range(4):
+    def totile(h, n, on_vector, banks=(0, 1, 2, 3)):
+        for b in banks:
             o, i = T[h][:, b:4 * n:4], T["ps%d" % b][:, 0:n]
             if b in on_vector:
                 ts(o, i, 0.0, 0.0625, A.max, A.mult, [], ["ps%d" % b, h + "_%d" % b])
@@ -234,13 +234,12 @@ def rank_program(g, core, T, topo):
         keys = totile(h, 2 * W, (0, 2))
         quant("m%d" % t, MR, 2 * W, T[h][:, 0:8 * W], keys, "me%d" % t)
         ends = {-1: (ML, MA), 1: (MR, 0)}
-        if t == 0:
-            halo(t + 1, "m%d" % t, "m%d" % t, W, ends, ["me%d" % t])
+        halo(t + 1, "m%d" % t, "m%d" % t, W, ends, ["me%d" % t], (True, False) if t == 0 else (False,))
         cost(t + 1, 0, "m%d" % t, MA - 128, ["me%d" % t])
         cost(t + 1, 3, "m%d" % t, ML - 128, ["me%d" % t, "mi%d" % t])
         share(t + 1)
         if t > 0:
-            halo(t + 1, "m%d" % t, "m%d" % t, W, ends, ["me%d" % t])
+            halo(t + 1, "m%d" % t, "m%d" % t, W, ends, ["me%d" % t], (True,))
 
     def pick(t):
         m, e, off = "m%d" % (t - 1), "e%d" % t, T["off%d" % t][:, 0:10]
@@ -359,36 +358,34 @@ def rank_program(g, core, T, topo):
     share(0)
     quant("e0", 0, 128, T.xt[:, 512:1024], ["xt"], "e0a")
     ts(T.jj[:], T.j0[:], T.p16[:, 0:1], None, A.add, None, ["j0", "p16"], ["jj"])
-    op("V", lambda: V.memset(T.pp[0:32, 3:32:4], -1000.0), ["pp"], ["ppa"])
-    op("V", lambda: V.memset(T.pp[32:W0, 3:32:4], -1000.0), ["pp"], ["ppb"])
     tt(T.wtm[0:32, :], T.wb[0:32, :], T.wa[0:32, :], A.subtract, ["wa", "wb"], ["wtm"])
-    clamp_lo()
-    ts(T.bu[:, 0:5], T.jj[:, 0:5], 8.0 + 2 * S, 0.0 if r == N - 1 else float(MA - S - MR), A.is_ge, A.mult, ["jj"], ["bur"])
-    ts(T.bu[:, 5:10], T.jj[:, 0:5], float(S), 0.0 if r == 0 else float(S - ML), A.is_lt, A.mult, ["jj"], ["bul"])
-    lin(T.bv[:, 0:5], T.jj[:, 0:5], 1, MR - 8, ["jj"], ["bvr"])
-    lin(T.bv[:, 5:10], T.jj[:, 0:5], 1, ML, ["jj"], ["bvl"])
-    clamp_hi()
     quant("qw", 0, 256, T.wt[:, 0:1024], ["wt0"], "qw0")
     quant("qw", 256, 256, T.wt[:, 1024:2048], ["wt1"], "qw1")
     products("e0", 128 + 2 * S, P, ["e0b"])
-    tt(T.base[:], T.bu[:], T.bv[:], A.add, ["bur", "bul", "bvr", "bvl"], ["base"])
+    clamp_lo()
     totile("hi0", P, (0, 2))
-    bound(0, "l")
-    bound(0, "r")
+    clamp_hi()
     interior_codes(0)
+    lin(T.bv[:, 0:5], T.jj[:, 0:5], 1, MR - 8, ["jj"], ["bvr"])
+    lin(T.bv[:, 5:10], T.jj[:, 0:5], 1, ML, ["jj"], ["bvl"])
     products("e0", 128 - 2 * S, 2 * W, ["e0a", "e0b", "arr0", "e0z", "e0zs"])
     edge_out(0)
     products("m0", I0, P, ["mi0"])
     totile("hi1", P, ())
-    dm, keys = borders(0, {})
+    dm, keys = borders(0, {
+        2: [lambda: op("V", lambda: V.memset(T.pp[0:32, 3:32:4], -1000.0), ["pp"], ["ppa"])],
+        3: [lambda: op("V", lambda: V.memset(T.pp[32:W0, 3:32:4], -1000.0), ["pp"], ["ppb"])],
+        4: [lambda: ts(T.bu[:, 0:5], T.jj[:, 0:5], 8.0 + 2 * S, 0.0 if r == N - 1 else float(MA - S - MR),
+                       A.is_ge, A.mult, ["jj"], ["bur"])],
+        5: [lambda: ts(T.bu[:, 5:10], T.jj[:, 0:5], float(S), 0.0 if r == 0 else float(S - ML),
+                       A.is_lt, A.mult, ["jj"], ["bul"])],
+        6: [lambda: tt(T.base[:], T.bu[:], T.bv[:], A.add, ["bur", "bul", "bvr", "bvl"], ["base"])],
+        7: [lambda: bound(1, "l")], 8: [lambda: bound(1, "r")]})
     tt(T.ss[:], dm[:, 31:64:4], dm[:, 32:65:4], A.add, keys, ["ss"])
-    bound(1, "l")
-    ts(T.dd0[:], T.ss[:], -128.0, None, A.add, None, ["ss"], ["dd0"])
-    bound(1, "r")
-    pl = picklist(0)
-    pl[0](), pl[1](), pl[2](), pl[3]()
     interior_codes(1)
-    pl[4](), pl[5]()
+    ts(T.dd0[:], T.ss[:], -128.0, None, A.add, None, ["ss"], ["dd0"])
+    for fn in picklist(0):
+        fn()
     d = T.dd0
     lin(T.xl[:, 0:32:4], d[:, 0:8], 1, W0 + S, ["dd0"], ["xl0"])
     lin(T.xl[:, 3:32:4], d[:, 1:9], -1, 1 - W0 - 2 * S, ["dd0"], ["xl3"])
@@ -437,40 +434,40 @@ def rank_program(g, core, T, topo):
     pl = picklist(1)
     pl[0](), pl[1]()
     dm, keys = borders(2, {
-        0: [pl[2]], 1: [pl[3]], 2: [clamp_lo], 3: [pl[4]], 4: [clamp_hi], 5: [consts], 6: [pl[5]],
-        7: [lambda: tt(T.bdr[:, 9:18], T.dev1[:], T.b256[:], A.add, ["dev1", "b256"], ["bd1"])],
-        8: [lambda: tt(T.kb[:], T.kd[:], T.b256[:], A.add, ["kd", "b256"], ["kb"])]})
+        0: [pl[2], pl[3]], 1: [pl[4]], 2: [clamp_lo], 3: [pl[5]], 4: [clamp_hi, consts],
+        5: [lambda: tt(T.bdr[:, 9:18], T.dev1[:], T.b256[:], A.add, ["dev1", "b256"], ["bd1"])],
+        6: [lambda: pick(2)],
+        7: [lambda: tt(T.kb[:], T.kd[:], T.b256[:], A.add, ["kd", "b256"], ["kb"])],
+        8: [lambda: totile("he2", 2 * W, (0,), (0, 1, 3))],
+        9: [lambda: totile("he2", 2 * W, (2,), (2,))]})
     ca, cb = 31 + 4 * r, 32 + 4 * r
     ts(T.ft[:], T.jk[:], dm[:, ca:ca + 1], dm[:, cb:cb + 1], A.add, A.add, keys + ["jk"], ["ft"])
     ts(T.fe[:], T.fc[:, 4:5], dm[:, ca + 4:ca + 5], dm[:, cb + 4:cb + 5], A.add, A.add, keys + ["fc4"], ["fe"])
-    pick(2)
+    quant("m2", FR, 2 * W + 2, T.he2[:, 0:8 * W + 8], ["he2_%d" % b for b in range(4)] + ["hez"], "me2")
+    mm(6, "qa", 0, "m2", FR, 2 * W + 2, ["qa", "me2"])
+    op("S", lambda: g.scalar.activation(T.ys[:, FR:FZ + 2], T.ps6[:, 0:2 * W + 2], F.Copy), [], ["ps6", "yse"])
     ts(T.fu1[:], T.ft[:], T.fc[:, 0:1], T.fc[:, 1:2], A.is_lt, A.mult, ["ft", "fc0", "fc1"], ["fu1"])
     ts(T.fu2[:], T.ft[:], T.fc[:, 2:3], T.fc[:, 3:4], A.is_ge, A.mult, ["ft", "fc2", "fc3"], ["fu2"])
     ts(T.fv[:], T.ft[:], T.fe[:, 0:1], 1000.0, A.is_ge, A.mult, ["ft", "fe"], ["fv"])
     tt(T.fw1[:], T.ft[:], T.fu1[:], A.add, ["ft", "fu1"], ["fw1"])
     tt(T.fw2[:], T.fu2[:], T.fv[:], A.add, ["fu2", "fv"], ["fw2"])
-    keys2 = totile("he2", 2 * W, (0, 2))
-    tt(T.fw[:], T.fw1[:], T.fw2[:], A.add, ["fw1", "fw2"], ["fw"])
-    quant("m2", FR, 2 * W + 2, T.he2[:, 0:8 * W + 8], keys2 + ["hez"], "me2")
-    mm(6, "qa", 0, "m2", FR, 2 * W + 2, ["qa", "me2"])
-    ts(T.off3[:, 0:25], T.fw[:], float(FZ), None, A.min, None, ["fw"], ["off3"])
     tt(T.s2[:], dm[:, 31:64:4], dm[:, 32:65:4], A.add, keys, ["s2"])
+    tt(T.fw[:], T.fw1[:], T.fw2[:], A.add, ["fw1", "fw2"], ["fw"])
+    tt(T.bdr[:, 18:27], T.s2[:], T.kb[:], A.add, ["s2", "kb"], ["bd2"])
+    store("Y", T.bd[:, :], T.bdr[0:1, 0:27], ["bd0", "bd1", "bd2"])
+    ts(T.off3[:, 0:25], T.fw[:], float(FZ), None, A.min, None, ["fw"], ["off3"])
 
     reads = ["mi2", "me2", "off3"]
-    lo, hi, hs = T.off3[:, 0:12], T.off3[:, 12:25], 192
-    op("V", lambda: V.tensor_copy(T.fin[:, 0:E].bitcast(dt.uint32),
-                                  T.m2[:, 0:FZ + 2].bitcast(dt.uint32).indirect(T.off3[:, 0:25])), reads, ["fin"])
-    op("S", lambda: g.scalar.activation(T.ys[:, FR:FZ + 2], T.ps6[:, 0:2 * W + 2], F.Copy), [], ["ps6", "yse"])
-    op("S", lambda: g.scalar.activation(T.yo[:, hs:E], T.ys[:, 0:FZ + 2].indirect(hi), F.Copy), ["ysi", "yse", "off3"], ["yob"])
-    op("V", lambda: V.tensor_copy(T.yo[:, 0:hs], T.ys[:, 0:FZ + 2].indirect(lo)), ["ysi", "yse", "off3"], ["yoa"])
-    op("S", lambda: g.scalar.activation(T.fins[:, hs:E], T.m2s[:, 0:FZ + 2].indirect(hi), F.Copy), reads, ["finb"])
-    op("V", lambda: V.tensor_copy(T.fins[:, 0:hs], T.m2s[:, 0:FZ + 2].indirect(lo)), reads, ["fina"])
-    tt(T.bdr[:, 18:27], T.s2[:], T.kb[:], A.add, ["s2", "kb"], ["bd2"])
+    off, lo, hi, hs = T.off3[:, 0:25], T.off3[:, 0:12], T.off3[:, 12:25], 192
+    op("V", lambda: V.tensor_copy(T.fin[:, 0:E].bitcast(dt.uint32), T.m2[:, 0:FZ + 2].bitcast(dt.uint32).indirect(off)),
+       reads, ["fin"])
+    op("S", lambda: g.scalar.activation(T.yo[:, 0:E], T.ys[:, 0:FZ + 2].indirect(off), F.Copy), ["ysi", "yse", "off3"], ["yo"])
+    op("V", lambda: V.tensor_copy(T.fins[:, hs:E], T.m2s[:, 0:FZ + 2].indirect(hi)), reads, ["finb"])
+    op("S", lambda: g.scalar.activation(T.fins[:, 0:hs], T.m2s[:, 0:FZ + 2].indirect(lo), F.Copy), reads, ["fina"])
     store("Y", T.oc[:, :], T.fin[:, 0:E].bitcast(dt.uint8), ["fin"])
-    store("Y", T.y[:, :], T.yo[:, 0:E], ["yoa", "yob"])
+    store("Y", T.y[:, :], T.yo[:, 0:E], ["yo"])
     for k in range(4):
         store("Y" if k < 2 else "S", T.osc[4 * k:4 * k + 4, :], T.fins[32 * k:32 * k + 4, 0:E], ["fina", "finb"])
-    store("S", T.bd[:, :], T.bdr[0:1, 0:27], ["bd0", "bd1", "bd2"])
 
     for s in SEMAPHORES:
         if s != "out" and total.get(s, 0) > waited.get(s, 0):

@@ -6,54 +6,38 @@ E = P + 2 * S * R
 W = 3 * S
 I0 = 80
 MR, ML, MA = I0 + P, I0 + P + W, I0 + P + 2 * W
-FR, FL, FZ = P, P + W, P + 2 * W
+L0 = MR + 4 * S
+A0 = L0 + 4 * S + 16
+FI = 2
+FR, FL, AL, AR, FE = FI + P, FI + P + W, FI + P + 2 * W, FI + P + 3 * W, FI + P + 4 * W
 W0 = 128 - W
-X4 = "float8_e4m3fn_x4"
+JL = 6
 
-SCRATCH = {
-    "xe": ("sbuf", [128, 512], "bfloat16"),
-    "xt": ("sbuf", [128, 4 * P], "bfloat16"),
-    "at": ("sbuf", [128, 512], "bfloat16"),
-    "wt": ("sbuf", [128, 2048], "bfloat16"),
-    "junk": ("sbuf", [128, 512], "bfloat16"),
-    "ys": ("sbuf", [128, FZ + 2], "float32"),
-    "yo": ("sbuf", [128, E], "float32"),
-    "pint": ("sbuf", [128, 2], "int32"),
-    "off1": ("sbuf", [128, 10], "uint16"),
-    "off2": ("sbuf", [128, 10], "uint16"),
-    "off3": ("sbuf", [128, 26], "uint16"),
-}
-for _n, _c in (("qxe", 128), ("qa", 128), ("qw", 512), ("e0", 128 + 2 * S + P), ("e1", 160), ("e2", 160),
-               ("m0", MA + W), ("m1", MA + W), ("m2", FZ + 2), ("fin", E)):
-    SCRATCH[_n] = ("sbuf", [128, _c], X4)
+SCRATCH = {"pint": ("sbuf", [128, 4], "int32"), "off1": ("sbuf", [128, 10], "uint16"), "off3": ("sbuf", [128, 26], "uint16")}
+for _n, _c in (("xe", 512), ("xt", 4 * P), ("at", 512), ("wt", 2048), ("junk", 512), ("hi0", 4 * (P + 2 * S)), ("hi1", 4 * P),
+               ("hi2", 4 * AL), ("he1", 8 * W), ("he2", 8 * W)):
+    SCRATCH[_n] = ("sbuf", [128, _c], "bfloat16")
+for _n, _c in (("qxe", 128), ("qa", 128), ("qw", 512), ("e0", 2 * S + P), ("e1", 160), ("e2", 2 * W),
+               ("m0", A0 + W), ("m1", MA), ("m2", FE), ("fin", E)):
+    SCRATCH[_n] = ("sbuf", [128, _c], "float8_e4m3fn_x4")
     SCRATCH[_n + "s"] = ("sbuf", [128, _c], "uint8")
-for _t in range(R):
-    SCRATCH["hi%d" % _t] = ("sbuf", [128, 4 * P], "bfloat16")
-    SCRATCH["he%d" % _t] = ("sbuf", [128, 4 * (2 * W + 2)], "bfloat16")
-    SCRATCH["cg%d" % _t] = ("sbuf", [128, 32], "float32")
-for _n, _c in (("tiny", 1), ("cadd", 128), ("pref", 132), ("dm0", 96), ("dm1", 96), ("ar", 32), ("amat", 32), ("bcol", 1),
-               ("xl", 32), ("sg", 32), ("pp", 32), ("val", 32), ("cap", 32), ("zz", 32), ("yt", 128), ("mx", 32), ("mt", 32),
-               ("th", 1), ("ind", 128), ("cnt", 1), ("cl", 32), ("wtm", 32), ("i1", 36), ("i2", 32), ("wa", 32), ("wb", 32),
-               ("pcol", 1), ("p16", 1), ("j0", 25), ("jj", 25), ("b256", 9), ("base", 10), ("bu", 10), ("bv", 10),
-               ("lt", 10), ("lu", 10), ("lw", 10), ("ss", 9), ("dd0", 9), ("dd1", 9), ("dev1", 9), ("kk", 9), ("kd", 9),
-               ("kb", 9), ("kx0", 9), ("kx3", 9), ("k2", 9), ("s2", 9),
-               ("bdr", 27), ("dl", 2), ("fc", 8), ("jk", 25), ("ft", 25), ("fe", 1), ("fu1", 25), ("fu2", 25),
-               ("fv", 25), ("fw1", 25), ("fw2", 25), ("fw", 25)):
+for _n, _c in (("tiny", 1), ("cadd", 192), ("pref", 196), ("dm", 96), ("nar", 32), ("val", 32), ("cap", 32), ("zz", 32),
+               ("yt", 192), ("tt", 68), ("hm", 68), ("th", 68), ("ind", 160), ("cnt", 1), ("cl", 32), ("rc", 1), ("pc", 4),
+               ("cg0", 32), ("cg1", 32), ("cg2", 32), ("yo", E), ("p16", 1), ("j0", 25), ("jj", 25), ("base", 10), ("bu", 10),
+               ("bv", 10), ("s0", 9), ("s1", 9), ("s2", 9), ("bk", 27), ("bdr", 27), ("jm", 25), ("ptb", 25), ("jfb", 25),
+               ("jv", 25), ("jf", 25), ("pt", 50), ("cst", 25), ("fm", 100), ("fu", 100), ("fs", 100)):
     SCRATCH[_n] = ("sbuf", [128, _c], "float32")
 for _b in range(8):
     SCRATCH["ps%d" % _b] = ("psum", [128, 512], "float32")
 
-SEMAPHORES = ["sV", "sS", "sT", "sG", "loc", "out", "h0", "h1", "h2", "a0", "a1", "a2"] + ["d%d" % _i for _i in range(8)]
+SEMAPHORES = ["sV", "sS", "sT", "sG", "loc", "out", "h0", "h1", "h2", "a0", "a1", "a2"] + ["d%d" % _i for _i in range(6)]
 
 A = AluOpType
 F = ActivationFunctionType
 
 
 def _bits(engs):
-    m = 0
-    for e in engs:
-        m |= 1 << e
-    return m
+    return sum(1 << e for e in engs)
 
 
 def _halo_engines(T, topo, q, side):
@@ -64,12 +48,12 @@ def _halo_engines(T, topo, q, side):
     return engs
 
 
-def _all_mask(T, topo, q):
+def _all_engines(T, topo, q):
     m = -1
     for o in range(N):
         if o != q:
             m &= topo.mask(T.cores[q], T.cores[o])
-    return m
+    return m, bin(m).count("1")
 
 
 def rank_program(g, core, T, topo):
@@ -115,10 +99,9 @@ def rank_program(g, core, T, topo):
         fn().then_inc(T.sem["s" + q], 1)
         done(q, "s" + q, 1, reads, writes)
 
-    def load(q, out, in_, key, reads=()):
+    def load(q, out, in_, key):
         s = "d%d" % nd[0]
         nd[0] += 1
-        need(q, list(reads), [])
         queue[q].dma_start(out, in_).then_inc(T.sem[s], 16)
         done(q, s, 16, [], [key])
 
@@ -131,29 +114,38 @@ def rank_program(g, core, T, topo):
         total[s] = n
         wr[key] = (s, n, {})
 
-    def ts(out, in0, s1, s2, o0, o1, reads, writes):
+    def ts(out, in0, s1, s2, o0, o1, reads, key):
         if s2 is None:
-            op("V", lambda: V.tensor_scalar(out, in0, s1, None, o0), reads, writes)
+            op("V", lambda: V.tensor_scalar(out, in0, s1, None, o0), reads, [key])
         else:
-            op("V", lambda: V.tensor_scalar(out, in0, s1, s2, o0, o1), reads, writes)
+            op("V", lambda: V.tensor_scalar(out, in0, s1, s2, o0, o1), reads, [key])
 
-    def tt(out, in0, in1, o, reads, writes):
-        op("V", lambda: V.tensor_tensor(out, in0, in1, o), reads, writes)
+    def add(out, in0, s1, reads, key):
+        ts(out, in0, s1, None, A.add, None, reads, key)
 
-    def turn(out, in_, reads, key):
-        op("V", lambda: V.transpose(out, in_), reads, [key])
+    def tt(out, in0, in1, o, reads, key):
+        op("V", lambda: V.tensor_tensor(out, in0, in1, o), reads, [key])
 
-    def fill(ap, c, key):
-        op("V", lambda: V.memset(ap, c), [], [key])
+    def cp(out, in_, reads, *keys):
+        op("V", lambda: V.tensor_copy(out, in_), reads, list(keys))
 
-    def lin(out, in_, scale, bias, reads, writes):
-        op("S", lambda: g.scalar.activation(out, in_, F.Identity, bias=float(bias), scale=float(scale)), reads, writes)
+    def scan(out, d0, d1, o0, reads, key):
+        op("V", lambda: V.tensor_tensor_scan(out, d0, d1, 0.0, o0, A.add), reads, [key])
 
-    def iota(out, pat, base, cm, key, flt=True):
-        if flt:
-            op("G", lambda: g.iota(out, pat, base, cm, allow_small_or_imprecise_dtypes=True), [], [key])
-        else:
-            op("G", lambda: g.iota(out, pat, base, cm), [], [key])
+    def turn(out, in_, reads, *keys):
+        op("V", lambda: V.transpose(out, in_), reads, list(keys))
+
+    def fill(ap, c, key, reads=()):
+        op("V", lambda: V.memset(ap, c), list(reads), [key])
+
+    def act(out, in_, f, reads, writes, **kw):
+        op("S", lambda: g.scalar.activation(out, in_, f, **kw), reads, writes)
+
+    def lin(out, in_, scale, bias, reads, key):
+        act(out, in_, F.Identity, reads, [key], bias=bias, scale=scale)
+
+    def iota(out, pat, key):
+        op("G", lambda: g.iota(out, pat, 0, 0, allow_small_or_imprecise_dtypes=True), [], [key])
 
     def quant(name, a, n, src, reads, key):
         op("V", lambda: V.quantize_mx(T[name][:, a:a + n], T[name + "s"][:, a:a + n], src), reads, [key])
@@ -162,6 +154,9 @@ def rank_program(g, core, T, topo):
         op("T", lambda: g.tensor.matmul_mx(T["ps%d" % bank][:, 0:n], T[ln][:, la:la + 128], T[ln + "s"][:, la:la + 128],
                                            T[rn][:, ra:ra + n], T[rn + "s"][:, ra:ra + n], True, True),
            reads, ["ps%d" % bank])
+
+    def u8(name, a, n):
+        return T[name][:, a:a + n].bitcast(dt.uint8)
 
     def dst(o):
         rid, pid = topo.addr(T.cores[o], core)
@@ -175,10 +170,7 @@ def rank_program(g, core, T, topo):
             trs = []
             for s in sides:
                 a, b = from_to[s]
-                if codes:
-                    i, o = T[src][:, a:a + n].bitcast(dt.uint8), T[dname][:, b:b + n].bitcast(dt.uint8)
-                else:
-                    i, o = T[src + "s"][:, a:a + n], T[dname + "s"][:, b:b + n]
+                i, o = (u8(src, a, n), u8(dname, b, n)) if codes else (T[src + "s"][:, a:a + n], T[dname + "s"][:, b:b + n])
                 engs = _halo_engines(T, topo, r, s)
                 trs.append(RemoteDMATransfer(dst_ids=[dst(r + s)], dma_engine_mask=_bits(engs),
                                              remote_sem=T.sem["h%d" % t], src=i, dst=o))
@@ -190,122 +182,93 @@ def rank_program(g, core, T, topo):
         need("G", ["c%d_%d" % (t, j) for j in range(4)], [])
         slot = T["cg%d" % t][:, 4 * r:4 * r + 4]
         others = [(r + k) % N for k in range(1, N)]
-        m = _all_mask(T, topo, r)
+        m, n = _all_engines(T, topo, r)
         g.remote_dma_fused([RemoteDMATransfer(dst_ids=[dst(o) for o in others], dma_engine_mask=m,
                                               remote_sem=T.sem["a%d" % t], srcs=[slot], dsts=[slot for o in others])],
                            local_sem=T.sem.loc)
-        total["loc"] = total.get("loc", 0) + bin(m).count("1")
-        arrives("ag%d" % t, "a%d" % t, sum(bin(_all_mask(T, topo, o)).count("1") for o in others))
+        total["loc"] = total.get("loc", 0) + n
+        arrives("ag%d" % t, "a%d" % t, sum(_all_engines(T, topo, o)[1] for o in others))
 
     def cost(t, j, name, a, reads):
         mm(4 + j, name, a, "qa", 0, 128, reads + ["qa"])
-        op("S", lambda: g.scalar.activation(T.junk[:, 128 * j:128 * j + 128], T["ps%d" % (4 + j)][:, 0:128], F.Sign,
-                                            bias=T.tiny[:, 0:1], accum_out=T["cg%d" % t][:, 4 * r + j:4 * r + j + 1]),
-           ["tiny"], ["ps%d" % (4 + j), "junk%d" % j, "c%d_%d" % (t, j)])
+        act(T.junk[:, 128 * j:128 * j + 128], T["ps%d" % (4 + j)][:, 0:128], F.Sign, ["tiny"],
+            ["ps%d" % (4 + j), "junk%d" % j, "c%d_%d" % (t, j)], bias=T.tiny[:, 0:1],
+            accum_out=T["cg%d" % t][:, 4 * r + j:4 * r + j + 1])
 
-    def products(src, a, n, reads):
+    def products(src, a, n, reads, bank=0):
         for b in range(4):
-            mm(b, "qw", 128 * b, src, a, n, reads + ["qw%d" % (b // 2)])
+            mm(bank + b, "qw", 128 * b, src, a, n, reads + ["qw%d" % (b // 2)])
 
-    def totile(h, n, on_vector, banks=(0, 1, 2, 3)):
-        for b in banks:
-            o, i = T[h][:, b:4 * n:4], T["ps%d" % b][:, 0:n]
-            if b in on_vector:
-                ts(o, i, 0.0, 0.0625, A.max, A.mult, [], ["ps%d" % b, h + "_%d" % b])
-            else:
-                op("S", lambda: g.scalar.activation(o, i, F.Relu, scale=0.0625), [], ["ps%d" % b, h + "_%d" % b])
+    def relu(o, i, on_vector, reads, writes):
+        if on_vector:
+            op("V", lambda: V.tensor_scalar(o, i, 0.0, 0.0625, A.max, A.mult), reads, writes)
+        else:
+            act(o, i, F.Relu, reads, writes, scale=0.0625)
+
+    def totile(h, n, on_vector, a=0, bank=0):
+        for b in range(4):
+            relu(T[h][:, 4 * a + b:4 * (a + n):4], T["ps%d" % (bank + b)][:, 0:n], b in on_vector, [],
+                 ["ps%d" % (bank + b), h + "_%d" % b])
         return [h + "_%d" % b for b in range(4)]
 
-    def bound(t, side):
-        h, n = "hi%d" % t, 4 * S * (t + 1)
-        v = T[h][:, 0:n] if side == "l" else T[h][:, 4 * P - n:4 * P]
-        ts(v, v, 2.0 ** 31, None, A.min, None, [h + "_%d" % b for b in range(4)], [h + side])
+    def bound(a, key):
+        v = T.hi1[:, a:a + 8 * S]
+        ts(v, v, 2.0 ** 31, None, A.min, None, ["hi1_%d" % b for b in range(4)], key)
 
-    def interior_codes(t):
-        h = "hi%d" % t
-        quant("m%d" % t, I0 if t < R - 1 else 0, P, T[h][:, 0:4 * P], [h + "_%d" % b for b in range(4)] + [h + "l", h + "r"],
-              "mi%d" % t)
-        if t < R - 1:
-            cost(t + 1, 1, "m%d" % t, I0, ["mi%d" % t])
-            cost(t + 1, 2, "m%d" % t, I0 + 128, ["mi%d" % t])
+    def interior_costs(t):
+        cost(t + 1, 1, "m%d" % t, I0, ["mi%d" % t])
+        cost(t + 1, 2, "m%d" % t, I0 + 128, ["mi%d" % t])
 
-    def edge_out(t):
-        h = "he%d" % t
-        keys = totile(h, 2 * W, (0, 2))
-        quant("m%d" % t, MR, 2 * W, T[h][:, 0:8 * W], keys, "me%d" % t)
-        ends = {-1: (ML, MA), 1: (MR, 0)}
-        halo(t + 1, "m%d" % t, "m%d" % t, W, ends, ["me%d" % t], (True, False) if t == 0 else (False,))
-        cost(t + 1, 0, "m%d" % t, MA - 128, ["me%d" % t])
-        cost(t + 1, 3, "m%d" % t, ML - 128, ["me%d" % t, "mi%d" % t])
+    def edge_costs(t):
+        cost(t + 1, 0, "m%d" % t, (L0 + W if t == 0 else MA) - 128, ["me%d" % t])
+        cost(t + 1, 3, "m%d" % t, (L0 if t == 0 else ML) - 128, ["me%d" % t, "mi%d" % t])
         share(t + 1)
-        if t > 0:
-            halo(t + 1, "m%d" % t, "m%d" % t, W, ends, ["me%d" % t], (True,))
-
-    def pick(t):
-        m, e, off = "m%d" % (t - 1), "e%d" % t, T["off%d" % t][:, 0:10]
-        reads = ["mi%d" % (t - 1), "me%d" % (t - 1), "arr%d" % t, "off%d" % t]
-        op("V", lambda: V.tensor_copy(T[e][:, 0:160].bitcast(dt.uint32), T[m][:, 0:MA + W].bitcast(dt.uint32).indirect(off)),
-           reads, ["ec%d" % t])
-        op("S", lambda: g.scalar.activation(T[e + "s"][:, 0:160], T[m + "s"][:, 0:MA + W].indirect(off), F.Copy),
-           reads, ["es%d" % t])
-        products(e, 8, 2 * W, ["ec%d" % t, "es%d" % t])
 
     def borders(t, between):
         def gap(k):
-            for fn in between.get(k, ()):
-                fn()
-        cg, dm = T["cg%d" % t], ("dm0" if t == 0 else "dm1")
+            if k in between:
+                between[k]()
+        cg = T["cg%d" % t]
         reads = ["ag%d" % t] + ["c%d_%d" % (t, j) for j in range(4)]
         if t > 0:
-            tt(T.zz[:], cg[:], T.cap[:], A.min, reads + ["cap"], ["zz"])
+            tt(T.zz[:], cg[:], T.cap[:], A.min, reads + ["cap"], "zz")
             cg, reads = T.zz, ["zz"]
         gap(0)
         for a in range(4):
             turn(T.yt[0:32, 32 * a:32 * a + 32], cg[32 * a:32 * a + 32, 0:32], reads, "yt%d" % a)
         gap(1)
-        op("V", lambda: V.tensor_tensor_scan(T.pref[0:32, 1:129], T.yt[0:32, 0:128], T.cadd[0:32, 0:128], 0.0, A.add, A.add),
-           ["yt%d" % a for a in range(4)] + ["cadd"], ["pref"])
+        scan(T.pref[0:32, 1:193], T.yt[0:32, 0:192], T.cadd[0:32, 0:192], A.add,
+             ["yt%d" % a for a in range(4)] + ["ytz", "cadd", "caddz"], "pref")
         gap(2)
-        ts(T.mx[0:32, :], T.wtm[0:32, :], T.pref[0:32, 128:129], None, A.mult, None, ["wtm", "pref"], ["mx"])
+        turn(T.tt[0:32, 0:64], T.pref[0:32, 128:192], ["pref"], "tt")
         gap(3)
-        turn(T.mt[0:32, :], T.mx[0:32, :], ["mx"], "mt")
+        scan(T.th[0:32, 0:65], T.hm[0:32, 0:65], T.tt[0:32, 0:65], A.mult, ["tt", "ttz", "hm", "hmh"], "th")
         gap(4)
-        op("V", lambda: V.tensor_reduce(T.th[0:32, :], T.mt[0:32, :], AxisListType.X, A.add), ["mt"], ["th"])
-        gap(5)
         w0 = 0 if t == 0 else W0
-        ts(T.ind[0:32, w0:128], T.pref[0:32, w0:128], T.th[0:32, 0:1], None, A.is_lt, None, ["pref", "pref0", "th"], ["ind"])
+        ts(T.ind[0:32, 32 + w0:160], T.pref[0:32, w0:128], T.th[0:32, 64:65], None, A.is_lt, None, ["pref", "pref0", "th"], "ind")
+        gap(5)
+        op("V", lambda: V.tensor_reduce(T.cnt[0:32, :], T.ind[0:32, 31 + w0:160], AxisListType.X, A.add), ["ind", "lo"], ["cnt"])
         gap(6)
-        op("V", lambda: V.tensor_reduce(T.cnt[0:32, :], T.ind[0:32, w0:128], AxisListType.X, A.add), ["ind"], ["cnt"])
+        ts(T.cl[0:32, :], T.yt[0:32, 128:160], T.cnt[0:32, 0:1], float(S), A.max, A.min, ["ytz", "cnt"], "cl")
         gap(7)
-        ts(T.cl[0:32, :], T.amat[0:32, :], T.cnt[0:32, 0:1], T.bcol[0:32, 0:1], A.max, A.min, ["amat", "bcol", "cnt"], ["cl"])
-        gap(8)
         for a in range(4):
-            turn(T[dm][32 * a:32 * a + 32, 32:64], T.cl[0:32, :], ["cl"], dm + "_%d" % a)
-        gap(9)
-        return T[dm], [dm + "_%d" % a for a in range(4)] + [dm + "a", dm + "b"]
+            turn(T.dm[32 * a:32 * a + 32, 32:64], T.cl[0:32, :], ["cl"], "dm%d" % a)
+        gap(8)
+        tt(T["s%d" % t][:], T.dm[:, 31:64:4], T.dm[:, 32:65:4], A.add, ["dm%d" % a for a in range(4)] + ["dma", "dmb"], "s%d" % t)
 
-    def clamp_lo():
-        turn(T.amat[0:32, :], T.ar[0:32, :], ["ar0", "ar3", "ar"], "amat")
-
-    def clamp_hi():
-        ts(T.bcol[0:32, :], T.amat[0:32, 0:1], float(S), None, A.add, None, ["amat"], ["bcol"])
-
-    def picklist(t):
-        d, dk = T["dd%d" % t], "dd%d" % t
-        dr, dlf = (-2.0 * S, float(I0 - S - ML)) if t == 0 else (T.dl[:, 0:1], T.dl[:, 1:2])
-        return [
-            lambda: ts(T.lt[:, 0:5], T.base[:, 0:5], d[:, r + 1:r + 2], None, A.add, None, ["base", dk], ["ltr"]),
-            lambda: ts(T.lt[:, 5:10], T.base[:, 5:10], d[:, r:r + 1], None, A.add, None, ["base", dk], ["ltl"]),
-            lambda: ts(T.lu[:, 0:5], T.lt[:, 0:5], float(MR), dr, A.is_lt, A.mult, ["ltr", "dl0"], ["lur"]),
-            lambda: ts(T.lu[:, 5:10], T.lt[:, 5:10], float(MA), dlf, A.is_ge, A.mult, ["ltl", "dl1"], ["lul"]),
-            lambda: tt(T.lw[:], T.lt[:], T.lu[:], A.add, ["ltr", "ltl", "lur", "lul"], ["lw"]),
-            lambda: op("V", lambda: V.tensor_copy(T["off%d" % (t + 1)][:], T.lw[:]), ["lw"], ["off%d" % (t + 1)])]
-
-    def valid():
-        tt(T.val[:], T.pp[:], T.xl[:], A.is_ge, ["pp", "ppa", "ppb", "xl0", "xl1", "xl2", "xl3"], ["val"])
+    def held(j, t):
+        s, o = (T["s%d" % t][:, 0:8], A.is_le) if j < 2 else (T["s%d" % t][:, 1:9], A.is_ge)
+        ts(T.val[:, j:32:4], s, T.pc[:, j:j + 1], None, o, None, ["s%d" % t, "pc", "pca", "pcb"], "val%d" % j)
 
     def mask():
-        ts(T.cap[:], T.val[:], 400.0, -130.0, A.mult, A.add, ["val"], ["cap"])
+        ts(T.cap[:], T.val[:], 400.0, -130.0, A.mult, A.add, ["val%d" % j for j in range(4)], "cap")
+
+    def start(j, t):
+        a = j // 3
+        ts(T.nar[0:32, j:32:4], T["s%d" % t][0:32, a:a + 8], -1.0, None, A.mult, None, ["s%d" % t, "nar"], "nar%d" % j)
+
+    def starts(w0):
+        turn(T.ind[0:32, w0:w0 + 32], T.nar[0:32, :], ["nar", "nar0", "nar3"], "lo", "ind")
 
     load("Y", T.xe[:, 0:4 * S], T.x[:, 4 * (P - S):4 * P], "xer")
     load("S", T.xe[:, 4 * S:8 * S], T.x[:, 0:4 * S], "xel")
@@ -314,160 +277,165 @@ def rank_program(g, core, T, topo):
     load("Y", T.wt[:, 0:1024], T.w[:, 0:1024], "wt0")
     load("S", T.wt[:, 1024:2048], T.w[:, 1024:2048], "wt1")
 
-    iota(T.pint[:, 0:1], [[1, 1]], 0, 1, "pint0", False)
-    iota(T.j0[:], [[16, 25]], 0, 0, "j0")
-    iota(T.pcol[:], [[1, 1]], 0, 1, "pcol")
-    iota(T.i1[0:32, :], [[1, 9], [0, 4]], 0, 0, "i1")
-    iota(T.i2[0:32, :], [[1, 32]], 0, -1, "i2")
-    iota(T.b256[:], [[P, 9]], 0, 0, "b256")
     fill(T.xe[:, 8 * S:512], 0.0, "xez")
+    fill(T.hm[0:32, 0:64], 1.0, "hm")
+    op("G", lambda: g.iota(T.pint[:, 0:2], [[1, 2]], 0, 1), [], ["pint0"])
+    iota(T.j0[:], [[16, 25]], "j0")
+    iota(T.bdr[:, 0:9], [[P, 9]], "bd0")
+    op("G", lambda: g.affine_select(T.hm[0:32, 32:64], T.hm[0:32, 32:64], [[-1, 32]], A.not_equal, -1.0, 0, 1), ["hm"], ["hm"])
     fill(T.tiny[:], -2.0 ** -120, "tiny")
-    fill(T.cg0[:, 4 * r + 1:4 * r + 2], -130.0, "c0_1")
-    fill(T.cg0[:, 4 * r + 2:4 * r + 3], -130.0, "c0_2")
-    fill(T.he2[:, 8 * W:8 * W + 8], 0.0, "hez")
-    fill(T.cadd[0:32, :], 130.0, "cadd")
+    fill(T.cg0[:, 4 * r + 1:4 * r + 3], -130.0, "c0_1")
+    wr["c0_2"] = wr["c0_1"]
+    fill(T.hm[0:32, 64:65], 0.5, "hmh")
+    fill(T.tt[0:32, 64:65], 0.0, "ttz")
+    fill(T.yt[0:32, 128:192], 0.0, "ytz")
+    fill(T.cadd[0:32, 0:128], 130.0, "cadd")
+    fill(T.cadd[0:32, 128:192], 0.0, "caddz")
     fill(T.pref[0:32, 0:1], 0.0, "pref0")
-    fill(T.dm0[:, 31:32], 128.0, "dm0a")
-    fill(T.dm0[:, 64:65], 0.0, "dm0b")
-    fill(T.dm1[:, 31:32], 2.0 * S, "dm1a")
-    fill(T.dm1[:, 64:65], 1.0 * S, "dm1b")
-    fill(T.ar[0:32, :], 0.0, "ar")
-    fill(T.sg[:], 1.0, "sg")
-    fill(T.xl[:, 1:32:4], 2.0 * S, "xl1")
-    fill(T.xl[:, 2:32:4], 1.0 - 128 + 2 * S, "xl2")
-    op("V", lambda: V.memset(T.ar[0:32, 3:32:4], 128.0 - S), ["ar"], ["ar3"])
-    op("V", lambda: V.memset(T.sg[:, 2:32:4], -1.0), ["sg"], ["sg2"])
-    op("V", lambda: V.memset(T.sg[:, 3:32:4], -1.0), ["sg"], ["sg3"])
+    fill(T.nar[0:32, :], 0.0, "nar")
 
     quant("qxe", 0, 128, T.xe[:], ["xer", "xel", "xez"], "qxe")
-    halo(0, "qxe", "e0", S, {-1: (S, 128), 1: (0, 128 + S)}, ["qxe"])
-    if len(sides) == 1:
-        z = 128 + S if r == 0 else 128
-        load("Y", T.e0[:, z:z + S].bitcast(dt.uint8), T.qxe[:, 2 * S:3 * S].bitcast(dt.uint8), "e0z", ["qxe"])
-        load("Y", T.e0s[:, z:z + S], T.qxes[:, 2 * S:3 * S], "e0zs", ["qxe"])
+    halo(0, "qxe", "e0", S, {-1: (S, S if r == 1 else 0), 1: (0, S)}, ["qxe"])
 
-    ts(T.pint[:, 1:2], T.pint[:, 0:1], 15, None, A.bitwise_and, None, ["pint0"], ["pint1"])
-    ts(T.pp[:], T.sg[:], T.pcol[:, 0:1], None, A.mult, None, ["sg", "sg2", "sg3", "pcol"], ["pp"])
-    ts(T.wa[0:32, :], T.i2[0:32, :], 0.0, None, A.is_gt, None, ["i2"], ["wa"])
-    ts(T.wb[0:32, :], T.i1[0:32, 1:33], 1.0 / N, None, A.mult, None, ["i1"], ["wb"])
-    op("V", lambda: V.tensor_copy(T.p16[:], T.pint[:, 1:2]), ["pint1"], ["p16"])
-    quant("e0", 128 + 2 * S, P, T.xt[:], ["xt"], "e0b")
+    fill(T.nar[0:32, 3:32:4], S - 128.0, "nar3", ["nar"])
+    ts(T.pint[:, 2:3], T.pint[:, 0:1], 15, None, A.bitwise_and, None, ["pint0"], "pint2")
+    ts(T.pint[:, 3:4], T.pint[:, 1:2], 2, None, A.arith_shift_right, None, ["pint0"], "pint3")
+    for j, c in enumerate((W0, S, 128 - W - 1, W0 + S - 1)):
+        add(T.pc[:, j:j + 1], T.pint[:, 0:1], -float(c), ["pint0"], "pc")
+    fill(T.dm[:, 31:32], float(S), "dma")
+    fill(T.dm[:, 64:65], 0.0, "dmb")
+    cp(T.p16[:], T.pint[:, 2:3], ["pint2"], "p16")
+    ts(T.rc[:], T.pint[:, 3:4], -2.0 / N, 1.0, A.mult, A.add, ["pint3"], "rc")
+    starts(0)
+    if len(sides) == 1:
+        z = 4 * (128 + S if r == 0 else 128)
+        fill(T.hi0[:, z:z + 4 * S], 0.0, "hi0z")
+
+    quant("e0", 2 * S, P, T.xt[:], ["xt"], "e0b")
     quant("qa", 0, 128, T.at[:], ["at"], "qa")
-    cost(0, 0, "e0", 128 + 2 * S, ["e0b"])
-    cost(0, 3, "e0", 256 + 2 * S, ["e0b"])
+    cost(0, 0, "e0", 2 * S, ["e0b"])
+    cost(0, 3, "e0", 128 + 2 * S, ["e0b"])
     share(0)
-    quant("e0", 0, 128, T.xt[:, 512:1024], ["xt"], "e0a")
-    ts(T.jj[:], T.j0[:], T.p16[:, 0:1], None, A.add, None, ["j0", "p16"], ["jj"])
-    tt(T.wtm[0:32, :], T.wb[0:32, :], T.wa[0:32, :], A.subtract, ["wa", "wb"], ["wtm"])
+    add(T.jj[:], T.j0[:], T.p16[:, 0:1], ["j0", "p16"], "jj")
+    ts(T.hm[0:32, 32:33], T.hm[0:32, 32:33], T.rc[0:32, 0:1], None, A.mult, None, ["rc"], "hm")
+    fill(T.pc[0:32, 3:4], 1000.0, "pca", ["pc"])
+    fill(T.pc[32:W0, 3:4], 1000.0, "pcb", ["pc"])
+    fill(T.s1[:], float(S), "s1")
+    c1, c4 = float(FL - AL - S), float(AR - FR - S)
+    fill(T.cst[:, 0:JL], -1.0 / (8 * c1), "cst0")
+    fill(T.cst[:, JL:25], 1.0 / (8 * c4), "cst1")
+    held(1, 1)
+    held(2, 1)
+    if len(sides) == 1:
+        quant("e2", 0, 2 * W, T.xt[:, 0:8 * W], ["xt"], "e2z")
+    lin(T.bv[:, 0:5], T.jj[:, 0:5], 1.0, MR - 8.0, ["jj"], "bvr")
+    lin(T.bv[:, 5:10], T.jj[:, 0:5], 1.0, float(L0 - S), ["jj"], "bvl")
+    lin(T.bk[:, 0:9], T.bdr[:, 0:9], 1.0, -float(S), ["bd0"], "bk0")
+    lin(T.jm[:, JL:25], T.jj[:, JL:25], 1.0, -float(P), ["jj"], "jm")
+    lin(T.ptb[:, 0:JL], T.jj[:, 0:JL], 1.0, -4.0 * S, ["jj"], "ptb0")
+    lin(T.jfb[:, 0:JL], T.jj[:, 0:JL], 1.0, AL + 0.25, ["jj"], "jfb0")
+    lin(T.pt[:, 1:2 * JL:2], T.jj[:, 0:JL], 1.0, -float(S), ["jj"], "pt1")
     quant("qw", 0, 256, T.wt[:, 0:1024], ["wt0"], "qw0")
     quant("qw", 256, 256, T.wt[:, 1024:2048], ["wt1"], "qw1")
-    products("e0", 128 + 2 * S, P, ["e0b"])
-    clamp_lo()
-    totile("hi0", P, (0, 2))
-    clamp_hi()
-    interior_codes(0)
-    lin(T.bv[:, 0:5], T.jj[:, 0:5], 1, MR - 8, ["jj"], ["bvr"])
-    lin(T.bv[:, 5:10], T.jj[:, 0:5], 1, ML, ["jj"], ["bvl"])
-    products("e0", 128 - 2 * S, 2 * W, ["e0a", "e0b", "arr0", "e0z", "e0zs"])
-    edge_out(0)
+    products("e0", 2 * S, P, ["e0b"])
+    own = []
+    for b in range(4):
+        for a, pa in ((0, 128), (128 + 2 * S, 0)):
+            own.append("own%d_%d" % (b, a))
+            relu(T.hi0[:, 4 * a + b:4 * (a + 128):4], T["ps%d" % b][:, pa:pa + 128], b % 2 == 0, ["ps%d" % b], own[-1:])
+    quant("m0", I0, 128, T.hi0[:, 4 * (128 + 2 * S):4 * (P + 2 * S)], own, "mi0a")
+    quant("m0", I0 + 128, 128, T.hi0[:, 0:512], own, "mi0")
+    products("e0", 0 if len(sides) == 2 else S, 128, ["e0b", "arr0"], 4)
+    keys = totile("hi0", S * len(sides), (0, 2), 128 + S if r == N - 1 else 128, 4)
+    quant("m0", MR, A0 - MR, T.hi0[:, 4 * W0:4 * (W0 + A0 - MR)], keys + own + ["hi0z"], "me0")
+    halo(1, "m0", "m0", W, {-1: (L0, A0), 1: (MR + S, 0)}, ["me0"])
+    interior_costs(0)
+    edge_costs(0)
     products("m0", I0, P, ["mi0"])
-    totile("hi1", P, ())
-    dm, keys = borders(0, {
-        2: [lambda: op("V", lambda: V.memset(T.pp[0:32, 3:32:4], -1000.0), ["pp"], ["ppa"])],
-        3: [lambda: op("V", lambda: V.memset(T.pp[32:W0, 3:32:4], -1000.0), ["pp"], ["ppb"])],
-        4: [lambda: ts(T.bu[:, 0:5], T.jj[:, 0:5], 8.0 + 2 * S, 0.0 if r == N - 1 else float(MA - S - MR),
-                       A.is_ge, A.mult, ["jj"], ["bur"])],
-        5: [lambda: ts(T.bu[:, 5:10], T.jj[:, 0:5], float(S), 0.0 if r == 0 else float(S - ML),
-                       A.is_lt, A.mult, ["jj"], ["bul"])],
-        6: [lambda: tt(T.base[:], T.bu[:], T.bv[:], A.add, ["bur", "bul", "bvr", "bvl"], ["base"])],
-        7: [lambda: bound(1, "l")], 8: [lambda: bound(1, "r")]})
-    tt(T.ss[:], dm[:, 31:64:4], dm[:, 32:65:4], A.add, keys, ["ss"])
-    interior_codes(1)
-    ts(T.dd0[:], T.ss[:], -128.0, None, A.add, None, ["ss"], ["dd0"])
-    for fn in picklist(0):
-        fn()
-    d = T.dd0
-    lin(T.xl[:, 0:32:4], d[:, 0:8], 1, W0 + S, ["dd0"], ["xl0"])
-    lin(T.xl[:, 3:32:4], d[:, 1:9], -1, 1 - W0 - 2 * S, ["dd0"], ["xl3"])
-    lin(T.ar[0:32, 0:32:4], d[0:32, 0:8], 1, S, ["dd0"], ["ar0"])
-    lin(T.ar[0:32, 3:32:4], d[0:32, 1:9], 1, S, ["dd0"], ["ar3"])
-    pick(1)
-    valid()
-    clamp_lo()
-    edge_out(1)
-    mask()
-    clamp_hi()
-    lin(T.kk[:], d[:], 2, W, ["dd0"], ["kk"])
-    lin(T.kx0[:], d[:], -2, W0 + S - W, ["dd0"], ["kx0"])
-    lin(T.kx3[:], d[:], 2, W + 1 - W0 - 2 * S, ["dd0"], ["kx3"])
-    lin(T.xl[:, 1:32:4], d[:, 0:8], 1, 2 * S, ["dd0"], ["xl1"])
-    lin(T.xl[:, 2:32:4], d[:, 1:9], -1, 1 - 128 + 2 * S, ["dd0"], ["xl2"])
-    lin(T.dl[:, 0:1], d[:, r + 1:r + 2], 1, -2 * S, ["dd0"], ["dl0"])
-    lin(T.dl[:, 1:2], d[:, r:r + 1], 1, I0 - S - ML, ["dd0"], ["dl1"])
-    products("m1", I0, P, ["mi1"])
-    totile("hi2", P, ())
-    dm, keys = borders(1, {2: [lambda: tt(T.bdr[:, 0:9], T.dd0[:], T.b256[:], A.add, ["dd0", "b256"], ["bd0"])]})
-    tt(T.ss[:], dm[:, 31:64:4], dm[:, 32:65:4], A.add, keys, ["ss"])
-    interior_codes(2)
-    mm(5, "qa", 0, "m2", 0, P, ["qa", "mi2"])
-    tt(T.xl[:, 0:32:4], T.ss[:, 0:8], T.kx0[:, 0:8], A.add, ["ss", "kx0"], ["xl0"])
-    tt(T.xl[:, 3:32:4], T.kx3[:, 1:9], T.ss[:, 1:9], A.subtract, ["ss", "kx3"], ["xl3"])
-    tt(T.dd1[:], T.ss[:], T.kk[:], A.subtract, ["ss", "kk"], ["dd1"])
-    valid()
-    tt(T.dev1[:], T.dd1[:], T.dd0[:], A.add, ["dd1", "dd0"], ["dev1"])
-    mask()
-    d = T.dd1
-    lin(T.ar[0:32, 0:32:4], d[0:32, 0:8], 1, S, ["dd1"], ["ar0"])
-    lin(T.ar[0:32, 3:32:4], d[0:32, 1:9], 1, S, ["dd1"], ["ar3"])
-    lin(T.k2[:], d[:], 2, W, ["dd1"], ["k2"])
-    lin(T.fc[:, 0:1], T.dev1[:, r:r + 1], 1, 2 * S, ["dev1"], ["fc0"])
-    lin(T.fc[:, 1:2], T.dev1[:, r:r + 1], -1, FL + S, ["dev1"], ["fc1"])
-    lin(T.fc[:, 2:3], T.dev1[:, r + 1:r + 2], 1, P - 2 * S, ["dev1"], ["fc2"])
-    lin(T.fc[:, 3:4], T.dev1[:, r + 1:r + 2], -1, FR - P + 2 * S, ["dev1"], ["fc3"])
-    op("S", lambda: g.scalar.activation(T.ys[:, 0:P], T.ps5[:, 0:P], F.Copy), [], ["ps5", "ysi"])
+    keys = totile("hi1", P, ())
+    borders(0, {
+        1: lambda: ts(T.bu[:, 0:5], T.jj[:, 0:5], 8.0 + 2 * S, 0.0 if r == N - 1 else float(A0 - 2 * S - MR),
+                      A.is_ge, A.mult, ["jj"], "bur"),
+        2: lambda: ts(T.bu[:, 5:10], T.jj[:, 0:5], float(S), 0.0 if r == 0 else float(S - L0), A.is_lt, A.mult, ["jj"], "bul"),
+        3: lambda: fill(T.fm[:, 0:100:4], 0.0, "fm0"),
+        4: lambda: tt(T.base[:], T.bu[:], T.bv[:], A.add, ["bur", "bul", "bvr", "bvl"], "base"),
+        5: lambda: fill(T.fm[:, 2:100:4], -8.0, "fm2"),
+        6: lambda: fill(T.fm[:, 3:4 * JL:4], c1, "fm3"),
+        7: lambda: fill(T.fm[:, 4 * JL + 3:100:4], c4, "fm4"),
+        8: lambda: fill(T.hi2[:, 0:4 * FI], 0.0, "hiz")})
+    bound(0, "hi1l")
+    sl, sr = T.s0[:, r:r + 1], T.s0[:, r + 1:r + 2]
+    add(T.off1[:, 0:5], T.base[:, 0:5], sr, ["base", "s0"], "off1r")
+    add(T.off1[:, 5:10], T.base[:, 5:10], sl, ["base", "s0"], "off1l")
+    bound(4 * P - 8 * S, "hi1r")
+    held(0, 0)
+    quant("m1", I0, P, T.hi1[:], keys + ["hi1l", "hi1r"], "mi1")
 
-    def consts():
-        tt(T.kd[:], T.dev1[:], T.k2[:], A.subtract, ["dev1", "k2"], ["kd"])
-        lin(T.fc[:, 4:5], T.kd[:, r + 1:r + 2], 1, P, ["kd"], ["fc4"])
-        op("S", lambda: g.scalar.activation(T.jk[:], T.jj[:], F.Identity, bias=T.kd[:, r:r + 1]), ["jj", "kd"], ["jk"])
+    reads, off = ["mi0", "me0", "arr1", "off1r", "off1l"], T.off1[:, 0:10]
+    cp(T.e1[:, 0:160].bitcast(dt.uint32), T.m0[:, 0:A0 + W].bitcast(dt.uint32).indirect(off), reads, "ec1")
+    act(T.e1s[:, 0:160], T.m0s[:, 0:A0 + W].indirect(off), F.Copy, reads, ["es1"])
+    interior_costs(1)
+    products("e1", 8, 2 * W, ["ec1", "es1"])
+    held(3, 0)
+    start(0, 0)
+    start(3, 0)
+    mask()
+    keys = totile("he1", 2 * W, (0, 2))
+    starts(W0)
+    quant("m1", MR, 2 * W, T.he1[:], keys, "me1")
+    ends = {-1: (ML, W), 1: (MR, 0)}
+    halo(2, "m1", "e2", W, ends, ["me1"], (False,))
+    edge_costs(1)
+    halo(2, "m1", "e2", W, ends, ["me1"], (True,))
+    products("m1", I0, E, ["mi1", "me1"])
+    keys = totile("hi2", E, (), FI)
+    lin(T.fm[:, 1:4 * JL:4], T.cst[:, 0:JL], sl, (FI - FL - 2 * S) / (-8 * c1), ["s0", "cst0"], "fm1")
+    lin(T.fm[:, 4 * JL + 1:100:4], T.cst[:, JL:25], sr, (FR - FI - P + 3 * S) / (-8 * c4), ["s0", "cst1"], "fm5")
+    borders(1, {0: lambda: held(1, 0), 1: lambda: held(2, 0),
+                2: lambda: tt(T.bdr[:, 0:9], T.s0[:], T.bk[:, 0:9], A.add, ["s0", "bk0"], "bd0"),
+                3: lambda: ts(T.ptb[:, JL:25], T.jm[:, JL:25], sl, sr, A.add, A.subtract, ["s0", "jm"], "ptb1"),
+                4: lambda: ts(T.jfb[:, JL:25], T.jj[:, JL:25], sl, FI + 0.25 - W, A.add, A.add, ["s0", "jj"], "jfb1"),
+                5: lambda: fill(T.fu[:, 1:4 * JL:4], 0.0, "fuz"),
+                6: lambda: add(T.bk[:, 9:18], T.bdr[:, 0:9], -float(S), ["bd0"], "bk1")})
+    sl, sr = T.s1[:, r:r + 1], T.s1[:, r + 1:r + 2]
+    held(0, 1)
+    held(3, 1)
+    start(0, 1)
+    mask()
+    start(3, 1)
+    quant("m2", 0, AL, T.hi2[:], keys + ["hiz"], "mi2")
+    lin(T.pt[:, 0:50:2], T.ptb[:], 1.0, sl, ["s1", "ptb0", "ptb1"], "pt0")
+    lin(T.jf[:], T.jfb[:], 1.0, sl, ["s1", "jfb0", "jfb1"], "jf")
 
-    pl = picklist(1)
-    pl[0](), pl[1]()
-    dm, keys = borders(2, {
-        0: [pl[2], pl[3]], 1: [pl[4]], 2: [clamp_lo], 3: [pl[5]], 4: [clamp_hi, consts],
-        5: [lambda: tt(T.bdr[:, 9:18], T.dev1[:], T.b256[:], A.add, ["dev1", "b256"], ["bd1"])],
-        6: [lambda: pick(2)],
-        7: [lambda: tt(T.kb[:], T.kd[:], T.b256[:], A.add, ["kd", "b256"], ["kb"])],
-        8: [lambda: totile("he2", 2 * W, (0,), (0, 1, 3))],
-        9: [lambda: totile("he2", 2 * W, (2,), (2,))]})
-    ca, cb = 31 + 4 * r, 32 + 4 * r
-    ts(T.ft[:], T.jk[:], dm[:, ca:ca + 1], dm[:, cb:cb + 1], A.add, A.add, keys + ["jk"], ["ft"])
-    ts(T.fe[:], T.fc[:, 4:5], dm[:, ca + 4:ca + 5], dm[:, cb + 4:cb + 5], A.add, A.add, keys + ["fc4"], ["fe"])
-    quant("m2", FR, 2 * W + 2, T.he2[:, 0:8 * W + 8], ["he2_%d" % b for b in range(4)] + ["hez"], "me2")
-    mm(6, "qa", 0, "m2", FR, 2 * W + 2, ["qa", "me2"])
-    op("S", lambda: g.scalar.activation(T.ys[:, FR:FZ + 2], T.ps6[:, 0:2 * W + 2], F.Copy), [], ["ps6", "yse"])
-    ts(T.fu1[:], T.ft[:], T.fc[:, 0:1], T.fc[:, 1:2], A.is_lt, A.mult, ["ft", "fc0", "fc1"], ["fu1"])
-    ts(T.fu2[:], T.ft[:], T.fc[:, 2:3], T.fc[:, 3:4], A.is_ge, A.mult, ["ft", "fc2", "fc3"], ["fu2"])
-    ts(T.fv[:], T.ft[:], T.fe[:, 0:1], 1000.0, A.is_ge, A.mult, ["ft", "fe"], ["fv"])
-    tt(T.fw1[:], T.ft[:], T.fu1[:], A.add, ["ft", "fu1"], ["fw1"])
-    tt(T.fw2[:], T.fu2[:], T.fv[:], A.add, ["fu2", "fv"], ["fw2"])
-    tt(T.s2[:], dm[:, 31:64:4], dm[:, 32:65:4], A.add, keys, ["s2"])
-    tt(T.fw[:], T.fw1[:], T.fw2[:], A.add, ["fw1", "fw2"], ["fw"])
-    tt(T.bdr[:, 18:27], T.s2[:], T.kb[:], A.add, ["s2", "kb"], ["bd2"])
+    products("e2", 0, 2 * W, ["arr2", "e2z"])
+    keys = totile("he2", 2 * W, ())
+    borders(2, {
+        0: lambda: starts(W0),
+        1: lambda: ts(T.jv[:, JL:25], T.ptb[:, JL:25], sl, sr, A.add, A.subtract, ["s1", "ptb1"], "jv"),
+        2: lambda: tt(T.bdr[:, 9:18], T.s1[:], T.bk[:, 9:18], A.add, ["s1", "bk1"], "bd1"),
+        3: lambda: add(T.pt[:, 2 * JL + 1:50:2], T.jv[:, JL:25], -float(S), ["jv"], "pt3"),
+        4: lambda: add(T.bk[:, 18:27], T.bdr[:, 9:18], -float(S), ["bd1"], "bk2")})
+    sl, sr = T.s2[:, r:r + 1], T.s2[:, r + 1:r + 2]
+    ts(T.fu[:, 0:100:2], T.pt[:], sl, 0.0, A.add, A.is_ge, ["s2", "pt0", "pt1", "pt3"], "fu0")
+    ts(T.fu[:, 4 * JL + 1:100:4], T.jv[:, JL:25], sl, sr, A.add, A.is_ge, ["s2", "jv"], "fu1")
+    add(T.fu[:, 3:100:4], T.jf[:], sl, ["s2", "jf"], "fu3")
+    tt(T.bdr[:, 18:27], T.s2[:], T.bk[:, 18:27], A.add, ["s2", "bk2"], "bd2")
     store("Y", T.bd[:, :], T.bdr[0:1, 0:27], ["bd0", "bd1", "bd2"])
-    ts(T.off3[:, 0:25], T.fw[:], float(FZ), None, A.min, None, ["fw"], ["off3"])
+    scan(T.fs[:], T.fm[:], T.fu[:], A.mult, ["fu0", "fu1", "fu3", "fuz"] + ["fm%d" % k for k in range(6)], "fs")
+    quant("m2", AL, 2 * W, T.he2[:], keys, "me2")
+    cp(T.off3[:, 0:25], T.fs[:, 3:100:4], ["fs"], "off3")
 
-    reads = ["mi2", "me2", "off3"]
-    off, lo, hi, hs = T.off3[:, 0:25], T.off3[:, 0:12], T.off3[:, 12:25], 192
-    op("V", lambda: V.tensor_copy(T.fin[:, 0:E].bitcast(dt.uint32), T.m2[:, 0:FZ + 2].bitcast(dt.uint32).indirect(off)),
-       reads, ["fin"])
-    op("S", lambda: g.scalar.activation(T.yo[:, 0:E], T.ys[:, 0:FZ + 2].indirect(off), F.Copy), ["ysi", "yse", "off3"], ["yo"])
-    op("V", lambda: V.tensor_copy(T.fins[:, hs:E], T.m2s[:, 0:FZ + 2].indirect(hi)), reads, ["finb"])
-    op("S", lambda: g.scalar.activation(T.fins[:, 0:hs], T.m2s[:, 0:FZ + 2].indirect(lo), F.Copy), reads, ["fina"])
-    store("Y", T.oc[:, :], T.fin[:, 0:E].bitcast(dt.uint8), ["fin"])
-    store("Y", T.y[:, :], T.yo[:, 0:E], ["yo"])
+    reads, off, h = ["mi2", "me2", "off3"], T.off3[:, 0:25], E // 2
+    cp(T.fin[:, 0:E].bitcast(dt.uint32), T.m2[:, 0:FE].bitcast(dt.uint32).indirect(off), reads, "fin")
+    act(T.fins[:, 0:E], T.m2s[:, 0:FE].indirect(off), F.Copy, reads, ["fins"])
+    store("Y", T.oc[:, :], u8("fin", 0, E), ["fin"])
     for k in range(4):
-        store("Y" if k < 2 else "S", T.osc[4 * k:4 * k + 4, :], T.fins[32 * k:32 * k + 4, 0:E], ["fina", "finb"])
+        store("YS"[k // 2], T.osc[4 * k:4 * k + 4, :], T.fins[32 * k:32 * k + 4, 0:E], ["fins"])
+    mm(4, "qa", 0, "fin", 0, h, ["qa", "fin", "fins"])
+    mm(5, "qa", 0, "fin", h, h, ["qa", "fin", "fins"])
+    act(T.yo[:, 0:h], T.ps4[:, 0:h], F.Copy, [], ["ps4", "yo0"])
+    cp(T.yo[:, h:E], T.ps5[:, 0:h], [], "ps5", "yo1")
+    store("Y", T.y[:, :], T.yo[:, 0:E], ["yo0", "yo1"])
 
     for s in SEMAPHORES:
         if s != "out" and total.get(s, 0) > waited.get(s, 0):

@@ -13,7 +13,7 @@ FR, FL, AL, AR, FE = FI + P, FI + P + W, FI + P + 2 * W, FI + P + 3 * W, FI + P 
 W0 = 128 - W
 JL = 6
 
-SCRATCH = {"pint": ("sbuf", [128, 4], "int32"), "off1": ("sbuf", [128, 10], "uint16"), "off3": ("sbuf", [128, 26], "uint16")}
+SCRATCH = {"pint": ("sbuf", [128, 8], "int32"), "off1": ("sbuf", [128, 10], "uint16"), "off3": ("sbuf", [128, 26], "uint16")}
 for _n, _c in (("xe", 512), ("xt", 4 * P), ("at", 512), ("wt", 2048), ("junk", 512), ("hi0", 4 * (P + 2 * S)), ("hi1", 4 * P),
                ("hi2", 4 * AL), ("he1", 8 * W), ("he2", 8 * W)):
     SCRATCH[_n] = ("sbuf", [128, _c], "bfloat16")
@@ -22,7 +22,8 @@ for _n, _c in (("qxe", 128), ("qa", 128), ("qw", 512), ("e0", 2 * S + P), ("e1",
     SCRATCH[_n] = ("sbuf", [128, _c], "float8_e4m3fn_x4")
     SCRATCH[_n + "s"] = ("sbuf", [128, _c], "uint8")
 for _n, _c in (("tiny", 1), ("cadd", 192), ("pref", 196), ("dm", 96), ("nar", 32), ("val", 32), ("cap", 32), ("zz", 32),
-               ("yt", 192), ("tt", 68), ("hm", 68), ("th", 68), ("ind", 160), ("cnt", 1), ("cl", 32), ("rc", 1), ("pc", 4),
+               ("yt", 192), ("tt", 68), ("hm", 68), ("th", 68), ("ind", 192), ("c24", 160), ("cs", 160), ("ec", 4),
+               ("cnt", 1), ("cl", 32), ("rc", 1), ("pc", 4),
                ("cg0", 32), ("cg1", 32), ("cg2", 32), ("yo", E), ("p16", 1), ("j0", 25), ("jj", 25), ("base", 10), ("bu", 10),
                ("bv", 10), ("s0", 9), ("s1", 9), ("s2", 9), ("bk", 27), ("bdr", 27), ("jm", 25), ("ptb", 25), ("jfb", 25),
                ("jv", 25), ("jf", 25), ("pt", 50), ("cst", 25), ("fm", 100), ("fu", 100), ("fs", 100)):
@@ -30,7 +31,7 @@ for _n, _c in (("tiny", 1), ("cadd", 192), ("pref", 196), ("dm", 96), ("nar", 32
 for _b in range(8):
     SCRATCH["ps%d" % _b] = ("psum", [128, 512], "float32")
 
-SEMAPHORES = ["sV", "sS", "sT", "sG", "loc", "out", "h0", "h1", "h2", "a0", "a1", "a2"] + ["d%d" % _i for _i in range(6)]
+SEMAPHORES = ["sV", "sS", "sT", "sG", "loc", "out", "h0", "h1", "h2", "a0", "a1", "a2"] + ["d%d" % _i for _i in range(8)]
 
 A = AluOpType
 F = ActivationFunctionType
@@ -197,7 +198,7 @@ def rank_program(g, core, T, topo):
 
     def products(src, a, n, reads, bank=0):
         for b in range(4):
-            mm(bank + b, "qw", 128 * b, src, a, n, reads + ["qw%d" % (b // 2)])
+            mm(bank + b, "qw", 128 * b, src, a, n, reads + ["qw%d" % b])
 
     def relu(o, i, on_vector, reads, writes):
         if on_vector:
@@ -244,17 +245,30 @@ def rank_program(g, core, T, topo):
         gap(3)
         scan(T.th[0:32, 0:65], T.hm[0:32, 0:65], T.tt[0:32, 0:65], A.mult, ["tt", "ttz", "hm", "hmh"], "th")
         gap(4)
-        w0 = 0 if t == 0 else W0
-        ts(T.ind[0:32, 32 + w0:160], T.pref[0:32, w0:128], T.th[0:32, 64:65], None, A.is_lt, None, ["pref", "pref0", "th"], "ind")
-        gap(5)
-        op("V", lambda: V.tensor_reduce(T.cnt[0:32, :], T.ind[0:32, 31 + w0:160], AxisListType.X, A.add), ["ind", "lo"], ["cnt"])
-        gap(6)
-        ts(T.cl[0:32, :], T.yt[0:32, 128:160], T.cnt[0:32, 0:1], float(S), A.max, A.min, ["ytz", "cnt"], "cl")
+        if t == 0:
+            ts(T.ind[0:32, 32:160], T.pref[0:32, 0:128], T.ec[0:32, 1:2], T.th[0:32, 64:65], A.mult, A.is_lt,
+               ["pref", "pref0", "th", "ec1"], "ind")
+            gap(5)
+            op("V", lambda: V.tensor_tensor_scan(T.cs[0:32, :], T.ind[0:32, 32:192], T.c24[0:32, :], T.ec[0:32, 2:3], A.add, A.min),
+               ["ind", "indz", "c24", "ec2"], ["cl"])
+            cl = T.cs[0:32, 128:160]
+        else:
+            ts(T.ind[0:32, 32 + W0:160], T.pref[0:32, W0:128], T.th[0:32, 64:65], None, A.is_lt, None, ["pref", "th"], "ind")
+            gap(5)
+            op("V", lambda: V.tensor_reduce(T.cnt[0:32, :], T.ind[0:32, 31 + W0:160], AxisListType.X, A.add), ["ind", "lo"], ["cnt"])
+            gap(6)
+            ts(T.cl[0:32, :], T.yt[0:32, 128:160], T.cnt[0:32, 0:1], float(S), A.max, A.min, ["ytz", "cnt"], "cl")
+            cl = T.cl[0:32, :]
         gap(7)
         for a in range(4):
-            turn(T.dm[32 * a:32 * a + 32, 32:64], T.cl[0:32, :], ["cl"], "dm%d" % a)
+            turn(T.dm[32 * a:32 * a + 32, 32:64], cl, ["cl"], "dm%d" % a)
         gap(8)
-        tt(T["s%d" % t][:], T.dm[:, 31:64:4], T.dm[:, 32:65:4], A.add, ["dm%d" % a for a in range(4)] + ["dma", "dmb"], "s%d" % t)
+        ks = ["dm%d" % a for a in range(4)] + ["dma", "dmb"]
+        if t == 0:
+            for a, c, key in ((0, 35 + 4 * r, "off1r"), (5, 31 + 4 * r, "off1l")):
+                ts(T.off1[:, a:a + 5], T.base[:, a:a + 5], T.dm[:, c + 1:c + 2], T.dm[:, c:c + 1], A.add, A.subtract,
+                   ks + ["base"], key)
+        tt(T["s%d" % t][:], T.dm[:, 32:65:4], T.dm[:, 31:64:4], A.add if t else A.subtract, ks, "s%d" % t)
 
     def held(j, t):
         s, o = (T["s%d" % t][:, 0:8], A.is_le) if j < 2 else (T["s%d" % t][:, 1:9], A.is_ge)
@@ -267,15 +281,15 @@ def rank_program(g, core, T, topo):
         a = j // 3
         ts(T.nar[0:32, j:32:4], T["s%d" % t][0:32, a:a + 8], -1.0, None, A.mult, None, ["s%d" % t, "nar"], "nar%d" % j)
 
-    def starts(w0):
-        turn(T.ind[0:32, w0:w0 + 32], T.nar[0:32, :], ["nar", "nar0", "nar3"], "lo", "ind")
+    def starts():
+        turn(T.ind[0:32, W0:W0 + 32], T.nar[0:32, :], ["nar", "nar0", "nar3"], "lo", "ind")
 
     load("Y", T.xe[:, 0:4 * S], T.x[:, 4 * (P - S):4 * P], "xer")
     load("S", T.xe[:, 4 * S:8 * S], T.x[:, 0:4 * S], "xel")
     load("Y", T.xt[:], T.x[:, :], "xt")
     load("S", T.at[:], T.a[:, :], "at")
-    load("Y", T.wt[:, 0:1024], T.w[:, 0:1024], "wt0")
-    load("S", T.wt[:, 1024:2048], T.w[:, 1024:2048], "wt1")
+    for b in range(4):
+        load("YS"[b % 2], T.wt[:, 512 * b:512 * b + 512], T.w[:, 512 * b:512 * b + 512], "wt%d" % b)
 
     fill(T.xe[:, 8 * S:512], 0.0, "xez")
     fill(T.hm[0:32, 0:64], 1.0, "hm")
@@ -286,8 +300,8 @@ def rank_program(g, core, T, topo):
     fill(T.tiny[:], -2.0 ** -120, "tiny")
     fill(T.cg0[:, 4 * r + 1:4 * r + 3], -130.0, "c0_1")
     wr["c0_2"] = wr["c0_1"]
-    fill(T.hm[0:32, 64:65], 0.5, "hmh")
-    fill(T.tt[0:32, 64:65], 0.0, "ttz")
+    fill(T.ind[0:32, 160:192], 0.0, "indz")
+    fill(T.cs[0:32, :], 0.0, "cl")
     fill(T.yt[0:32, 128:192], 0.0, "ytz")
     fill(T.cadd[0:32, 0:128], 130.0, "cadd")
     fill(T.cadd[0:32, 128:192], 0.0, "caddz")
@@ -297,16 +311,21 @@ def rank_program(g, core, T, topo):
     quant("qxe", 0, 128, T.xe[:], ["xer", "xel", "xez"], "qxe")
     halo(0, "qxe", "e0", S, {-1: (S, S if r == 1 else 0), 1: (0, S)}, ["qxe"])
 
-    fill(T.nar[0:32, 3:32:4], S - 128.0, "nar3", ["nar"])
+    ts(T.pint[:, 4:5], T.pint[:, 0:1], 3, None, A.bitwise_and, None, ["pint0"], "pint4")
     ts(T.pint[:, 2:3], T.pint[:, 0:1], 15, None, A.bitwise_and, None, ["pint0"], "pint2")
     ts(T.pint[:, 3:4], T.pint[:, 1:2], 2, None, A.arith_shift_right, None, ["pint0"], "pint3")
     for j, c in enumerate((W0, S, 128 - W - 1, W0 + S - 1)):
-        add(T.pc[:, j:j + 1], T.pint[:, 0:1], -float(c), ["pint0"], "pc")
-    fill(T.dm[:, 31:32], float(S), "dma")
-    fill(T.dm[:, 64:65], 0.0, "dmb")
+        add(T.pc[:, j:j + 1], T.pint[:, 0:1], -float(c), ["pint0"], "pc%d" % j)
+    wr["pc"] = wr["pc3"]
+    ts(T.ec[:, 0:1], T.pint[:, 4:5], 3.0, -1.0, A.is_equal, A.mult, ["pint4"], "ec0")
+    fill(T.dm[:, 31:32], 0.0, "dma")
+    fill(T.dm[:, 64:65], float(S), "dmb")
     cp(T.p16[:], T.pint[:, 2:3], ["pint2"], "p16")
     ts(T.rc[:], T.pint[:, 3:4], -2.0 / N, 1.0, A.mult, A.add, ["pint3"], "rc")
-    starts(0)
+    ts(T.ec[:, 1:2], T.ec[:, 0:1], 2.0, 1.0, A.mult, A.add, ["ec0"], "ec1")
+    ts(T.ec[:, 2:3], T.ec[:, 0:1], float(S), float(S), A.mult, A.add, ["ec0"], "ec2")
+    add(T.hm[0:32, 64:65], T.ec[0:32, 0:1], 0.5, ["ec0"], "hmh")
+    ts(T.tt[0:32, 64:65], T.ec[0:32, 0:1], -0.125, None, A.mult, None, ["ec0"], "ttz")
     if len(sides) == 1:
         z = 4 * (128 + S if r == 0 else 128)
         fill(T.hi0[:, z:z + 4 * S], 0.0, "hi0z")
@@ -318,6 +337,7 @@ def rank_program(g, core, T, topo):
     share(0)
     add(T.jj[:], T.j0[:], T.p16[:, 0:1], ["j0", "p16"], "jj")
     ts(T.hm[0:32, 32:33], T.hm[0:32, 32:33], T.rc[0:32, 0:1], None, A.mult, None, ["rc"], "hm")
+    ts(T.c24[0:32, :], T.cs[0:32, :], T.ec[0:32, 2:3], float(S), A.add, A.add, ["cl", "ec2"], "c24")
     fill(T.pc[0:32, 3:4], 1000.0, "pca", ["pc"])
     fill(T.pc[32:W0, 3:4], 1000.0, "pcb", ["pc"])
     fill(T.s1[:], float(S), "s1")
@@ -335,8 +355,8 @@ def rank_program(g, core, T, topo):
     lin(T.ptb[:, 0:JL], T.jj[:, 0:JL], 1.0, -4.0 * S, ["jj"], "ptb0")
     lin(T.jfb[:, 0:JL], T.jj[:, 0:JL], 1.0, AL + 0.25, ["jj"], "jfb0")
     lin(T.pt[:, 1:2 * JL:2], T.jj[:, 0:JL], 1.0, -float(S), ["jj"], "pt1")
-    quant("qw", 0, 256, T.wt[:, 0:1024], ["wt0"], "qw0")
-    quant("qw", 256, 256, T.wt[:, 1024:2048], ["wt1"], "qw1")
+    for b in range(4):
+        quant("qw", 128 * b, 128, T.wt[:, 512 * b:512 * b + 512], ["wt%d" % b], "qw%d" % b)
     products("e0", 2 * S, P, ["e0b"])
     own = []
     for b in range(4):
@@ -352,69 +372,69 @@ def rank_program(g, core, T, topo):
     interior_costs(0)
     edge_costs(0)
     products("m0", I0, P, ["mi0"])
-    keys = totile("hi1", P, ())
+    ki = totile("hi1", P, ())
     borders(0, {
         1: lambda: ts(T.bu[:, 0:5], T.jj[:, 0:5], 8.0 + 2 * S, 0.0 if r == N - 1 else float(A0 - 2 * S - MR),
                       A.is_ge, A.mult, ["jj"], "bur"),
         2: lambda: ts(T.bu[:, 5:10], T.jj[:, 0:5], float(S), 0.0 if r == 0 else float(S - L0), A.is_lt, A.mult, ["jj"], "bul"),
         3: lambda: fill(T.fm[:, 0:100:4], 0.0, "fm0"),
         4: lambda: tt(T.base[:], T.bu[:], T.bv[:], A.add, ["bur", "bul", "bvr", "bvl"], "base"),
-        5: lambda: fill(T.fm[:, 2:100:4], -8.0, "fm2"),
-        6: lambda: fill(T.fm[:, 3:4 * JL:4], c1, "fm3"),
-        7: lambda: fill(T.fm[:, 4 * JL + 3:100:4], c4, "fm4"),
-        8: lambda: fill(T.hi2[:, 0:4 * FI], 0.0, "hiz")})
-    bound(0, "hi1l")
+        5: lambda: (fill(T.hm[0:32, 64:65], 0.5, "hmh"), fill(T.tt[0:32, 64:65], 0.0, "ttz")),
+        7: lambda: bound(0, "hi1l"),
+        8: lambda: bound(4 * P - 8 * S, "hi1r")})
     sl, sr = T.s0[:, r:r + 1], T.s0[:, r + 1:r + 2]
-    add(T.off1[:, 0:5], T.base[:, 0:5], sr, ["base", "s0"], "off1r")
-    add(T.off1[:, 5:10], T.base[:, 5:10], sl, ["base", "s0"], "off1l")
-    bound(4 * P - 8 * S, "hi1r")
-    held(0, 0)
-    quant("m1", I0, P, T.hi1[:], keys + ["hi1l", "hi1r"], "mi1")
 
     reads, off = ["mi0", "me0", "arr1", "off1r", "off1l"], T.off1[:, 0:10]
     cp(T.e1[:, 0:160].bitcast(dt.uint32), T.m0[:, 0:A0 + W].bitcast(dt.uint32).indirect(off), reads, "ec1")
     act(T.e1s[:, 0:160], T.m0s[:, 0:A0 + W].indirect(off), F.Copy, reads, ["es1"])
-    interior_costs(1)
     products("e1", 8, 2 * W, ["ec1", "es1"])
+    held(0, 0)
     held(3, 0)
+    quant("m1", I0, P, T.hi1[:], ki + ["hi1l", "hi1r"], "mi1")
+    keys = totile("he1", 2 * W, (0, 2))
+    interior_costs(1)
+    mask()
     start(0, 0)
     start(3, 0)
-    mask()
-    keys = totile("he1", 2 * W, (0, 2))
-    starts(W0)
     quant("m1", MR, 2 * W, T.he1[:], keys, "me1")
     ends = {-1: (ML, W), 1: (MR, 0)}
     halo(2, "m1", "e2", W, ends, ["me1"], (False,))
     edge_costs(1)
     halo(2, "m1", "e2", W, ends, ["me1"], (True,))
     products("m1", I0, E, ["mi1", "me1"])
-    keys = totile("hi2", E, (), FI)
+    keys = totile("hi2", E, (), FI) + ["hiz"]
     lin(T.fm[:, 1:4 * JL:4], T.cst[:, 0:JL], sl, (FI - FL - 2 * S) / (-8 * c1), ["s0", "cst0"], "fm1")
     lin(T.fm[:, 4 * JL + 1:100:4], T.cst[:, JL:25], sr, (FR - FI - P + 3 * S) / (-8 * c4), ["s0", "cst1"], "fm5")
-    borders(1, {0: lambda: held(1, 0), 1: lambda: held(2, 0),
+    borders(1, {0: starts, 1: lambda: held(2, 0), 7: lambda: held(1, 0), 8: lambda: fill(T.hi2[:, 0:4 * FI], 0.0, "hiz"),
                 2: lambda: tt(T.bdr[:, 0:9], T.s0[:], T.bk[:, 0:9], A.add, ["s0", "bk0"], "bd0"),
                 3: lambda: ts(T.ptb[:, JL:25], T.jm[:, JL:25], sl, sr, A.add, A.subtract, ["s0", "jm"], "ptb1"),
                 4: lambda: ts(T.jfb[:, JL:25], T.jj[:, JL:25], sl, FI + 0.25 - W, A.add, A.add, ["s0", "jj"], "jfb1"),
-                5: lambda: fill(T.fu[:, 1:4 * JL:4], 0.0, "fuz"),
-                6: lambda: add(T.bk[:, 9:18], T.bdr[:, 0:9], -float(S), ["bd0"], "bk1")})
+                5: lambda: (fill(T.fu[:, 1:4 * JL:4], 0.0, "fuz"), fill(T.dm[:, 31:32], float(S), "dma")),
+                6: lambda: (add(T.bk[:, 9:18], T.bdr[:, 0:9], -float(S), ["bd0"], "bk1"), fill(T.dm[:, 64:65], 0.0, "dmb"))})
     sl, sr = T.s1[:, r:r + 1], T.s1[:, r + 1:r + 2]
+    n = AL // 3
+    quant("m2", 0, n, T.hi2[:, 0:4 * n], keys, "mi2a")
     held(0, 1)
     held(3, 1)
     start(0, 1)
-    mask()
     start(3, 1)
-    quant("m2", 0, AL, T.hi2[:], keys + ["hiz"], "mi2")
+    quant("m2", n, n, T.hi2[:, 4 * n:8 * n], keys, "mi2b")
+    mask()
+    quant("m2", 2 * n, n, T.hi2[:, 8 * n:12 * n], keys, "mi2")
     lin(T.pt[:, 0:50:2], T.ptb[:], 1.0, sl, ["s1", "ptb0", "ptb1"], "pt0")
     lin(T.jf[:], T.jfb[:], 1.0, sl, ["s1", "jfb0", "jfb1"], "jf")
 
     products("e2", 0, 2 * W, ["arr2", "e2z"])
     keys = totile("he2", 2 * W, ())
     borders(2, {
-        0: lambda: starts(W0),
+        0: starts,
         1: lambda: ts(T.jv[:, JL:25], T.ptb[:, JL:25], sl, sr, A.add, A.subtract, ["s1", "ptb1"], "jv"),
         2: lambda: tt(T.bdr[:, 9:18], T.s1[:], T.bk[:, 9:18], A.add, ["s1", "bk1"], "bd1"),
         3: lambda: add(T.pt[:, 2 * JL + 1:50:2], T.jv[:, JL:25], -float(S), ["jv"], "pt3"),
-        4: lambda: add(T.bk[:, 18:27], T.bdr[:, 9:18], -float(S), ["bd1"], "bk2")})
+        4: lambda: add(T.bk[:, 18:27], T.bdr[:, 9:18], -float(S), ["bd1"], "bk2"),
+        5: lambda: fill(T.fm[:, 4 * JL + 3:100:4], c4, "fm4"),
+        6: lambda: fill(T.fm[:, 2:100:4], -8.0, "fm2"),
+        7: lambda: fill(T.fm[:, 3:4 * JL:4], c1, "fm3")})
     sl, sr = T.s2[:, r:r + 1], T.s2[:, r + 1:r + 2]
     ts(T.fu[:, 0:100:2], T.pt[:], sl, 0.0, A.add, A.is_ge, ["s2", "pt0", "pt1", "pt3"], "fu0")
     ts(T.fu[:, 4 * JL + 1:100:4], T.jv[:, JL:25], sl, sr, A.add, A.is_ge, ["s2", "jv"], "fu1")
@@ -425,17 +445,22 @@ def rank_program(g, core, T, topo):
     quant("m2", AL, 2 * W, T.he2[:], keys, "me2")
     cp(T.off3[:, 0:25], T.fs[:, 3:100:4], ["fs"], "off3")
 
-    reads, off, h = ["mi2", "me2", "off3"], T.off3[:, 0:25], E // 2
-    cp(T.fin[:, 0:E].bitcast(dt.uint32), T.m2[:, 0:FE].bitcast(dt.uint32).indirect(off), reads, "fin")
-    act(T.fins[:, 0:E], T.m2s[:, 0:FE].indirect(off), F.Copy, reads, ["fins"])
-    store("Y", T.oc[:, :], u8("fin", 0, E), ["fin"])
+    reads, cuts = ["mi2", "me2", "off3"], (0, 8, 16, 25)
+    for k in range(3):
+        a, b = 16 * cuts[k], 16 * cuts[k + 1]
+        off = T.off3[:, cuts[k]:cuts[k + 1]]
+        cp(T.fin[:, a:b].bitcast(dt.uint32), T.m2[:, 0:FE].bitcast(dt.uint32).indirect(off), reads, "fin%d" % k)
+        act(T.fins[:, a:b], T.m2s[:, 0:FE].indirect(off), F.Copy, reads, ["fins%d" % k])
+        store("Y", T.oc[:, 4 * a:4 * b], u8("fin", a, b - a), ["fin%d" % k])
+        mm(4 + k, "qa", 0, "fin", a, b - a, ["qa", "fin%d" % k, "fins%d" % k])
+    a, b = 16 * cuts[1], 16 * cuts[2]
+    cp(T.yo[:, 0:a], T.ps4[:, 0:a], [], "ps4", "yo0")
+    act(T.yo[:, a:b], T.ps5[:, 0:b - a], F.Copy, [], ["ps5", "yo1"])
+    cp(T.yo[:, b:E], T.ps6[:, 0:E - b], [], "ps6", "yo2")
+    store("Y", T.y[:, 0:b], T.yo[:, 0:b], ["yo0", "yo1"])
     for k in range(4):
-        store("YS"[k // 2], T.osc[4 * k:4 * k + 4, :], T.fins[32 * k:32 * k + 4, 0:E], ["fins"])
-    mm(4, "qa", 0, "fin", 0, h, ["qa", "fin", "fins"])
-    mm(5, "qa", 0, "fin", h, h, ["qa", "fin", "fins"])
-    act(T.yo[:, 0:h], T.ps4[:, 0:h], F.Copy, [], ["ps4", "yo0"])
-    cp(T.yo[:, h:E], T.ps5[:, 0:h], [], "ps5", "yo1")
-    store("Y", T.y[:, :], T.yo[:, 0:E], ["yo0", "yo1"])
+        store("S", T.osc[4 * k:4 * k + 4, :], T.fins[32 * k:32 * k + 4, 0:E], ["fins0", "fins1", "fins2"])
+    store("Y", T.y[:, b:E], T.yo[:, b:E], ["yo2"])
 
     for s in SEMAPHORES:
         if s != "out" and total.get(s, 0) > waited.get(s, 0):

from concourse.bass import DstId, RemoteDMATransfer
from concourse.mybir import dt, AluOpType, AxisListType, ActivationFunctionType

N, P, S, R = 8, 256, 24, 3
E = P + 2 * S * R
W = 3 * S
I0 = 80
MR, ML, MA = I0 + P, I0 + P + W, I0 + P + 2 * W
L0 = MR + 4 * S
A0 = L0 + 4 * S + 16
FI = 2
FR, FL, AL, AR, FE = FI + P, FI + P + W, FI + P + 2 * W, FI + P + 3 * W, FI + P + 4 * W
W0 = 128 - W
JL = 6

SCRATCH = {"pint": ("sbuf", [128, 8], "int32"), "off1": ("sbuf", [128, 10], "uint16"), "off3": ("sbuf", [128, 26], "uint16")}
for _n, _c in (("xe", 512), ("xt", 4 * P), ("at", 512), ("wt", 2048), ("junk", 512), ("hi0", 4 * (P + 2 * S)), ("hi1", 4 * P),
               ("hi2", 4 * AL), ("he1", 8 * W), ("he2", 8 * W)):
    SCRATCH[_n] = ("sbuf", [128, _c], "bfloat16")
for _n, _c in (("qxe", 128), ("qa", 128), ("qw", 512), ("e0", 2 * S + P), ("e1", 160), ("e2", 2 * W),
               ("m0", A0 + W), ("m1", MA), ("m2", FE), ("fin", E)):
    SCRATCH[_n] = ("sbuf", [128, _c], "float8_e4m3fn_x4")
    SCRATCH[_n + "s"] = ("sbuf", [128, _c], "uint8")
for _n, _c in (("tiny", 1), ("cadd", 192), ("pref", 196), ("dm", 96), ("nar", 32), ("val", 32), ("cap", 32), ("zz", 32),
               ("yt", 192), ("tt", 68), ("hm", 68), ("th", 68), ("ind", 192), ("c24", 160), ("cs", 160), ("ec", 4),
               ("cnt", 1), ("cl", 32), ("rc", 1), ("pc", 4),
               ("cg0", 32), ("cg1", 32), ("cg2", 32), ("yo", E), ("p16", 1), ("j0", 25), ("jj", 25), ("base", 10), ("bu", 10),
               ("bv", 10), ("s0", 9), ("s1", 9), ("s2", 9), ("bk", 27), ("bdr", 27), ("jm", 25), ("ptb", 25), ("jfb", 25),
               ("jv", 25), ("jf", 25), ("pt", 50), ("cst", 25), ("fm", 100), ("fu", 100), ("fs", 100)):
    SCRATCH[_n] = ("sbuf", [128, _c], "float32")
for _b in range(8):
    SCRATCH["ps%d" % _b] = ("psum", [128, 512], "float32")

SEMAPHORES = ["sV", "sS", "sT", "sG", "loc", "out", "h0", "h1", "h2", "a0", "a1", "a2"] + ["d%d" % _i for _i in range(8)]

A = AluOpType
F = ActivationFunctionType


def _bits(engs):
    return sum(1 << e for e in engs)


def _halo_engines(T, topo, q, side):
    engs = topo.engines(T.cores[q], T.cores[q + side])
    if 0 < q < N - 1:
        h = len(engs) // 2
        return engs[:h] if side < 0 else engs[h:]
    return engs


def _all_engines(T, topo, q):
    m = -1
    for o in range(N):
        if o != q:
            m &= topo.mask(T.cores[q], T.cores[o])
    return m, bin(m).count("1")


def rank_program(g, core, T, topo):
    r = T.rank_of(core)
    if r is None:
        return
    V = g.vector
    queue = {"V": g.vector, "S": g.scalar, "T": g.tensor, "G": g, "Y": g.sync}
    known = {k: {} for k in queue}
    total, waited, wr, rd = {}, {}, {}, {}
    nd = [0]

    def need(q, reads, writes):
        evs = {}
        cand = [wr[k] for k in reads if k in wr] + [wr[k] for k in writes if k in wr]
        for k in writes:
            cand += rd.get(k, [])
        for ev in cand:
            if ev[0] not in evs or evs[ev[0]][1] < ev[1]:
                evs[ev[0]] = ev
        for s, ev in evs.items():
            if any(o[2].get(s, 0) >= ev[1] for s2, o in evs.items() if s2 != s):
                continue
            if known[q].get(s, 0) < ev[1]:
                queue[q].wait_ge(T.sem[s], ev[1])
                waited[s] = max(waited.get(s, 0), ev[1])
        for s, ev in evs.items():
            known[q][s] = max(known[q].get(s, 0), ev[1])
            for s2, v in ev[2].items():
                known[q][s2] = max(known[q].get(s2, 0), v)

    def done(q, s, n, reads, writes):
        total[s] = total.get(s, 0) + n
        ev = (s, total[s], dict(known[q]))
        for k in reads:
            rd.setdefault(k, []).append(ev)
        for k in writes:
            wr[k] = ev
            rd[k] = []

    def op(q, fn, reads, writes):
        need(q, reads, writes)
        fn().then_inc(T.sem["s" + q], 1)
        done(q, "s" + q, 1, reads, writes)

    def load(q, out, in_, key):
        s = "d%d" % nd[0]
        nd[0] += 1
        queue[q].dma_start(out, in_).then_inc(T.sem[s], 16)
        done(q, s, 16, [], [key])

    def store(q, out, in_, reads):
        need(q, reads, [])
        queue[q].dma_start(out, in_).then_inc(T.sem.out, 16)
        total["out"] = total.get("out", 0) + 16

    def arrives(key, s, n):
        total[s] = n
        wr[key] = (s, n, {})

    def ts(out, in0, s1, s2, o0, o1, reads, key):
        if s2 is None:
            op("V", lambda: V.tensor_scalar(out, in0, s1, None, o0), reads, [key])
        else:
            op("V", lambda: V.tensor_scalar(out, in0, s1, s2, o0, o1), reads, [key])

    def add(out, in0, s1, reads, key):
        ts(out, in0, s1, None, A.add, None, reads, key)

    def tt(out, in0, in1, o, reads, key):
        op("V", lambda: V.tensor_tensor(out, in0, in1, o), reads, [key])

    def cp(out, in_, reads, *keys):
        op("V", lambda: V.tensor_copy(out, in_), reads, list(keys))

    def scan(out, d0, d1, o0, reads, key):
        op("V", lambda: V.tensor_tensor_scan(out, d0, d1, 0.0, o0, A.add), reads, [key])

    def turn(out, in_, reads, *keys):
        op("V", lambda: V.transpose(out, in_), reads, list(keys))

    def fill(ap, c, key, reads=()):
        op("V", lambda: V.memset(ap, c), list(reads), [key])

    def act(out, in_, f, reads, writes, **kw):
        op("S", lambda: g.scalar.activation(out, in_, f, **kw), reads, writes)

    def lin(out, in_, scale, bias, reads, key):
        act(out, in_, F.Identity, reads, [key], bias=bias, scale=scale)

    def iota(out, pat, key):
        op("G", lambda: g.iota(out, pat, 0, 0, allow_small_or_imprecise_dtypes=True), [], [key])

    def quant(name, a, n, src, reads, key):
        op("V", lambda: V.quantize_mx(T[name][:, a:a + n], T[name + "s"][:, a:a + n], src), reads, [key])

    def mm(bank, ln, la, rn, ra, n, reads):
        op("T", lambda: g.tensor.matmul_mx(T["ps%d" % bank][:, 0:n], T[ln][:, la:la + 128], T[ln + "s"][:, la:la + 128],
                                           T[rn][:, ra:ra + n], T[rn + "s"][:, ra:ra + n], True, True),
           reads, ["ps%d" % bank])

    def u8(name, a, n):
        return T[name][:, a:a + n].bitcast(dt.uint8)

    def dst(o):
        rid, pid = topo.addr(T.cores[o], core)
        return DstId(rid=rid, pnc=pid)

    sides = [s for s in (-1, 1) if 0 <= r + s < N]

    def halo(t, src, dname, n, from_to, reads, calls=(True, False)):
        need("G", reads, [])
        for codes in calls:
            trs = []
            for s in sides:
                a, b = from_to[s]
                i, o = (u8(src, a, n), u8(dname, b, n)) if codes else (T[src + "s"][:, a:a + n], T[dname + "s"][:, b:b + n])
                engs = _halo_engines(T, topo, r, s)
                trs.append(RemoteDMATransfer(dst_ids=[dst(r + s)], dma_engine_mask=_bits(engs),
                                             remote_sem=T.sem["h%d" % t], src=i, dst=o))
                total["loc"] = total.get("loc", 0) + len(engs)
            g.remote_dma_fused(trs, local_sem=T.sem.loc)
        arrives("arr%d" % t, "h%d" % t, sum(2 * len(_halo_engines(T, topo, r + s, -s)) for s in sides))

    def share(t):
        need("G", ["c%d_%d" % (t, j) for j in range(4)], [])
        slot = T["cg%d" % t][:, 4 * r:4 * r + 4]
        others = [(r + k) % N for k in range(1, N)]
        m, n = _all_engines(T, topo, r)
        g.remote_dma_fused([RemoteDMATransfer(dst_ids=[dst(o) for o in others], dma_engine_mask=m,
                                              remote_sem=T.sem["a%d" % t], srcs=[slot], dsts=[slot for o in others])],
                           local_sem=T.sem.loc)
        total["loc"] = total.get("loc", 0) + n
        arrives("ag%d" % t, "a%d" % t, sum(_all_engines(T, topo, o)[1] for o in others))

    def cost(t, j, name, a, reads):
        mm(4 + j, name, a, "qa", 0, 128, reads + ["qa"])
        act(T.junk[:, 128 * j:128 * j + 128], T["ps%d" % (4 + j)][:, 0:128], F.Sign, ["tiny"],
            ["ps%d" % (4 + j), "junk%d" % j, "c%d_%d" % (t, j)], bias=T.tiny[:, 0:1],
            accum_out=T["cg%d" % t][:, 4 * r + j:4 * r + j + 1])

    def products(src, a, n, reads, bank=0):
        for b in range(4):
            mm(bank + b, "qw", 128 * b, src, a, n, reads + ["qw%d" % b])

    def relu(o, i, on_vector, reads, writes):
        if on_vector:
            op("V", lambda: V.tensor_scalar(o, i, 0.0, 0.0625, A.max, A.mult), reads, writes)
        else:
            act(o, i, F.Relu, reads, writes, scale=0.0625)

    def totile(h, n, on_vector, a=0, bank=0):
        for b in range(4):
            relu(T[h][:, 4 * a + b:4 * (a + n):4], T["ps%d" % (bank + b)][:, 0:n], b in on_vector, [],
                 ["ps%d" % (bank + b), h + "_%d" % b])
        return [h + "_%d" % b for b in range(4)]

    def bound(a, key):
        v = T.hi1[:, a:a + 8 * S]
        ts(v, v, 2.0 ** 31, None, A.min, None, ["hi1_%d" % b for b in range(4)], key)

    def interior_costs(t):
        cost(t + 1, 1, "m%d" % t, I0, ["mi%d" % t])
        cost(t + 1, 2, "m%d" % t, I0 + 128, ["mi%d" % t])

    def edge_costs(t):
        cost(t + 1, 0, "m%d" % t, (L0 + W if t == 0 else MA) - 128, ["me%d" % t])
        cost(t + 1, 3, "m%d" % t, (L0 if t == 0 else ML) - 128, ["me%d" % t, "mi%d" % t])
        share(t + 1)

    def borders(t, between):
        def gap(k):
            if k in between:
                between[k]()
        cg = T["cg%d" % t]
        reads = ["ag%d" % t] + ["c%d_%d" % (t, j) for j in range(4)]
        if t > 0:
            tt(T.zz[:], cg[:], T.cap[:], A.min, reads + ["cap"], "zz")
            cg, reads = T.zz, ["zz"]
        gap(0)
        for a in range(4):
            turn(T.yt[0:32, 32 * a:32 * a + 32], cg[32 * a:32 * a + 32, 0:32], reads, "yt%d" % a)
        gap(1)
        scan(T.pref[0:32, 1:193], T.yt[0:32, 0:192], T.cadd[0:32, 0:192], A.add,
             ["yt%d" % a for a in range(4)] + ["ytz", "cadd", "caddz"], "pref")
        gap(2)
        turn(T.tt[0:32, 0:64], T.pref[0:32, 128:192], ["pref"], "tt")
        gap(3)
        scan(T.th[0:32, 0:65], T.hm[0:32, 0:65], T.tt[0:32, 0:65], A.mult, ["tt", "ttz", "hm", "hmh"], "th")
        gap(4)
        if t == 0:
            ts(T.ind[0:32, 32:160], T.pref[0:32, 0:128], T.ec[0:32, 1:2], T.th[0:32, 64:65], A.mult, A.is_lt,
               ["pref", "pref0", "th", "ec1"], "ind")
            gap(5)
            op("V", lambda: V.tensor_tensor_scan(T.cs[0:32, :], T.ind[0:32, 32:192], T.c24[0:32, :], T.ec[0:32, 2:3], A.add, A.min),
               ["ind", "indz", "c24", "ec2"], ["cl"])
            cl = T.cs[0:32, 128:160]
        else:
            ts(T.ind[0:32, 32 + W0:160], T.pref[0:32, W0:128], T.th[0:32, 64:65], None, A.is_lt, None, ["pref", "th"], "ind")
            gap(5)
            op("V", lambda: V.tensor_reduce(T.cnt[0:32, :], T.ind[0:32, 31 + W0:160], AxisListType.X, A.add), ["ind", "lo"], ["cnt"])
            gap(6)
            ts(T.cl[0:32, :], T.yt[0:32, 128:160], T.cnt[0:32, 0:1], float(S), A.max, A.min, ["ytz", "cnt"], "cl")
            cl = T.cl[0:32, :]
        gap(7)
        for a in range(4):
            turn(T.dm[32 * a:32 * a + 32, 32:64], cl, ["cl"], "dm%d" % a)
        gap(8)
        ks = ["dm%d" % a for a in range(4)] + ["dma", "dmb"]
        if t == 0:
            for a, c, key in ((0, 35 + 4 * r, "off1r"), (5, 31 + 4 * r, "off1l")):
                ts(T.off1[:, a:a + 5], T.base[:, a:a + 5], T.dm[:, c + 1:c + 2], T.dm[:, c:c + 1], A.add, A.subtract,
                   ks + ["base"], key)
        tt(T["s%d" % t][:], T.dm[:, 32:65:4], T.dm[:, 31:64:4], A.add if t else A.subtract, ks, "s%d" % t)

    def held(j, t):
        s, o = (T["s%d" % t][:, 0:8], A.is_le) if j < 2 else (T["s%d" % t][:, 1:9], A.is_ge)
        ts(T.val[:, j:32:4], s, T.pc[:, j:j + 1], None, o, None, ["s%d" % t, "pc", "pca", "pcb"], "val%d" % j)

    def mask():
        ts(T.cap[:], T.val[:], 400.0, -130.0, A.mult, A.add, ["val%d" % j for j in range(4)], "cap")

    def start(j, t):
        a = j // 3
        ts(T.nar[0:32, j:32:4], T["s%d" % t][0:32, a:a + 8], -1.0, None, A.mult, None, ["s%d" % t, "nar"], "nar%d" % j)

    def starts():
        turn(T.ind[0:32, W0:W0 + 32], T.nar[0:32, :], ["nar", "nar0", "nar3"], "lo", "ind")

    load("Y", T.xe[:, 0:4 * S], T.x[:, 4 * (P - S):4 * P], "xer")
    load("S", T.xe[:, 4 * S:8 * S], T.x[:, 0:4 * S], "xel")
    load("Y", T.xt[:], T.x[:, :], "xt")
    load("S", T.at[:], T.a[:, :], "at")
    for b in range(4):
        load("YS"[b % 2], T.wt[:, 512 * b:512 * b + 512], T.w[:, 512 * b:512 * b + 512], "wt%d" % b)

    fill(T.xe[:, 8 * S:512], 0.0, "xez")
    fill(T.hm[0:32, 0:64], 1.0, "hm")
    op("G", lambda: g.iota(T.pint[:, 0:2], [[1, 2]], 0, 1), [], ["pint0"])
    iota(T.j0[:], [[16, 25]], "j0")
    iota(T.bdr[:, 0:9], [[P, 9]], "bd0")
    op("G", lambda: g.affine_select(T.hm[0:32, 32:64], T.hm[0:32, 32:64], [[-1, 32]], A.not_equal, -1.0, 0, 1), ["hm"], ["hm"])
    fill(T.tiny[:], -2.0 ** -120, "tiny")
    fill(T.cg0[:, 4 * r + 1:4 * r + 3], -130.0, "c0_1")
    wr["c0_2"] = wr["c0_1"]
    fill(T.ind[0:32, 160:192], 0.0, "indz")
    fill(T.cs[0:32, :], 0.0, "cl")
    fill(T.yt[0:32, 128:192], 0.0, "ytz")
    fill(T.cadd[0:32, 0:128], 130.0, "cadd")
    fill(T.cadd[0:32, 128:192], 0.0, "caddz")
    fill(T.pref[0:32, 0:1], 0.0, "pref0")
    fill(T.nar[0:32, :], 0.0, "nar")

    quant("qxe", 0, 128, T.xe[:], ["xer", "xel", "xez"], "qxe")
    halo(0, "qxe", "e0", S, {-1: (S, S if r == 1 else 0), 1: (0, S)}, ["qxe"])

    ts(T.pint[:, 4:5], T.pint[:, 0:1], 3, None, A.bitwise_and, None, ["pint0"], "pint4")
    ts(T.pint[:, 2:3], T.pint[:, 0:1], 15, None, A.bitwise_and, None, ["pint0"], "pint2")
    ts(T.pint[:, 3:4], T.pint[:, 1:2], 2, None, A.arith_shift_right, None, ["pint0"], "pint3")
    for j, c in enumerate((W0, S, 128 - W - 1, W0 + S - 1)):
        add(T.pc[:, j:j + 1], T.pint[:, 0:1], -float(c), ["pint0"], "pc%d" % j)
    wr["pc"] = wr["pc3"]
    ts(T.ec[:, 0:1], T.pint[:, 4:5], 3.0, -1.0, A.is_equal, A.mult, ["pint4"], "ec0")
    fill(T.dm[:, 31:32], 0.0, "dma")
    fill(T.dm[:, 64:65], float(S), "dmb")
    cp(T.p16[:], T.pint[:, 2:3], ["pint2"], "p16")
    ts(T.rc[:], T.pint[:, 3:4], -2.0 / N, 1.0, A.mult, A.add, ["pint3"], "rc")
    ts(T.ec[:, 1:2], T.ec[:, 0:1], 2.0, 1.0, A.mult, A.add, ["ec0"], "ec1")
    ts(T.ec[:, 2:3], T.ec[:, 0:1], float(S), float(S), A.mult, A.add, ["ec0"], "ec2")
    add(T.hm[0:32, 64:65], T.ec[0:32, 0:1], 0.5, ["ec0"], "hmh")
    ts(T.tt[0:32, 64:65], T.ec[0:32, 0:1], -0.125, None, A.mult, None, ["ec0"], "ttz")
    if len(sides) == 1:
        z = 4 * (128 + S if r == 0 else 128)
        fill(T.hi0[:, z:z + 4 * S], 0.0, "hi0z")

    quant("e0", 2 * S, P, T.xt[:], ["xt"], "e0b")
    quant("qa", 0, 128, T.at[:], ["at"], "qa")
    cost(0, 0, "e0", 2 * S, ["e0b"])
    cost(0, 3, "e0", 128 + 2 * S, ["e0b"])
    share(0)
    add(T.jj[:], T.j0[:], T.p16[:, 0:1], ["j0", "p16"], "jj")
    ts(T.hm[0:32, 32:33], T.hm[0:32, 32:33], T.rc[0:32, 0:1], None, A.mult, None, ["rc"], "hm")
    ts(T.c24[0:32, :], T.cs[0:32, :], T.ec[0:32, 2:3], float(S), A.add, A.add, ["cl", "ec2"], "c24")
    fill(T.pc[0:32, 3:4], 1000.0, "pca", ["pc"])
    fill(T.pc[32:W0, 3:4], 1000.0, "pcb", ["pc"])
    fill(T.s1[:], float(S), "s1")
    c1, c4 = float(FL - AL - S), float(AR - FR - S)
    fill(T.cst[:, 0:JL], -1.0 / (8 * c1), "cst0")
    fill(T.cst[:, JL:25], 1.0 / (8 * c4), "cst1")
    held(1, 1)
    held(2, 1)
    if len(sides) == 1:
        quant("e2", 0, 2 * W, T.xt[:, 0:8 * W], ["xt"], "e2z")
    lin(T.bv[:, 0:5], T.jj[:, 0:5], 1.0, MR - 8.0, ["jj"], "bvr")
    lin(T.bv[:, 5:10], T.jj[:, 0:5], 1.0, float(L0 - S), ["jj"], "bvl")
    lin(T.bk[:, 0:9], T.bdr[:, 0:9], 1.0, -float(S), ["bd0"], "bk0")
    lin(T.jm[:, JL:25], T.jj[:, JL:25], 1.0, -float(P), ["jj"], "jm")
    lin(T.ptb[:, 0:JL], T.jj[:, 0:JL], 1.0, -4.0 * S, ["jj"], "ptb0")
    lin(T.jfb[:, 0:JL], T.jj[:, 0:JL], 1.0, AL + 0.25, ["jj"], "jfb0")
    lin(T.pt[:, 1:2 * JL:2], T.jj[:, 0:JL], 1.0, -float(S), ["jj"], "pt1")
    for b in range(4):
        quant("qw", 128 * b, 128, T.wt[:, 512 * b:512 * b + 512], ["wt%d" % b], "qw%d" % b)
    products("e0", 2 * S, P, ["e0b"])
    own = []
    for b in range(4):
        for a, pa in ((0, 128), (128 + 2 * S, 0)):
            own.append("own%d_%d" % (b, a))
            relu(T.hi0[:, 4 * a + b:4 * (a + 128):4], T["ps%d" % b][:, pa:pa + 128], b % 2 == 0, ["ps%d" % b], own[-1:])
    quant("m0", I0, 128, T.hi0[:, 4 * (128 + 2 * S):4 * (P + 2 * S)], own, "mi0a")
    quant("m0", I0 + 128, 128, T.hi0[:, 0:512], own, "mi0")
    products("e0", 0 if len(sides) == 2 else S, 128, ["e0b", "arr0"], 4)
    keys = totile("hi0", S * len(sides), (0, 2), 128 + S if r == N - 1 else 128, 4)
    quant("m0", MR, A0 - MR, T.hi0[:, 4 * W0:4 * (W0 + A0 - MR)], keys + own + ["hi0z"], "me0")
    halo(1, "m0", "m0", W, {-1: (L0, A0), 1: (MR + S, 0)}, ["me0"])
    interior_costs(0)
    edge_costs(0)
    products("m0", I0, P, ["mi0"])
    ki = totile("hi1", P, ())
    borders(0, {
        1: lambda: ts(T.bu[:, 0:5], T.jj[:, 0:5], 8.0 + 2 * S, 0.0 if r == N - 1 else float(A0 - 2 * S - MR),
                      A.is_ge, A.mult, ["jj"], "bur"),
        2: lambda: ts(T.bu[:, 5:10], T.jj[:, 0:5], float(S), 0.0 if r == 0 else float(S - L0), A.is_lt, A.mult, ["jj"], "bul"),
        3: lambda: fill(T.fm[:, 0:100:4], 0.0, "fm0"),
        4: lambda: tt(T.base[:], T.bu[:], T.bv[:], A.add, ["bur", "bul", "bvr", "bvl"], "base"),
        5: lambda: (fill(T.hm[0:32, 64:65], 0.5, "hmh"), fill(T.tt[0:32, 64:65], 0.0, "ttz")),
        7: lambda: bound(0, "hi1l"),
        8: lambda: bound(4 * P - 8 * S, "hi1r")})
    sl, sr = T.s0[:, r:r + 1], T.s0[:, r + 1:r + 2]

    reads, off = ["mi0", "me0", "arr1", "off1r", "off1l"], T.off1[:, 0:10]
    cp(T.e1[:, 0:160].bitcast(dt.uint32), T.m0[:, 0:A0 + W].bitcast(dt.uint32).indirect(off), reads, "ec1")
    act(T.e1s[:, 0:160], T.m0s[:, 0:A0 + W].indirect(off), F.Copy, reads, ["es1"])
    products("e1", 8, 2 * W, ["ec1", "es1"])
    held(0, 0)
    held(3, 0)
    quant("m1", I0, P, T.hi1[:], ki + ["hi1l", "hi1r"], "mi1")
    keys = totile("he1", 2 * W, (0, 2))
    interior_costs(1)
    mask()
    start(0, 0)
    start(3, 0)
    quant("m1", MR, 2 * W, T.he1[:], keys, "me1")
    ends = {-1: (ML, W), 1: (MR, 0)}
    halo(2, "m1", "e2", W, ends, ["me1"], (False,))
    edge_costs(1)
    halo(2, "m1", "e2", W, ends, ["me1"], (True,))
    products("m1", I0, E, ["mi1", "me1"])
    keys = totile("hi2", E, (), FI) + ["hiz"]
    lin(T.fm[:, 1:4 * JL:4], T.cst[:, 0:JL], sl, (FI - FL - 2 * S) / (-8 * c1), ["s0", "cst0"], "fm1")
    lin(T.fm[:, 4 * JL + 1:100:4], T.cst[:, JL:25], sr, (FR - FI - P + 3 * S) / (-8 * c4), ["s0", "cst1"], "fm5")
    borders(1, {0: starts, 1: lambda: held(2, 0), 7: lambda: held(1, 0), 8: lambda: fill(T.hi2[:, 0:4 * FI], 0.0, "hiz"),
                2: lambda: tt(T.bdr[:, 0:9], T.s0[:], T.bk[:, 0:9], A.add, ["s0", "bk0"], "bd0"),
                3: lambda: ts(T.ptb[:, JL:25], T.jm[:, JL:25], sl, sr, A.add, A.subtract, ["s0", "jm"], "ptb1"),
                4: lambda: ts(T.jfb[:, JL:25], T.jj[:, JL:25], sl, FI + 0.25 - W, A.add, A.add, ["s0", "jj"], "jfb1"),
                5: lambda: (fill(T.fu[:, 1:4 * JL:4], 0.0, "fuz"), fill(T.dm[:, 31:32], float(S), "dma")),
                6: lambda: (add(T.bk[:, 9:18], T.bdr[:, 0:9], -float(S), ["bd0"], "bk1"), fill(T.dm[:, 64:65], 0.0, "dmb"))})
    sl, sr = T.s1[:, r:r + 1], T.s1[:, r + 1:r + 2]
    n = AL // 3
    quant("m2", 0, n, T.hi2[:, 0:4 * n], keys, "mi2a")
    held(0, 1)
    held(3, 1)
    start(0, 1)
    start(3, 1)
    quant("m2", n, n, T.hi2[:, 4 * n:8 * n], keys, "mi2b")
    mask()
    quant("m2", 2 * n, n, T.hi2[:, 8 * n:12 * n], keys, "mi2")
    lin(T.pt[:, 0:50:2], T.ptb[:], 1.0, sl, ["s1", "ptb0", "ptb1"], "pt0")
    lin(T.jf[:], T.jfb[:], 1.0, sl, ["s1", "jfb0", "jfb1"], "jf")

    products("e2", 0, 2 * W, ["arr2", "e2z"])
    keys = totile("he2", 2 * W, ())
    borders(2, {
        0: starts,
        1: lambda: ts(T.jv[:, JL:25], T.ptb[:, JL:25], sl, sr, A.add, A.subtract, ["s1", "ptb1"], "jv"),
        2: lambda: tt(T.bdr[:, 9:18], T.s1[:], T.bk[:, 9:18], A.add, ["s1", "bk1"], "bd1"),
        3: lambda: add(T.pt[:, 2 * JL + 1:50:2], T.jv[:, JL:25], -float(S), ["jv"], "pt3"),
        4: lambda: add(T.bk[:, 18:27], T.bdr[:, 9:18], -float(S), ["bd1"], "bk2"),
        5: lambda: fill(T.fm[:, 4 * JL + 3:100:4], c4, "fm4"),
        6: lambda: fill(T.fm[:, 2:100:4], -8.0, "fm2"),
        7: lambda: fill(T.fm[:, 3:4 * JL:4], c1, "fm3")})
    sl, sr = T.s2[:, r:r + 1], T.s2[:, r + 1:r + 2]
    ts(T.fu[:, 0:100:2], T.pt[:], sl, 0.0, A.add, A.is_ge, ["s2", "pt0", "pt1", "pt3"], "fu0")
    ts(T.fu[:, 4 * JL + 1:100:4], T.jv[:, JL:25], sl, sr, A.add, A.is_ge, ["s2", "jv"], "fu1")
    add(T.fu[:, 3:100:4], T.jf[:], sl, ["s2", "jf"], "fu3")
    tt(T.bdr[:, 18:27], T.s2[:], T.bk[:, 18:27], A.add, ["s2", "bk2"], "bd2")
    store("Y", T.bd[:, :], T.bdr[0:1, 0:27], ["bd0", "bd1", "bd2"])
    scan(T.fs[:], T.fm[:], T.fu[:], A.mult, ["fu0", "fu1", "fu3", "fuz"] + ["fm%d" % k for k in range(6)], "fs")
    quant("m2", AL, 2 * W, T.he2[:], keys, "me2")
    cp(T.off3[:, 0:25], T.fs[:, 3:100:4], ["fs"], "off3")

    reads, cuts = ["mi2", "me2", "off3"], (0, 8, 16, 25)
    for k in range(3):
        a, b = 16 * cuts[k], 16 * cuts[k + 1]
        off = T.off3[:, cuts[k]:cuts[k + 1]]
        cp(T.fin[:, a:b].bitcast(dt.uint32), T.m2[:, 0:FE].bitcast(dt.uint32).indirect(off), reads, "fin%d" % k)
        act(T.fins[:, a:b], T.m2s[:, 0:FE].indirect(off), F.Copy, reads, ["fins%d" % k])
        store("Y", T.oc[:, 4 * a:4 * b], u8("fin", a, b - a), ["fin%d" % k])
        mm(4 + k, "qa", 0, "fin", a, b - a, ["qa", "fin%d" % k, "fins%d" % k])
    a, b = 16 * cuts[1], 16 * cuts[2]
    cp(T.yo[:, 0:a], T.ps4[:, 0:a], [], "ps4", "yo0")
    act(T.yo[:, a:b], T.ps5[:, 0:b - a], F.Copy, [], ["ps5", "yo1"])
    cp(T.yo[:, b:E], T.ps6[:, 0:E - b], [], "ps6", "yo2")
    store("Y", T.y[:, 0:b], T.yo[:, 0:b], ["yo0", "yo1"])
    for k in range(4):
        store("S", T.osc[4 * k:4 * k + 4, :], T.fins[32 * k:32 * k + 4, 0:E], ["fins0", "fins1", "fins2"])
    store("Y", T.y[:, b:E], T.yo[:, b:E], ["yo2"])

    for s in SEMAPHORES:
        if s != "out" and total.get(s, 0) > waited.get(s, 0):
            g.wait_ge(T.sem[s], total[s])
    g.wait_ge(T.sem.out, total["out"])
